import numpy as np, ml_dtypes
CORES = [23,119,17,113]
N = 4
BF = ml_dtypes.bfloat16
def gentries(a):
    return np.ascontiguousarray(a.reshape(8, 16, -1).transpose(0, 2, 1)).reshape(8, -1)
def gtable(e):
    e = np.asarray(e); return np.ascontiguousarray(e.reshape(8, -1, 16).transpose(0, 2, 1)).reshape(128, -1).astype(np.int32)
W, TT, M, Q, SC = 2048, 2, 4, 2, 0.5
def tries(prev, cur, c):
    cs, ds = [], []
    for m in range(M):
        v = np.take_along_axis(prev, c[:, None, :], 2) - cur; d = np.add.reduce(v * v, axis=1)
        cs.append(c); ds.append(d); c = (5 * c + d + 1) & (W - 1)
    return np.stack(cs, axis=1), np.stack(ds, axis=1)
def parts(rng):
    return rng.integers(0, 16, (N, 8, 16, TT, W)), rng.integers(0, 16, (N, 8, 16, W)), rng.integers(0, 256, (N, 8, 16, W)), rng.integers(0, W, (N, 8, TT, W))
def walk(x, xb, c):
    d = np.zeros((N, 8, M, TT, W), np.int64); prev = xb[0]
    for r in range(N):
        for s in range(TT):
            cur = x[r, :, :, s]; d[r, :, :, s] = tries(prev, cur, c[r, :, s])[1]; prev = cur
    return d
def pack(x, xb, tb, c, th):
    return {"x": np.ascontiguousarray(x.reshape(N, 128, TT * W)).astype(np.float32).astype(BF), "xb": np.ascontiguousarray(xb.reshape(N, 128, W)).astype(np.float32).astype(BF),
            "tb": np.ascontiguousarray(tb.reshape(N, 128, W)).astype(np.float32).astype(BF),
            "c0": np.stack([gtable(a.reshape(8, -1)) for a in c]), "th": np.stack([gtable(a.reshape(8, -1)) for a in th])}
def setup_inputs(rng):
    x, xb, tb, c = parts(rng)
    th = rng.integers(350, 950, (N, 8, M, TT, W)) + rng.integers(-100, 101, (N, 8, 1, TT, 1))
    return pack(x, xb, tb, c, th)
def setup_inputs_ties(rng):
    x, xb, tb, c = parts(rng); d = walk(x, xb, c)
    return pack(x, xb, tb, c, np.clip(d + rng.integers(-1, 3, d.shape), 0, 4095))
def setup_inputs_counts(rng):
    x, xb, tb, c = parts(rng); d = walk(x, xb, c); a = rng.integers(0, 40, d.shape)
    p = rng.random(d.shape) < rng.random((N, 8, 1, TT, W))
    p[:, 0] = False; p[:, 1] = True; p[:, 2] = False; p[:, 2, M - 1] = True; p[:, 3] = False; p[:, 3, 0] = True
    return pack(x, xb, tb, c, np.where(p, np.minimum(d + 1 + a, 4095), np.maximum(d - a, 0)))
def setup_inputs_ends(rng):
    x, xb, tb, c = parts(rng); x = 15 * (x >> 3); xb = 15 * (xb >> 3); tb = 255 * (tb >> 7)
    even = ((np.arange(N * TT) & 1) == 0).reshape(N, 1, TT, 1)
    x[:, 5] = 15 * even; xb[:, 5] = 0; x[:, 6] = 0; xb[:, 6] = 0
    x[:, 3] = 15; xb[:, 3] = 15; tb[:, 3] = 255
    x[:, 2] = rng.integers(13, 16, (N, 16, TT, W)); xb[:, 2] = rng.integers(13, 16, (N, 16, W)); tb[:, 2] = rng.integers(240, 256, (N, 16, W))
    c = rng.choice(np.array([0, 1, W // 2, W - 1]), (N, 8, TT, W)); c[:, 4] = W - 1; c[:, 7] = 0; c[:, 2] = rng.integers(0, W, (N, TT, W))
    th = 225 * rng.integers(4, 13, (N, 8, M, TT, W)) + rng.integers(0, 2, (N, 8, M, TT, W))
    th[:, 5] = 3600 + rng.integers(0, 2, (N, M, TT, W)); th[:, 6] = rng.integers(0, 2, (N, M, TT, W)); th[:, 0, :, :, ::5] = 4095; th[:, 1, :, :, ::5] = 0
    th[:, 3] = rng.integers(0, 2, (N, M, TT, W)); th[:, 2] = rng.integers(10, 35, (N, M, TT, W))
    return pack(x, xb, tb, c, th)
def setup_inputs_alike(rng):
    x, xb, tb, c = parts(rng)
    x[:, ::2] = np.take_along_axis(rng.integers(0, 16, (N, 4, 16, TT, 8)), rng.integers(0, 8, (N, 4, 1, TT, W)), 4)
    c[:, 1] = rng.integers(0, W, (N, TT, 1)); c[:, 4] = rng.integers(0, W, (N, TT, 1))
    v = rng.integers(0, 15, 16); e = np.zeros(16, np.int64); e[rng.permutation(16)[:3]] = 1
    odd = (np.arange(N * TT) & 1).reshape(N, 1, TT, 1)
    x[:, 3] = v[None, :, None, None] + odd * e[None, :, None, None]; xb[:, 3] = (v + e)[None, :, None]
    same = (W // 8) * rng.integers(1, 9, (N, TT, W)) - 1
    c[:, 3] = np.where(rng.random((N, TT, W)) < 0.8, same, c[:, 3])
    d = walk(x, xb, c); th = np.clip(d + rng.integers(-60, 61, d.shape), 0, 4095)
    th[:, 3] = rng.integers(2, 6, (N, M, TT, W))
    return pack(x, xb, tb, c, th)
def setup_inputs_spread(rng):
    x, xb, tb, c = parts(rng)
    x = (np.exp2(rng.integers(0, 5, (N, 8, 1, TT, W))) * rng.random(x.shape)).astype(np.int64) * (rng.random((N, 8, 1, TT, W)) > 0.0625)
    xb = (np.exp2(rng.integers(0, 5, (N, 8, 1, W))) * rng.random(xb.shape)).astype(np.int64) * (rng.random((N, 8, 1, W)) > 0.0625)
    tb = np.minimum((np.exp2(8 * rng.random((N, 8, 1, W))) * rng.random(tb.shape)).astype(np.int64), 255)
    th = np.clip(np.exp2(12 * rng.random((N, 8, M, TT, W))).astype(np.int64) - 1, 0, 4095)
    return pack(x, xb, tb, c, th)
def check_inputs(d):
    bad = []
    for k, hi in (("x", 15), ("xb", 15), ("tb", 255), ("c0", W - 1), ("th", 4095)):
        v = np.asarray(d[k]).astype(np.float64)
        if np.min(v) < 0 or np.max(v) > hi: bad.append("range of " + k)
        if np.any(v != np.floor(v)): bad.append("whole numbers in " + k)
    return bad
def reference(x, xb, tb, c0, th):
    X = x.astype(np.float32).astype(np.int64).reshape(N, 8, 16, TT, W)
    prev = xb[0].astype(np.float32).astype(np.int64).reshape(8, 16, W); tau = tb[0].astype(np.float64).reshape(8, 16, W)
    C = np.stack([gentries(a) for a in c0]).astype(np.int64).reshape(N, 8, TT, W); H = np.stack([gentries(a) for a in th]).astype(np.int64).reshape(N, 8, M, TT, W)
    J = np.zeros((N, 8, Q, TT, W), np.int64); Y = []
    for r in range(N):
        for s in range(TT):
            cur = X[r, :, :, s]; cs, ds = tries(prev, cur, C[r, :, s])
            ok = ds < H[r, :, :, s]; n = np.add.accumulate(ok.astype(np.int64), axis=1)
            tot = np.zeros((8, 16, W))
            for q in range(Q):
                hit = ok & (n == q + 1)
                j = np.where(np.any(hit, axis=1), np.add.reduce(np.where(hit, cs, 0), axis=1), cs[:, M - 1])
                J[r, :, q, s] = j; tot = tot + np.take_along_axis(tau, j[:, None, :], 2)
            tau = tot * SC + cur; prev = cur
        Y.append(tau.reshape(128, W))
    return {"yj": np.stack([gtable(a.reshape(8, -1)) for a in J]).astype(np.float32), "ytau": np.stack(Y).astype(np.float32)}

@@ -1,0 +1,481 @@
+from concourse.bass import DstId, RemoteDMATransfer
+from concourse.mybir import AluOpType, ActivationFunctionType
+
+W = 2048
+H = 1024
+NS = 4
+NB = 448
+ASPLIT = 2
+KEY = 16384
+STEP = [(1, 512, 0.0, 0), (3, 224, 0.7, 3), (2, 288, 1.0, 1), (1, 256, 1.9, 0.5), (3, 224, 0.0, 3), (3, 64, 2.4, 3),
+        (2, 320, 0.2, 2), (3, 160, 2.3, 1)]
+STEP0 = [(0, 416, 2.7, 0), (0, 480, 1.8, 0), (0, 128, 0.2, 0), (0, 512, 2.9, 0), (0, 512, 0.5, 0)]
+STEPZ = [(1, 512, 0.4, 3), (3, 288, 0.1, 2), (2, 224, 1.1, 2), (1, 320, 2.5, 0), (3, 192, 0.4, 3), (2, 416, 2.0, 3),
+         (3, 96, 2.6, 3)]
+STORES = [256] * 8
+UNITS = {0: [(0, 0), (0, 1), (2, 0), (2, 1), (4, 1), (5, 1)],
+         1: [(3, 0), (3, 1), (4, 0), (6, 0), (6, 1)],
+         2: [(5, 0), (1, 0), (1, 1)],
+         3: [(7, 0), (7, 1)]}
+RUN = {2: (5, 1, 0), 3: (7, 3, 1)}
+ZBY, ZTO, ZSEG = 1, 3, {2: 101, 6: 125}
+LOADS0 = ["x0a", "x0b", "x1a", "th", "x1b", "tb"]
+N_ = None
+SENDS = [(0, 2, "c", 1, N_, 0), (0, 2, "x", 0, N_, 0), (0, 2, "x", 1, 0, 0), (0, 2, "x", 1, 1, 0), (0, 2, "t", 1, N_, 0),
+         (0, 2, "u", 1, N_, 0), (0, 3, "b", 0, N_, 9), (0, 2, "b", 0, N_, 0), (0, 3, "x", 1, N_, (0, 1)),
+         (2, 1, "x", 4, N_, 0), (2, 1, "l", 4, 0, 0), (2, 3, "x", 0, N_, 0), (2, 1, "x", 5, 0, 0), (2, 1, "x", 5, 1, (1, 1)),
+         (2, 0, "x", 4, N_, 0), (2, 0, "x", 5, 1, 0), (2, 0, "l", 5, 1, 0), (2, 0, "l", 4, 1, 0),
+         (1, 0, "x", 2, N_, 0), (1, 0, "l", 2, N_, 0), (1, 0, "x", 3, N_, 0), (1, 2, "x", 2, N_, (3, 1)), (0, 2, "x", 3, N_, 0),
+         (1, 3, "x", 4, N_, 0), (1, 3, "x", 5, N_, 0),
+         (3, 1, "x", 6, N_, 0), (3, 1, "l", 6, N_, 0), (3, 1, "x", 7, N_, 0)]
+WIDE = {0, 1, 2, 3}
+DUE = {(0, 1): 1, (1, 0): 5, (1, 1): 6, (2, 0): 13, (2, 1): 15, (5, 0): 30, (3, 0): 0, (3, 1): 2, (4, 0): 15, (4, 1): 20,
+       (6, 0): 30, (6, 1): 30, (5, 1): 25}
+UHOLD = {(2, 0): 19, (2, 1): 19, (4, 1): 30}
+PACE, STRETCH = 5.1, 1.3
+
+SCRATCH = {n: ("sbuf", [128, c], d) for n, c, d in [
+    ("X", 9 * W, "bfloat16"), ("TB", W, "bfloat16"), ("TS", W, "bfloat16"), ("XS", 8 * W, "bfloat16"),
+    ("CT", 4096, "int32"), ("JL", 2048, "uint16"), ("JF", 512, "float32"), ("JG", 2048, "float32"),
+    ("V", NS * H, "bfloat16"), ("SQ", NS * H, "bfloat16"), ("OF", NS * 64, "uint16"), ("LI", NS * 384, "int32"),
+    ("LF", NS * 448, "float32"), ("W0", W, "float32"), ("W1", W, "float32"), ("WS", W, "float32"), ("P", W, "float32"),
+    ("Q", W, "float32"), ("ZP", W, "bfloat16"), ("ZQ", W, "bfloat16"), ("ONE", 144, "bfloat16"), ("SEL", 144, "bfloat16"),
+    ("ID", 128, "bfloat16"), ("NID", 128, "bfloat16"), ("ID32", 128, "float32"), ("SID", 8 * 128, "bfloat16")]}
+for _b in range(8):
+    SCRATCH["ps%d" % _b] = ("psum", [128, 512], "float32")
+SEMAPHORES = ["pe", "act", "dve", "pool", "sent"] + ["d%d" % _i for _i in range(70)]
+SIZE = {"bfloat16": 2, "uint16": 2, "int32": 4, "float32": 4}
+
+EST = dict(cyc=1.04e-3, gat=1.56, pe=0.52e-3, fix=0.06, wake=0.12, own=0.08, issue=0.1, rissue=0.7, first=1.5,
+           lat=1.8, rlat=2.0, loc=300e3, chip=150e3, off=85e3, wide=250e3, look=0.1)
+
+
+def A(name, a, b, step=1):
+    return ("ap", name, a, b, step)
+
+
+def IND(win, off):
+    return ("ind", win, off)
+
+
+def cost(o, E):
+    k, n = o["cost"]
+    return {"v": max(64, n) * E["cyc"] + E["fix"] * 0.3, "g": n * E["gat"] * E["cyc"] + E["fix"],
+            "pe": n * E["pe"] + E["fix"] * 0.3, "pool": 0.17 + 2 * n * E["cyc"], "dma": E["issue"], "rdma": E["rissue"]}[k]
+
+
+def build(cores, topo):
+    ops, acc, nsem, jsent = [], {}, {r: 0 for r in range(4)}, {}
+
+    def touch(o, r, ap, wr, rq):
+        if ap[0] == "ind":
+            touch(o, r, ap[1], wr, rq)
+            touch(o, r, ap[2], False, rq)
+            return
+        name, a, b = ap[1], ap[2], ap[3]
+        if name not in SCRATCH:
+            return
+        psum = SCRATCH[name][0] == "psum"
+        lst = acc.setdefault((r, name), [])
+        for (p, pa, pb, pw, pq) in lst:
+            if p is not o and ((pa < b and a < pb and (wr or pw)) or (psum and pq != rq)):
+                hard = not (wr and pq == rq == "pe" and not o["calls"][0][4])
+                o["deps"][p["id"]] = o["deps"].get(p["id"], False) or hard
+        lst.append((o, a, b, wr, rq))
+
+    def op(r, q, calls, reads, writes, c, prio, **kw):
+        o = dict(id=len(ops), r=r, q=q, calls=calls, cost=c, prio=prio, deps={}, **kw)
+        for ap in reads:
+            touch(o, r, ap, False, q)
+        for ap in writes:
+            touch(o, kw.get("to", r), ap, True, "far" if "to" in kw else q)
+        ops.append(o)
+        return o
+
+    def sem(r):
+        nsem[r] += 1
+        return "d%d" % (nsem[r] - 1)
+
+    def width(ap):
+        return 16 * (ap[2][3] - ap[2][2]) if ap[0] == "ind" else (ap[3] - ap[2] + ap[4] - 1) // ap[4]
+
+    def nbytes(ap, other):
+        return 128 * width(ap) * SIZE[SCRATCH[ap[1] if ap[1] in SCRATCH else other[1]][2]]
+
+    def tt(r, out, a, b, alu, pr):
+        n = width(out)
+        c = ("g", n) if a[0] == "ind" else ("v", n if a[1][:2] == "ps" or b[1][:2] == "ps" else 2 * n)
+        return op(r, "dve", [("tt", out, a, b, alu)], [a, b], [out], c, pr)
+
+    def ts(r, out, a, s1, s2, o0, o1, pr):
+        n = width(out) // (2 if SIZE[SCRATCH[a[1]][2]] + SIZE[SCRATCH[out[1]][2]] == 4 else 1)
+        return op(r, "dve", [("ts", out, a, s1, s2, o0, o1)], [a], [out], ("v", n), pr)
+
+    def cp(r, out, a, pr):
+        return op(r, "dve", [("cp", out, a)], [a], [out], ("v", width(out)), pr)
+
+    def act(r, out, a, f, scale, pr):
+        return op(r, "act", [("act", out, a, f, scale)], [a], [out], ("g" if a[0] == "ind" else "v", width(out)), pr)
+
+    def mm(r, lst, pr):
+        n = sum(max(64, width(m[1])) * (4 if SCRATCH[m[2][1]][2] == "float32" else 1) for m in lst)
+        return op(r, "pe", lst, [m[2] for m in lst] + [m[3] for m in lst], [m[1] for m in lst], ("pe", n), pr)
+
+    def dma(r, q, out, src, pr):
+        return op(r, q, [("dma", out, src)], [src], [out], ("dma", 0), pr, sem=sem(r), inc=16,
+                  bytes=nbytes(out, src), pipe="loc")
+
+    def send(r, to, pairs, pr, hold=0.0, wide=False):
+        a, b = cores[r], cores[to]
+        eng = topo.engines(a, b)
+        same = topo.chip(a) == topo.chip(b)
+        if same and not wide:
+            far = [c for c in cores if topo.chip(c) != topo.chip(a)][0]
+            eng = [e for e in eng if e not in topo.engines(a, far)]
+        per = len(eng) // len(pairs)
+        masks = [sum(1 << e for e in eng[i * per:(i + 1) * per]) for i in range(len(pairs))]
+        return op(r, "pool", [("send", b, pairs, masks)], [p[1] for p in pairs], [p[0] for p in pairs], ("rdma", 0), pr,
+                  to=to, sem=sem(to), inc=per * len(pairs), bytes=sum(nbytes(p[0], p[1]) for p in pairs),
+                  pipe="wide" if wide else "chip" if same else "off", hold=hold)
+
+    def xs(t, a=0, b=W):
+        return A("X", (t + 1) * W + a, (t + 1) * W + b)
+
+    def lists(t, h, n=64):
+        c = (t // 2) * 1024 + (t % 2) * 128 + h * 64
+        return [A("CT", c + 256 * m, c + 256 * m + n) for m in range(4)]
+
+    def jl(t, h, q, a=0, b=64):
+        c = t * 256 + h * 128 + q * 64
+        return A("JL", c + a, c + b)
+
+    def jf(t, h, q):
+        c = (q * 2 + t % 2) * 128 + h * 64
+        return A("JF", c, c + 64)
+
+    def sid(t):
+        return A("SID", t * 128, t * 128 + 128)
+
+    ADD, SUB, MUL, MAX, MIN = "add", "subtract", "mult", "max", "min"
+
+    for r in range(4):
+        t0, t1 = 2 * r, 2 * r + 1
+        what = {"th": (A("CT", r * 1024 + 256, r * 1024 + 1024), A("th", 0, 768)), "x0": (xs(t0), A("x", 0, W)),
+                "x0a": (xs(t0, 0, H), A("x", 0, H)), "x0b": (xs(t0, H, W), A("x", H, W)), "xb": (xs(-1), A("xb", 0, W)),
+                "x1a": (xs(t1, 0, H), A("x", W, W + H)), "x1b": (xs(t1, H, W), A("x", W + H, 2 * W)),
+                "tb": (A("TB", 0, W), A("tb", 0, W))}
+        dma(r, "act", A("CT", r * 1024, r * 1024 + 256), A("c0", 0, 256), 0)
+        for i, k in enumerate(["xb"] + LOADS0 if r == 0 else ["x0", "x1a", "x1b", "th"]):
+            dma(r, "sp", what[k][0], what[k][1], i)
+        one, sel, ident = A("ONE", 0, 144), A("SEL", 0, 144), A("ID", 0, 128)
+        op(r, "dve", [("set", one, 1.0)], [], [one], ("v", 72), 0)
+        op(r, "pool", [("sel", ident, A("ONE", 0, 128), [[-1, 128]], "is_equal", 0, 1)], [one], [ident], ("pool", 128), 0)
+        op(r, "pool", [("sel", sel, one, [[-16, 9], [0, 16]], "is_ge", 0, 1)], [one], [sel], ("pool", 144), 1)
+        op(r, "pool", [("sel", sel, sel, [[16, 9], [0, 16]], "is_ge", 15, -1)], [sel], [sel], ("pool", 144), 2)
+        op(r, "pool", [("sel", sel, sel, [[0, 9], [1, 16]], "is_equal", -15, 0)], [sel], [sel], ("pool", 144), 3)
+        ts(r, A("NID", 0, 128), ident, -1.0, None, MUL, None, 0)
+        if r in RUN:
+            cp(r, A("ID32", 0, 128), ident, 1)
+        mine = [t + i for t in ZSEG for i in (0, 1)]
+        for t in range(8):
+            if (r == ZBY and t in mine) or (r == ZTO and t not in mine) or (r in RUN and r != ZTO and t <= RUN[r][0]):
+                ts(r, sid(t), ident, 2.0 ** (t - RUN[ZTO if r == ZBY else r][0]), None, MUL, None, 1)
+
+    before, after = {}, []
+    for i, (r, to, k, t, h, hold) in enumerate(SENDS):
+        if k == "x":
+            aps = [xs(t) if h is None else xs(t, h * H, h * H + H)]
+        elif k == "b":
+            aps = [A("TB", 0, W)]
+        else:
+            aps = lists(t, 0, 128) if h is None else lists(t, h)
+            aps = {"l": aps, "c": aps[:1], "t": aps[1:2], "u": aps[2:]}[k]
+        o = send(r, to, [(a, a) for a in aps], 10 + 0.1 * i, 0.0 if isinstance(hold, tuple) else hold, i in WIDE)
+        if isinstance(hold, tuple):
+            after.append((o, hold))
+        key = (r, o["pipe"] == "off")
+        if key in before:
+            o["deps"].setdefault(before[key], False)
+        before[key] = o["id"]
+
+    def unit(r, t, h, slot, pr):
+        c0, th = lists(t, h)[0], lists(t, h)[1:]
+        prev, o, na = xs(t - 1), slot * H, H - NB
+        bank = "ps%d" % slot
+        d, bsub = A(bank, 448, 512), A(bank, 0, NB)
+        sb, so = "ps%d" % (4 + slot // 2), (slot % 2) * 256
+        pa, k0, k2, mn = [A(sb, so + 64 * i, so + 64 * i + 64) for i in range(4)]
+        off = A("OF", slot * 64, slot * 64 + 64)
+        li, lf = slot * 384, slot * 448
+        e, c, jk, jm = A("LI", li, li + 64), A("LI", li + 64, li + 128), A("LI", li + 128, li + 256), A("LI", li + 256, li + 384)
+        P = [A("LF", lf + 64 * i, lf + 64 * i + 64) for i in range(4)]
+        k1, mx, tq = [A("LF", lf + 64 * i, lf + 64 * i + 64) for i in (4, 5, 6)]
+        cp(r, off, c0, pr)["hold"] = UHOLD.get((t, h), 0.0)
+        ts(r, P[0], c0, 5.0, 1.0 + 3 * KEY, MUL, ADD, pr)
+        for m in range(3):
+            g = A("V", o + na, o + H)
+            act(r, g, IND(prev, A("OF", off[2] + na // 16, off[3])), "Copy", 1.0, pr)
+            mm(r, [("mm", bsub, A("ID", 0, 128), g, True, False),
+                   ("mm", bsub, A("NID", 0, 128), xs(t, h * H + na, h * H + H), False, True)], pr)
+            cuts = [32 * ((na // 32) * i // ASPLIT) for i in range(ASPLIT + 1)]
+            for i in range(ASPLIT):
+                a, b = cuts[i], cuts[i + 1]
+                tt(r, A("V", o + a, o + b), IND(prev, A("OF", off[2] + a // 16, off[2] + b // 16)),
+                   xs(t, h * H + a, h * H + b), SUB, pr)
+                act(r, A("SQ", o + a, o + b), A("V", o + a, o + b), "Square", 1.0, pr)
+            act(r, A("SQ", o + na, o + H), bsub, "Square", 1.0, pr)
+            mm(r, [("mm", d, A("SEL", 15 - p, 143 - p), A("SQ", o + p, o + H, 16), p == 0, p == 15) for p in range(16)], pr)
+            tt(r, e, d, P[m], ADD, pr)
+            tt(r, pa, d, th[m], "is_lt", pr)
+            ts(r, c, e, W - 1, None, "bitwise_and", None, pr)
+            if m < 2:
+                cp(r, off, c, pr)
+            tt(r, (k0, k1, k2)[m], pa, P[m], MUL, pr)
+            ts(r, P[m + 1], c, 5.0, 1.0 + (2 - m) * KEY, MUL, ADD, pr)
+            if m == 1:
+                tt(r, mx, k0, k1, MAX, pr)
+                tt(r, mn, k0, k1, MIN, pr)
+        tt(r, tq, k2, mx, MIN, pr)
+        tt(r, pa, k2, mx, MAX, pr)
+        tt(r, k0, mn, tq, MAX, pr)
+        tt(r, A("LI", jk[2], jk[2] + 64), pa, P[3], MAX, pr)
+        tt(r, A("LI", jk[2] + 64, jk[3]), k0, P[3], MAX, pr)
+        ts(r, jm, jk, KEY - 1, None, "bitwise_and", None, pr)
+        c = t * 256 + h * 128
+        both, own = A("JL", c, c + 128), t // 2
+        ts(r, both, jm, 0.2, None, MUL, None, pr)
+        for k in (3, 2):
+            if k != r and t <= RUN[k][0]:
+                jsent.setdefault((t, h), send(r, k, [(both, both)], 5)["id"])
+        if t - 1 in ZSEG and r != ZBY:
+            send(r, ZBY, [(both, both)], 7)
+        if own == r:
+            for q in range(2):
+                cp(r, jf(t, h, q), jl(t, h, q), pr + 1.5)
+        elif own in RUN:
+            cp(r, A("JG", c, c + 128), both, pr + 1.5)
+            send(r, own, [(jf(t, h, q), A("JG", c + 64 * q, c + 64 * q + 64)) for q in range(2)], 40)
+        else:
+            send(r, own, [(both, both)], 6)
+            for q in range(2):
+                cp(own, jf(t, h, q), jl(t, h, q), 290)
+
+    for r in range(4):
+        for i, (t, h) in enumerate(UNITS[r]):
+            n0 = len(ops)
+            unit(r, t, h, i % NS, 100.0)
+            due, last = DUE.get((t, h), PACE * (t + 0.5 * h)), {}
+            for o in reversed(ops[n0:]):
+                if o["r"] == r and o["q"] != "pool":
+                    x = last.get(o["id"], due + (8.0 if o["prio"] > 101 else 0.0)) - cost(o, EST) * STRETCH
+                    o["prio"] = 100 + x
+                    for j in o["deps"]:
+                        last[j] = min(last.get(j, 1e9), x - EST["wake"])
+    for o, u in after:
+        o["deps"].setdefault(jsent[u], False)
+    for r in range(4):
+        dma(r, "sp", A("yj", 0, 512), A("JF", 0, 512), 900)
+
+    for t, pr in ZSEG.items():
+        for i in range(4):
+            a, b, h = 512 * i, 512 * i + 512, i // 2
+            j1, j2 = [IND(xs(t), jl(t + 1, h, q, (i % 2) * 32, (i % 2) * 32 + 32)) for q in range(2)]
+            p, q, ps = A("ZP", a, b), A("ZQ", a, b), A("ps%d" % (6 + i % 2), 0, 512)
+            z = A("XS", (t + 1) * W + a, (t + 1) * W + b)
+            act(ZBY, p, j1, "Copy", 1.0, pr)
+            tt(ZBY, q, j2, p, ADD, pr)
+            mm(ZBY, [("mm", ps, sid(t), q, True, False), ("mm", ps, sid(t + 1), xs(t + 1, a, b), False, True)], pr)
+            if i % 2:
+                act(ZBY, z, ps, "Copy", 1.0, pr)
+                z = A("XS", (t + 1) * W + h * H, (t + 1) * W + h * H + H)
+                send(ZBY, ZTO, [(z, z)], 8)
+            else:
+                cp(ZBY, z, ps, pr)
+
+    for r in RUN:
+        last, hand, to = RUN[r]
+        sc = 2.0 ** (-1 - last)
+        ts(r, A("TS", 0, 1376), A("TB", 0, 1376), sc, None, MUL, None, 90)
+        act(r, A("TS", 1376, W), A("TB", 1376, W), "Copy", sc, 90)
+        win, nb, i32 = "TS", 6, A("ID32", 0, 128)
+        for t in range(last + 1):
+            out = "WS" if t == hand else ("W0" if win != "W0" else "W1")
+            wn, a, pr = A(win, 0, W), 0, 300 + 10 * t
+            bare, made = r == ZTO and t in ZSEG, r == ZTO and t - 1 in ZSEG
+            for (way, n, pw, late) in (STEP0 if bare else STEPZ if made else STEP):
+                b, h = a + n, a // H
+                j1 = IND(wn, jl(t, h, 0, (a - h * H) // 16, (b - h * H) // 16))
+                j2 = IND(wn, jl(t, h, 1, (a - h * H) // 16, (b - h * H) // 16))
+                p, q, o, pi = A("P", a, b), A("Q", a, b), A(out, a, b), pr + pw
+                x2 = A("XS", t * W + a, t * W + b)
+                if way == 0:
+                    act(r, p, j1, "Copy", 1.0, pi)
+                    tt(r, o, j2, p, ADD, pi)
+                elif way == 1:
+                    if not made:
+                        ts(r, x2, xs(t, a, b), 2.0 ** (t - last), None, MUL, None, pr - 5)
+                    tt(r, q, j2, x2, ADD, pi)
+                    tt(r, o, j1, q, ADD, pi)
+                else:
+                    ps = A("ps%d" % nb, 0, n)
+                    nb = (nb + 1) % 8
+                    mm(r, [("mm", ps, A("ID", 0, 128) if made else sid(t), x2 if made else xs(t, a, b), True, way == 2)], pi + 1)
+                    act(r, p, j1, "Copy", 1.0, pi)
+                    if way == 3:
+                        act(r, q, j2, "Copy", 1.0, pi)
+                        mm(r, [("mm", ps, i32, p, False, False)], pi)
+                    else:
+                        tt(r, q, j2, p, ADD, pi - 1)
+                    if way == 2:
+                        tt(r, o, q, ps, ADD, pi + late)
+                    else:
+                        mm(r, [("mm", ps, i32, q, False, True)], pi)
+                        act(r, o, ps, "Copy", 1.0, pi + late)
+                a = b
+            if t == last:
+                a = 0
+                for n in STORES:
+                    dma(r, "sp", A("ytau", a, a + n), A(out, a, a + n), 950)
+                    a += n
+            if t == hand:
+                for h in range(2):
+                    ws = A("WS", h * H, h * H + H)
+                    send(r, to, [(ws, ws)], 20)
+                    act(to, A("W0", h * H, h * H + H), ws, "Copy", 2.0 ** (last - hand), 295)
+                    dma(to, "sp", A("ytau", h * H, h * H + H), A("W0", h * H, h * H + H), 950)
+            win = out
+    return ops
+
+
+def finish(o, start, E, pipes, seen):
+    end = start + cost(o, E)
+    if "pipe" not in o:
+        return end, end
+    far = o["cost"][0] == "rdma"
+    if far and o["r"] not in seen:
+        seen.add(o["r"])
+        end += E["first"]
+    lat = E["rlat"] if far else E["lat"]
+    sets = [(o["r"], k) for k in {"loc": (0, 1), "off": (0,), "chip": (1,), "wide": (0, 1)}[o["pipe"]]]
+    go = max([end + lat * 0.5] + [pipes.get(k, 0.0) for k in sets])
+    for k in sets:
+        pipes[k] = go + o["bytes"] / E[o["pipe"]]
+    return end, pipes[sets[0]] + lat * 0.5
+
+
+def ready_at(o, ops, done, E):
+    return max([0.0] + [done[i] + (E["own"] if (ops[i]["r"], ops[i]["q"]) == (o["r"], o["q"]) else E["wake"])
+                        for i, hard in o["deps"].items() if hard])
+
+
+def schedule(ops, E):
+    left = {o["id"]: len(o["deps"]) for o in ops}
+    users = {o["id"]: [] for o in ops}
+    for o in ops:
+        for i in o["deps"]:
+            users[i].append(o["id"])
+    ready = {o["id"]: 0.0 for o in ops if not o["deps"]}
+    free, done, pipes, seen, queues = {}, {}, {}, set(), {}
+    while ready:
+        est = {i: max(t, free.get((ops[i]["r"], ops[i]["q"]), 0.0)) for i, t in ready.items()}
+        i0 = min(est, key=lambda i: (est[i], ops[i]["prio"], i))
+        key = (ops[i0]["r"], ops[i0]["q"])
+        i = min((j for j in est if (ops[j]["r"], ops[j]["q"]) == key and est[j] <= est[i0] + E["look"]),
+                key=lambda j: (ops[j]["prio"], j))
+        o = ops[i]
+        free[key], done[i] = finish(o, est[i], E, pipes, seen)
+        o["t"] = (est[i], done[i])
+        queues.setdefault(key, []).append(o)
+        del ready[i]
+        for u in users[i]:
+            left[u] -= 1
+            if not left[u]:
+                ready[u] = max(ready_at(ops[u], ops, done, E), ops[u].get("hold", 0.0))
+    for key, lst in queues.items():
+        n = 0
+        for o in lst:
+            if "sem" not in o:
+                n += 1
+                o["sem"], o["inc"], o["val"] = key[1], 1, n
+            else:
+                o["val"] = o["inc"]
+    return queues
+
+
+PLAN = {}
+
+
+def rank_program(g, core, T, topo):
+    r = T.rank_of(core)
+    if r is None:
+        return
+    if not PLAN:
+        PLAN["ops"] = build(list(T.cores), topo)
+        PLAN["queues"] = schedule(PLAN["ops"], EST)
+    ops, queues = PLAN["ops"], PLAN["queues"]
+    Q = {"pe": g.tensor, "act": g.scalar, "dve": g.vector, "pool": g, "sp": g.sync}
+    ALU = {"add": AluOpType.add, "subtract": AluOpType.subtract, "mult": AluOpType.mult, "max": AluOpType.max,
+           "min": AluOpType.min, "is_lt": AluOpType.is_lt, "is_ge": AluOpType.is_ge, "is_equal": AluOpType.is_equal,
+           "bitwise_and": AluOpType.bitwise_and}
+    FN = {"Copy": ActivationFunctionType.Copy, "Square": ActivationFunctionType.Square}
+
+    def R(ap):
+        if ap[0] == "ind":
+            return R(ap[1]).indirect(R(ap[2]))
+        return T[ap[1]][:, ap[2]:ap[3]] if ap[4] == 1 else T[ap[1]][:, ap[2]:ap[3]:ap[4]]
+
+    total, seen_all, sent = {}, {}, 0
+    for o in ops:
+        if o.get("to", o["r"]) == r:
+            total[o["sem"]] = max(total.get(o["sem"], 0), o["val"])
+    for q in ("sp", "act", "dve", "pe", "pool"):
+        eng, seen = Q[q], {}
+        for o in queues.get((r, q), []):
+            want = {}
+            for i, hard in o["deps"].items():
+                if hard:
+                    want[ops[i]["sem"]] = max(want.get(ops[i]["sem"], 0), ops[i]["val"])
+            for s, v in want.items():
+                if seen.get(s, 0) < v:
+                    eng.wait_ge(T.sem[s], v)
+                    seen[s] = v
+                    seen_all[s] = max(seen_all.get(s, 0), v)
+            ins = None
+            for c in o["calls"]:
+                k = c[0]
+                if k == "tt":
+                    ins = eng.tensor_tensor(R(c[1]), R(c[2]), R(c[3]), ALU[c[4]])
+                elif k == "ts" and c[6] is None:
+                    ins = eng.tensor_scalar(R(c[1]), R(c[2]), c[3], None, ALU[c[5]])
+                elif k == "ts":
+                    ins = eng.tensor_scalar(R(c[1]), R(c[2]), c[3], c[4], ALU[c[5]], ALU[c[6]])
+                elif k == "cp":
+                    ins = eng.tensor_copy(R(c[1]), R(c[2]))
+                elif k == "set":
+                    ins = eng.memset(R(c[1]), c[2])
+                elif k == "act" and c[4] == 1.0:
+                    ins = eng.activation(R(c[1]), R(c[2]), FN[c[3]])
+                elif k == "act":
+                    ins = eng.activation(R(c[1]), R(c[2]), FN[c[3]], scale=c[4])
+                elif k == "mm":
+                    ins = eng.matmul(R(c[1]), R(c[2]), R(c[3]), c[4], c[5])
+                elif k == "sel":
+                    ins = eng.affine_select(R(c[1]), R(c[2]), c[3], ALU[c[4]], 0.0, c[5], c[6])
+                elif k == "dma":
+                    ins = eng.dma_start(R(c[1]), R(c[2]))
+                else:
+                    rid, pid = topo.addr(c[1])[:2]
+                    if len(c[2]) == 1:
+                        eng.remote_dma(R(c[2][0][0]), R(c[2][0][1]), T.sem[o["sem"]], T.sem.sent, pid, rid, c[3][0])
+                    else:
+                        eng.remote_dma_fused(
+                            [RemoteDMATransfer(dst_ids=[DstId(rid=rid, pnc=pid)], dma_engine_mask=m, remote_sem=T.sem[o["sem"]],
+                                               src=R(p[1]), dst=R(p[0])) for p, m in zip(c[2], c[3])], local_sem=T.sem.sent)
+                    sent += o["inc"]
+            if ins is not None:
+                ins.then_inc(T.sem[o["sem"]], o["inc"])
+    if sent:
+        g.wait_ge(T.sem.sent, sent)
+    for s, v in total.items():
+        if seen_all.get(s, 0) < v:
+            g.wait_ge(T.sem[s], v)

@@ -3,55 +3,73 @@ from concourse.mybir import AluOpType, ActivationFunctionType
 
 W = 2048
 H = 1024
-NS = 4
-NB = 448
-ASPLIT = 2
-KEY = 16384
-STEP = [(1, 512, 0.0, 0), (3, 224, 0.7, 3), (2, 288, 1.0, 1), (1, 256, 1.9, 0.5), (3, 224, 0.0, 3), (3, 64, 2.4, 3),
-        (2, 320, 0.2, 2), (3, 160, 2.3, 1)]
-STEP0 = [(0, 416, 2.7, 0), (0, 480, 1.8, 0), (0, 128, 0.2, 0), (0, 512, 2.9, 0), (0, 512, 0.5, 0)]
-STEPZ = [(1, 512, 0.4, 3), (3, 288, 0.1, 2), (2, 224, 1.1, 2), (1, 320, 2.5, 0), (3, 192, 0.4, 3), (2, 416, 2.0, 3),
-         (3, 96, 2.6, 3)]
-STORES = [256] * 8
-UNITS = {0: [(0, 0), (0, 1), (2, 0), (2, 1), (4, 1), (5, 1)],
-         1: [(3, 0), (3, 1), (4, 0), (6, 0), (6, 1)],
-         2: [(5, 0), (1, 0), (1, 1)],
-         3: [(7, 0), (7, 1)]}
-RUN = {2: (5, 1, 0), 3: (7, 3, 1)}
-ZBY, ZTO, ZSEG = 1, 3, {2: 101, 6: 125}
-LOADS0 = ["x0a", "x0b", "x1a", "th", "x1b", "tb"]
+NS = 6
+ONEP = 1.0 + 2.0 ** -9
+BIG = 1.5 * 2.0 ** 34
+LEVEL3 = 13
+DIAG = [5, ONEP, 1, -5, -0.5, -W] + [w * W for w in (19, 17, 15, 10.5, 5, 10)]
+CHAIN = {0: 0, 2: 1, 1: 0, 3: 1}
+ACROSS = {0: 1, 2: 3}
+
 N_ = None
-SENDS = [(0, 2, "c", 1, N_, 0), (0, 2, "x", 0, N_, 0), (0, 2, "x", 1, 0, 0), (0, 2, "x", 1, 1, 0), (0, 2, "t", 1, N_, 0),
-         (0, 2, "u", 1, N_, 0), (0, 3, "b", 0, N_, 9), (0, 2, "b", 0, N_, 0), (0, 3, "x", 1, N_, (0, 1)),
-         (2, 1, "x", 4, N_, 0), (2, 1, "l", 4, 0, 0), (2, 3, "x", 0, N_, 0), (2, 1, "x", 5, 0, 0), (2, 1, "x", 5, 1, (1, 1)),
-         (2, 0, "x", 4, N_, 0), (2, 0, "x", 5, 1, 0), (2, 0, "l", 5, 1, 0), (2, 0, "l", 4, 1, 0),
-         (1, 0, "x", 2, N_, 0), (1, 0, "l", 2, N_, 0), (1, 0, "x", 3, N_, 0), (1, 2, "x", 2, N_, (3, 1)), (0, 2, "x", 3, N_, 0),
-         (1, 3, "x", 4, N_, 0), (1, 3, "x", 5, N_, 0),
-         (3, 1, "x", 6, N_, 0), (3, 1, "l", 6, N_, 0), (3, 1, "x", 7, N_, 0)]
-WIDE = {0, 1, 2, 3}
-DUE = {(0, 1): 1, (1, 0): 5, (1, 1): 6, (2, 0): 13, (2, 1): 15, (5, 0): 30, (3, 0): 0, (3, 1): 2, (4, 0): 15, (4, 1): 20,
-       (6, 0): 30, (6, 1): 30, (5, 1): 25}
-UHOLD = {(2, 0): 19, (2, 1): 19, (4, 1): 30}
-PACE, STRETCH = 5.1, 1.3
+CFG = dict(
+    NB=352, ASPLIT=2, STRETCH=1.0, HOLD={}, BIAS={}, ROUNDS=0,
+    UNITS={0: [(0, 0, H), (0, H, W), (1, 0, H), (2, 0, H), (6, H, W)],
+           2: [(5, 0, H), (1, H, W), (2, H, W), (4, H, W), (5, H, W)],
+           1: [(3, 0, H), (3, H, W), (4, 0, H)],
+           3: [(7, 0, H), (7, H, W), (6, 0, H)]},
+    STEP=[(1, 256, "cp"), (2, 256, "pq"), (2, 256, "pq"), (2, 256, "pq")],
+    STEP0=[(5, 256, "v"), (4, 256, "v"), (4, 256, "v"), (4, 256, "v")],
+    STEPL=[(1, 256, ""), (3, 256, ""), (2, 256, ""), (2, 256, "")],
+    OUT=[512, 512], LAST=[512, 256, 256],
+    IO=[(0, N_, "c", 0), (0, N_, "x", -1, 0, W, 0), (0, N_, "x", 0, 0, H, 0), (0, N_, "x", 0, H, W, 0), (0, N_, "t", 0, 1, 0),
+        (0, N_, "F", -1, 0, 0, 2), (0, N_, "F", -1, 1, 1, 2), (0, N_, "x", 1, 0, W, 2), (0, N_, "t", 1, 3, 2),
+        (0, N_, "F", 0, 0, 2, 2), (0, N_, "F", 1, 0, 3, 2),
+        (1, N_, "c", 0), (1, N_, "x", 2, 0, W, 0), (1, N_, "x", 3, 0, W, 0), (1, N_, "t", 0, 3, 0),
+        (1, N_, "F", 2, 1, 2, 1), (1, N_, "F", 3, 1, 3, 0),
+        (2, N_, "c", 0), (2, N_, "x", 4, 0, W, 0), (2, N_, "x", 5, 0, W, 0), (2, N_, "t", 0, 3, 0),
+        (3, N_, "c", 0), (3, N_, "x", 6, 0, W, 0), (3, N_, "x", 7, 0, W, 0), (3, N_, "t", 0, 3, 0),
+        (3, N_, "F", 6, 0, 6, 1), (3, N_, "F", 7, 0, 7, 0),
+        (0, 2, "c", 1, H, W, False), (0, 2, "x", 0, 0, W, True), (0, 1, "f", -1, 0, False), (0, 3, "f", -1, 1, False),
+        (0, 2, "x", 1, 0, W, False), (0, 2, "t", 1, H, W, False), (0, 2, "u", 1, H, W, False),
+        (0, 1, "f", 0, 2, False), (0, 1, "f", 1, 3, False),
+        (2, 1, "x", 4, 0, H, False), (2, 1, "l", 4, 0, H, False), (2, 3, "x", 5, 0, W, False),
+        (2, N_, "R", 0, 1, 0, 0), (2, 3, "f", 0, 0, False), (2, N_, "R", 1, 1, 1, 0), (2, 3, "f", 1, 1, False),
+        (2, 0, "x", 5, 0, W, False),
+        (2, N_, "F", 4, 0, 2, 0), (2, N_, "F", 4, 1, 3, 0), (2, N_, "F", 5, 0, 4, 0),
+        (2, 1, "f", 4, 2, False), (2, 3, "f", 4, 3, False), (2, 1, "f", 5, 4, False),
+        (1, 0, "x", 2, 0, H, False), (1, 2, "x", 2, H, W, False), (1, 0, "l", 2, 0, H, False), (1, 2, "l", 2, H, W, False),
+        (1, 2, "x", 3, 0, W, False), (1, 3, "f", 2, 2, False), (1, 3, "f", 3, 3, False),
+        (3, 0, "x", 6, H, W, False), (3, 0, "l", 6, H, W, False), (3, 1, "f", 6, 6, False), (3, 1, "f", 7, 7, False)],
+)
 
 SCRATCH = {n: ("sbuf", [128, c], d) for n, c, d in [
-    ("X", 9 * W, "bfloat16"), ("TB", W, "bfloat16"), ("TS", W, "bfloat16"), ("XS", 8 * W, "bfloat16"),
-    ("CT", 4096, "int32"), ("JL", 2048, "uint16"), ("JF", 512, "float32"), ("JG", 2048, "float32"),
+    ("X", 9 * W, "bfloat16"), ("TB", W, "bfloat16"), ("FX", 8 * H, "bfloat16"), ("XS", 8 * 256, "bfloat16"),
+    ("CT", 4096, "int32"), ("CQ", 4096, "float16"), ("JL", 2048, "uint16"), ("OFF", 1024, "uint16"), ("JF", 512, "float32"), ("JG", 2048, "float32"),
     ("V", NS * H, "bfloat16"), ("SQ", NS * H, "bfloat16"), ("OF", NS * 64, "uint16"), ("LI", NS * 384, "int32"),
-    ("LF", NS * 448, "float32"), ("W0", W, "float32"), ("W1", W, "float32"), ("WS", W, "float32"), ("P", W, "float32"),
-    ("Q", W, "float32"), ("ZP", W, "bfloat16"), ("ZQ", W, "bfloat16"), ("ONE", 144, "bfloat16"), ("SEL", 144, "bfloat16"),
-    ("ID", 128, "bfloat16"), ("NID", 128, "bfloat16"), ("ID32", 128, "float32"), ("SID", 8 * 128, "bfloat16")]}
+    ("LF", NS * 256, "float32"), ("LB", NS * 256, "float16"), ("LC", NS * 192, "float16"), ("O16", 128, "float16"),
+    ("KM", 128 * len(DIAG), "float16"), ("WN", 4 * W, "float32"), ("P", H, "float32"), ("Q", H, "float32"),
+    ("PB", H, "bfloat16"), ("QB", H, "bfloat16"), ("QH", H, "float16"), ("UH", H, "float16"), ("UL", H, "float16"),
+    ("LA", 2 * H, "float32"), ("YS", 2 * H, "float32"),
+    ("ONE", 256, "bfloat16"), ("SEL", 144, "bfloat16"), ("ID", 128, "bfloat16"), ("NID", 128, "bfloat16"),
+    ("EYE", 256, "bfloat16"), ("EM", 256, "bfloat16"), ("ET", 8 * 256, "bfloat16"), ("ID32", 128, "float32"),
+    ("RO32", 128, "float32"), ("IL32", 128, "float32"), ("ID16", 128, "float16"), ("RO16", 128, "float16"), ("IB", 256, "bfloat16"),
+    ("IS", 256, "bfloat16"), ("U16", 4 * H, "uint16")]}
 for _b in range(8):
     SCRATCH["ps%d" % _b] = ("psum", [128, 512], "float32")
-SEMAPHORES = ["pe", "act", "dve", "pool", "sent"] + ["d%d" % _i for _i in range(70)]
-SIZE = {"bfloat16": 2, "uint16": 2, "int32": 4, "float32": 4}
+SEMAPHORES = ["pe", "act", "dve", "pool", "sent"] + ["d%d" % _i for _i in range(90)]
+SIZE = {"bfloat16": 2, "float16": 2, "uint16": 2, "int32": 4, "float32": 4}
 
 EST = dict(cyc=1.04e-3, gat=1.56, pe=0.52e-3, fix=0.06, wake=0.12, own=0.08, issue=0.1, rissue=0.7, first=1.5,
-           lat=1.8, rlat=2.0, loc=300e3, chip=150e3, off=85e3, wide=250e3, look=0.1)
+           lat=1.8, rlat=2.0, loc=300e3, chip=150e3, off=85e3, wide=250e3, look=0.1, eng=0.0, row=0.0, far=0.0)
 
 
-def A(name, a, b, step=1):
-    return ("ap", name, a, b, step)
+def A(name, a, b, step=1, p0=0, p1=128):
+    return ("ap", name, a, b, step, p0, p1)
+
+
+def blk(ap, k):
+    return ap[:5] + (64 * k, 64 * k + 64)
 
 
 def IND(win, off):
@@ -61,30 +79,39 @@ def IND(win, off):
 def cost(o, E):
     k, n = o["cost"]
     return {"v": max(64, n) * E["cyc"] + E["fix"] * 0.3, "g": n * E["gat"] * E["cyc"] + E["fix"],
-            "pe": n * E["pe"] + E["fix"] * 0.3, "pool": 0.17 + 2 * n * E["cyc"], "dma": E["issue"], "rdma": E["rissue"]}[k]
+            "pe": n * E["pe"] + E["fix"] * 0.3, "pool": 0.17 + 2 * n * E["cyc"], "dma": E["issue"], "rdma": E["rissue"],
+            "none": 0.0}[k]
 
 
-def build(cores, topo):
-    ops, acc, nsem, jsent = [], {}, {r: 0 for r in range(4)}, {}
+def with_helpers(cores, topo):
+    return list(cores) + [[c for c in topo.cores_of(k) if topo.die(c) == topo.die(k) and c not in cores][0] for k in cores]
+
+
+def build(cores, topo, C):
+    cores = with_helpers(cores, topo)
+    ops, acc, nsem, job, chain = [], {}, {r: 0 for r in range(len(cores))}, [None], {}
+
+    ahead = [0.0]
 
     def touch(o, r, ap, wr, rq):
         if ap[0] == "ind":
             touch(o, r, ap[1], wr, rq)
             touch(o, r, ap[2], False, rq)
             return
-        name, a, b = ap[1], ap[2], ap[3]
+        name, a, b, p0, p1 = ap[1], ap[2], ap[3], ap[5], ap[6]
         if name not in SCRATCH:
             return
         psum = SCRATCH[name][0] == "psum"
         lst = acc.setdefault((r, name), [])
-        for (p, pa, pb, pw, pq) in lst:
-            if p is not o and ((pa < b and a < pb and (wr or pw)) or (psum and pq != rq)):
+        for (p, pa, pb, q0, q1, pw, pq) in lst:
+            if p is not o and ((pa < b and a < pb and q0 < p1 and p0 < q1 and (wr or pw)) or (psum and pq != rq)):
+                assert not ("to" in p and p["to"] != o["r"]), "the source of a remote write is never overwritten"
                 hard = not (wr and pq == rq == "pe" and not o["calls"][0][4])
                 o["deps"][p["id"]] = o["deps"].get(p["id"], False) or hard
-        lst.append((o, a, b, wr, rq))
+        lst.append((o, a, b, p0, p1, wr, rq))
 
-    def op(r, q, calls, reads, writes, c, prio, **kw):
-        o = dict(id=len(ops), r=r, q=q, calls=calls, cost=c, prio=prio, deps={}, **kw)
+    def op(r, q, calls, reads, writes, c, **kw):
+        o = dict(id=len(ops), r=r, q=q, calls=calls, cost=c, deps={}, job=job[0], ahead=ahead[0], **kw)
         for ap in reads:
             touch(o, r, ap, False, q)
         for ap in writes:
@@ -99,251 +126,524 @@ def build(cores, topo):
     def width(ap):
         return 16 * (ap[2][3] - ap[2][2]) if ap[0] == "ind" else (ap[3] - ap[2] + ap[4] - 1) // ap[4]
 
-    def nbytes(ap, other):
-        return 128 * width(ap) * SIZE[SCRATCH[ap[1] if ap[1] in SCRATCH else other[1]][2]]
+    def size(ap):
+        return SIZE[SCRATCH[ap[1]][2]]
 
-    def tt(r, out, a, b, alu, pr):
+    def nbytes(ap, other):
+        return (ap[6] - ap[5]) * width(ap) * size(ap if ap[1] in SCRATCH else other)
+
+    def tt(r, out, a, b, alu):
         n = width(out)
         c = ("g", n) if a[0] == "ind" else ("v", n if a[1][:2] == "ps" or b[1][:2] == "ps" else 2 * n)
-        return op(r, "dve", [("tt", out, a, b, alu)], [a, b], [out], c, pr)
+        return op(r, "dve", [("tt", out, a, b, alu)], [a, b], [out], c)
 
-    def ts(r, out, a, s1, s2, o0, o1, pr):
-        n = width(out) // (2 if SIZE[SCRATCH[a[1]][2]] + SIZE[SCRATCH[out[1]][2]] == 4 else 1)
-        return op(r, "dve", [("ts", out, a, s1, s2, o0, o1)], [a], [out], ("v", n), pr)
+    def ts(r, out, a, s1, s2, o0, o1=None):
+        n = width(out) // (2 if size(a) + size(out) == 4 else 1)
+        return op(r, "dve", [("ts", out, a, s1, s2, o0, o1)], [a], [out], ("v", n))
 
-    def cp(r, out, a, pr):
-        return op(r, "dve", [("cp", out, a)], [a], [out], ("v", width(out)), pr)
+    def cp(r, out, a):
+        n = width(out) // (2 if a[0] != "ind" and size(a) + size(out) == 4 else 1)
+        return op(r, "dve", [("cp", out, a)], [a], [out], ("g" if a[0] == "ind" else "v", n))
 
-    def act(r, out, a, f, scale, pr):
-        return op(r, "act", [("act", out, a, f, scale)], [a], [out], ("g" if a[0] == "ind" else "v", width(out)), pr)
+    def act(r, out, a, f="Copy", scale=1.0):
+        return op(r, "act", [("act", out, a, f, scale)], [a], [out], ("g" if a[0] == "ind" else "v", width(out)))
 
-    def mm(r, lst, pr):
-        n = sum(max(64, width(m[1])) * (4 if SCRATCH[m[2][1]][2] == "float32" else 1) for m in lst)
-        return op(r, "pe", lst, [m[2] for m in lst] + [m[3] for m in lst], [m[1] for m in lst], ("pe", n), pr)
+    def mm(r, lst):
+        n = sum(max(64, width(m[1])) * (4 if size(m[2]) == 4 else 1) for m in lst)
+        return op(r, "pe", lst, [m[2] for m in lst] + [m[3] for m in lst], [m[1] for m in lst], ("pe", n))
 
-    def dma(r, q, out, src, pr):
-        return op(r, q, [("dma", out, src)], [src], [out], ("dma", 0), pr, sem=sem(r), inc=16,
-                  bytes=nbytes(out, src), pipe="loc")
+    def follow(o, key):
+        if key in chain:
+            o["deps"].setdefault(chain[key], False)
+        chain[key] = o["id"]
 
-    def send(r, to, pairs, pr, hold=0.0, wide=False):
+    def dma(r, q, pairs):
+        return [op(r, q, [("dma", out, src)], [src], [out], ("dma", 0), sem=sem(r), inc=16, bytes=nbytes(out, src), pipe="loc")
+                for out, src in pairs]
+
+    def send(r, to, pairs, wide=False, half=None):
         a, b = cores[r], cores[to]
         eng = topo.engines(a, b)
         same = topo.chip(a) == topo.chip(b)
         if same and not wide:
             far = [c for c in cores if topo.chip(c) != topo.chip(a)][0]
             eng = [e for e in eng if e not in topo.engines(a, far)]
+        if half is not None:
+            eng = eng[half * len(eng) // 2:(half + 1) * len(eng) // 2]
         per = len(eng) // len(pairs)
         masks = [sum(1 << e for e in eng[i * per:(i + 1) * per]) for i in range(len(pairs))]
-        return op(r, "pool", [("send", b, pairs, masks)], [p[1] for p in pairs], [p[0] for p in pairs], ("rdma", 0), pr,
-                  to=to, sem=sem(to), inc=per * len(pairs), bytes=sum(nbytes(p[0], p[1]) for p in pairs),
-                  pipe="wide" if wide else "chip" if same else "off", hold=hold)
+        return op(r, "pool", [("send", b, pairs, masks)], [p[1] for p in pairs], [p[0] for p in pairs], ("rdma", 0),
+                  to=to, sem=sem(to), inc=per * len(pairs), rows=128 // per, bytes=sum(nbytes(p[0], p[1]) for p in pairs),
+                  pipe="wide" if wide and same else "chip" if same else "off")
 
     def xs(t, a=0, b=W):
         return A("X", (t + 1) * W + a, (t + 1) * W + b)
 
-    def lists(t, h, n=64):
-        c = (t // 2) * 1024 + (t % 2) * 128 + h * 64
-        return [A("CT", c + 256 * m, c + 256 * m + n) for m in range(4)]
+    def lists(t, a, b):
+        c = (t // 2) * 1024 + (t % 2) * 128
+        return [A("CT", c + 256 * m + a // 16, c + 256 * m + b // 16) for m in range(4)]
 
-    def jl(t, h, q, a=0, b=64):
-        c = t * 256 + h * 128 + q * 64
-        return A("JL", c + a, c + b)
+    def packed(t, a, b):
+        c, n = t * 512 + a // 4, (b - a) // 16
+        return [A("CQ", c + m * n, c + m * n + n) for m in range(4)]
 
-    def jf(t, h, q):
-        c = (q * 2 + t % 2) * 128 + h * 64
-        return A("JF", c, c + 64)
+    pack = {(e[1], e[3], e[4]) for e in C["IO"] if e[2] == "q"}
 
-    def sid(t):
-        return A("SID", t * 128, t * 128 + 128)
+    def fx(k, a=0, b=H):
+        return A("FX", k * H + a, k * H + b)
 
-    ADD, SUB, MUL, MAX, MIN = "add", "subtract", "mult", "max", "min"
+    folded = {(e[1], e[3]) for e in C["IO"] if e[2] == "f"}
+    span = {r: range(C["HANDT"] + 1) if r in ACROSS else range(C["HANDT"] + 1, 8) for r in CHAIN}
 
-    for r in range(4):
-        t0, t1 = 2 * r, 2 * r + 1
-        what = {"th": (A("CT", r * 1024 + 256, r * 1024 + 1024), A("th", 0, 768)), "x0": (xs(t0), A("x", 0, W)),
-                "x0a": (xs(t0, 0, H), A("x", 0, H)), "x0b": (xs(t0, H, W), A("x", H, W)), "xb": (xs(-1), A("xb", 0, W)),
-                "x1a": (xs(t1, 0, H), A("x", W, W + H)), "x1b": (xs(t1, H, W), A("x", W + H, 2 * W)),
-                "tb": (A("TB", 0, W), A("tb", 0, W))}
-        dma(r, "act", A("CT", r * 1024, r * 1024 + 256), A("c0", 0, 256), 0)
-        for i, k in enumerate(["xb"] + LOADS0 if r == 0 else ["x0", "x1a", "x1b", "th"]):
-            dma(r, "sp", what[k][0], what[k][1], i)
-        one, sel, ident = A("ONE", 0, 144), A("SEL", 0, 144), A("ID", 0, 128)
-        op(r, "dve", [("set", one, 1.0)], [], [one], ("v", 72), 0)
-        op(r, "pool", [("sel", ident, A("ONE", 0, 128), [[-1, 128]], "is_equal", 0, 1)], [one], [ident], ("pool", 128), 0)
-        op(r, "pool", [("sel", sel, one, [[-16, 9], [0, 16]], "is_ge", 0, 1)], [one], [sel], ("pool", 144), 1)
-        op(r, "pool", [("sel", sel, sel, [[16, 9], [0, 16]], "is_ge", 15, -1)], [sel], [sel], ("pool", 144), 2)
-        op(r, "pool", [("sel", sel, sel, [[0, 9], [1, 16]], "is_equal", -15, 0)], [sel], [sel], ("pool", 144), 3)
-        ts(r, A("NID", 0, 128), ident, -1.0, None, MUL, None, 0)
-        if r in RUN:
-            cp(r, A("ID32", 0, 128), ident, 1)
-        mine = [t + i for t in ZSEG for i in (0, 1)]
-        for t in range(8):
-            if (r == ZBY and t in mine) or (r == ZTO and t not in mine) or (r in RUN and r != ZTO and t <= RUN[r][0]):
-                ts(r, sid(t), ident, 2.0 ** (t - RUN[ZTO if r == ZBY else r][0]), None, MUL, None, 1)
+    def xscale(r, t):
+        return 2.0 ** (t + 1 if r in ACROSS else t - C["REF"] if t < 7 else 0)
 
-    before, after = {}, []
-    for i, (r, to, k, t, h, hold) in enumerate(SENDS):
-        if k == "x":
-            aps = [xs(t) if h is None else xs(t, h * H, h * H + H)]
-        elif k == "b":
-            aps = [A("TB", 0, W)]
-        else:
-            aps = lists(t, 0, 128) if h is None else lists(t, h)
-            aps = {"l": aps, "c": aps[:1], "t": aps[1:2], "u": aps[2:]}[k]
-        o = send(r, to, [(a, a) for a in aps], 10 + 0.1 * i, 0.0 if isinstance(hold, tuple) else hold, i in WIDE)
-        if isinstance(hold, tuple):
-            after.append((o, hold))
-        key = (r, o["pipe"] == "off")
-        if key in before:
-            o["deps"].setdefault(before[key], False)
-        before[key] = o["id"]
+    ADD, SUB, MUL, MAX, AND = "add", "subtract", "mult", "max", "bitwise_and"
 
-    def unit(r, t, h, slot, pr):
-        c0, th = lists(t, h)[0], lists(t, h)[1:]
-        prev, o, na = xs(t - 1), slot * H, H - NB
-        bank = "ps%d" % slot
-        d, bsub = A(bank, 448, 512), A(bank, 0, NB)
-        sb, so = "ps%d" % (4 + slot // 2), (slot % 2) * 256
-        pa, k0, k2, mn = [A(sb, so + 64 * i, so + 64 * i + 64) for i in range(4)]
-        off = A("OF", slot * 64, slot * 64 + 64)
-        li, lf = slot * 384, slot * 448
-        e, c, jk, jm = A("LI", li, li + 64), A("LI", li + 64, li + 128), A("LI", li + 128, li + 256), A("LI", li + 256, li + 384)
-        P = [A("LF", lf + 64 * i, lf + 64 * i + 64) for i in range(4)]
-        k1, mx, tq = [A("LF", lf + 64 * i, lf + 64 * i + 64) for i in (4, 5, 6)]
-        cp(r, off, c0, pr)["hold"] = UHOLD.get((t, h), 0.0)
-        ts(r, P[0], c0, 5.0, 1.0 + 3 * KEY, MUL, ADD, pr)
-        for m in range(3):
-            g = A("V", o + na, o + H)
-            act(r, g, IND(prev, A("OF", off[2] + na // 16, off[3])), "Copy", 1.0, pr)
-            mm(r, [("mm", bsub, A("ID", 0, 128), g, True, False),
-                   ("mm", bsub, A("NID", 0, 128), xs(t, h * H + na, h * H + H), False, True)], pr)
-            cuts = [32 * ((na // 32) * i // ASPLIT) for i in range(ASPLIT + 1)]
-            for i in range(ASPLIT):
-                a, b = cuts[i], cuts[i + 1]
-                tt(r, A("V", o + a, o + b), IND(prev, A("OF", off[2] + a // 16, off[2] + b // 16)),
-                   xs(t, h * H + a, h * H + b), SUB, pr)
-                act(r, A("SQ", o + a, o + b), A("V", o + a, o + b), "Square", 1.0, pr)
-            act(r, A("SQ", o + na, o + H), bsub, "Square", 1.0, pr)
-            mm(r, [("mm", d, A("SEL", 15 - p, 143 - p), A("SQ", o + p, o + H, 16), p == 0, p == 15) for p in range(16)], pr)
-            tt(r, e, d, P[m], ADD, pr)
-            tt(r, pa, d, th[m], "is_lt", pr)
-            ts(r, c, e, W - 1, None, "bitwise_and", None, pr)
-            if m < 2:
-                cp(r, off, c, pr)
-            tt(r, (k0, k1, k2)[m], pa, P[m], MUL, pr)
-            ts(r, P[m + 1], c, 5.0, 1.0 + (2 - m) * KEY, MUL, ADD, pr)
-            if m == 1:
-                tt(r, mx, k0, k1, MAX, pr)
-                tt(r, mn, k0, k1, MIN, pr)
-        tt(r, tq, k2, mx, MIN, pr)
-        tt(r, pa, k2, mx, MAX, pr)
-        tt(r, k0, mn, tq, MAX, pr)
-        tt(r, A("LI", jk[2], jk[2] + 64), pa, P[3], MAX, pr)
-        tt(r, A("LI", jk[2] + 64, jk[3]), k0, P[3], MAX, pr)
-        ts(r, jm, jk, KEY - 1, None, "bitwise_and", None, pr)
-        c = t * 256 + h * 128
-        both, own = A("JL", c, c + 128), t // 2
-        ts(r, both, jm, 0.2, None, MUL, None, pr)
-        for k in (3, 2):
-            if k != r and t <= RUN[k][0]:
-                jsent.setdefault((t, h), send(r, k, [(both, both)], 5)["id"])
-        if t - 1 in ZSEG and r != ZBY:
-            send(r, ZBY, [(both, both)], 7)
-        if own == r:
-            for q in range(2):
-                cp(r, jf(t, h, q), jl(t, h, q), pr + 1.5)
-        elif own in RUN:
-            cp(r, A("JG", c, c + 128), both, pr + 1.5)
-            send(r, own, [(jf(t, h, q), A("JG", c + 64 * q, c + 64 * q + 64)) for q in range(2)], 40)
-        else:
-            send(r, own, [(both, both)], 6)
-            for q in range(2):
-                cp(own, jf(t, h, q), jl(t, h, q), 290)
-
-    for r in range(4):
-        for i, (t, h) in enumerate(UNITS[r]):
-            n0 = len(ops)
-            unit(r, t, h, i % NS, 100.0)
-            due, last = DUE.get((t, h), PACE * (t + 0.5 * h)), {}
-            for o in reversed(ops[n0:]):
-                if o["r"] == r and o["q"] != "pool":
-                    x = last.get(o["id"], due + (8.0 if o["prio"] > 101 else 0.0)) - cost(o, EST) * STRETCH
-                    o["prio"] = 100 + x
-                    for j in o["deps"]:
-                        last[j] = min(last.get(j, 1e9), x - EST["wake"])
-    for o, u in after:
-        o["deps"].setdefault(jsent[u], False)
-    for r in range(4):
-        dma(r, "sp", A("yj", 0, 512), A("JF", 0, 512), 900)
-
-    for t, pr in ZSEG.items():
-        for i in range(4):
-            a, b, h = 512 * i, 512 * i + 512, i // 2
-            j1, j2 = [IND(xs(t), jl(t + 1, h, q, (i % 2) * 32, (i % 2) * 32 + 32)) for q in range(2)]
-            p, q, ps = A("ZP", a, b), A("ZQ", a, b), A("ps%d" % (6 + i % 2), 0, 512)
-            z = A("XS", (t + 1) * W + a, (t + 1) * W + b)
-            act(ZBY, p, j1, "Copy", 1.0, pr)
-            tt(ZBY, q, j2, p, ADD, pr)
-            mm(ZBY, [("mm", ps, sid(t), q, True, False), ("mm", ps, sid(t + 1), xs(t + 1, a, b), False, True)], pr)
-            if i % 2:
-                act(ZBY, z, ps, "Copy", 1.0, pr)
-                z = A("XS", (t + 1) * W + h * H, (t + 1) * W + h * H + H)
-                send(ZBY, ZTO, [(z, z)], 8)
+    loads = {r: [] for r in range(len(cores))}
+    for e in C["IO"]:
+        r, to, k = e[:3]
+        job[0] = ("io", r)
+        if to is None:
+            ct = r * 1024
+            if k == "x":
+                t, a, b = e[3:6]
+                pairs = [(xs(t, a, b), A("xb", a, b) if t < 0 else A("x", (t % 2) * W + a, (t % 2) * W + b))]
+            elif k == "c":
+                pairs = [(A("CT", ct, ct + 256), A("c0", 0, 256))]
+            elif k == "t":
+                pairs = [(A("CT", ct + 256 + 256 * e[3], ct + 256 + 256 * e[4]), A("th", 256 * e[3], 256 * e[4]))]
+            elif k == "B":
+                pairs = [(blk(A("TB", H * (h ^ j), H * (h ^ j) + H), j), blk(A("tb", H * h, H * h + H), 0))
+                         for h in range(2) for j in range(2)]
             else:
-                cp(ZBY, z, ps, pr)
+                t, fb, slot = e[3:6]
+                src = [A("tb", h * H, h * H + H) if t < 0 else xs(t, h * H, h * H + H) if k == "R" else
+                       A("x", (t % 2) * W + h * H, (t % 2) * W + h * H + H) for h in range(2)]
+                pairs = [(blk(fx(slot), h), blk(src[h], fb)) for h in range(2)]
+            q = "act" if k == "c" else "sp"
+            made = dma(r, q, pairs)
+            for o in made:
+                follow(o, (r, q))
+                if e[-1]:
+                    o["deps"][loads[r][-e[-1]]["id"]] = True
+            loads[r].append(made[-1])
+            continue
+        if k == "x":
+            pairs = [(xs(*e[3:6]), xs(*e[3:6]))]
+        elif k == "q":
+            job[0] = ("pack", r)
+            for m, (src, dst) in enumerate(zip(lists(*e[3:6]), packed(*e[3:6]))):
+                ts(r, dst, src, -float(W if m else H), None, ADD)
+            job[0] = ("io", r)
+            tile = A("CQ", packed(*e[3:6])[0][2], packed(*e[3:6])[3][3])
+            pairs = [(tile, tile)]
+        elif k == "g":
+            pairs = [(fx(e[3]), fx(e[3]))]
+        elif k == "f":
+            pairs = [(A("TB", 0, H) if e[3] < 0 else fx(e[3]), fx(e[4]))]
+        else:
+            aps = lists(*e[3:6])
+            pairs = [(p, p) for p in {"l": aps, "c": aps[:1], "t": aps[1:2], "u": aps[2:]}[k]]
+        o = send(r, to, pairs, e[-2])
+        o["hold"] = e[-1]
+        follow(o, (r, o["pipe"] == "off"))
+        if k == "f" and e[3] < 0:
+            job[0] = ("tb", to)
+            cp(to, blk(A("TB", H, W), 1), blk(A("TB", 0, H), 0))
+            cp(to, blk(A("TB", H, H + 640), 0), blk(A("TB", 0, 640), 1))
+            act(to, blk(A("TB", H + 640, W), 0), blk(A("TB", 640, H), 1))
 
-    for r in RUN:
-        last, hand, to = RUN[r]
-        sc = 2.0 ** (-1 - last)
-        ts(r, A("TS", 0, 1376), A("TB", 0, 1376), sc, None, MUL, None, 90)
-        act(r, A("TS", 1376, W), A("TB", 1376, W), "Copy", sc, 90)
-        win, nb, i32 = "TS", 6, A("ID32", 0, 128)
-        for t in range(last + 1):
-            out = "WS" if t == hand else ("W0" if win != "W0" else "W1")
-            wn, a, pr = A(win, 0, W), 0, 300 + 10 * t
-            bare, made = r == ZTO and t in ZSEG, r == ZTO and t - 1 in ZSEG
-            for (way, n, pw, late) in (STEP0 if bare else STEPZ if made else STEP):
-                b, h = a + n, a // H
-                j1 = IND(wn, jl(t, h, 0, (a - h * H) // 16, (b - h * H) // 16))
-                j2 = IND(wn, jl(t, h, 1, (a - h * H) // 16, (b - h * H) // 16))
-                p, q, o, pi = A("P", a, b), A("Q", a, b), A(out, a, b), pr + pw
-                x2 = A("XS", t * W + a, t * W + b)
-                if way == 0:
-                    act(r, p, j1, "Copy", 1.0, pi)
-                    tt(r, o, j2, p, ADD, pi)
-                elif way == 1:
-                    if not made:
-                        ts(r, x2, xs(t, a, b), 2.0 ** (t - last), None, MUL, None, pr - 5)
-                    tt(r, q, j2, x2, ADD, pi)
-                    tt(r, o, j1, q, ADD, pi)
+    for r in range(4):
+        job[0] = ("const", r)
+        one, sel, eye, ident = A("ONE", 0, 256), A("SEL", 0, 144), A("EYE", 0, 256), A("EYE", 64, 192)
+        op(r, "dve", [("set", one, 1.0)], [], [one], ("v", 128))
+        o144 = A("ONE", 0, 144)
+        op(r, "pool", [("sel", eye, one, [[-1, 256]], "is_equal", 64, 1)], [one], [eye], ("pool", 256))
+        op(r, "pool", [("sel", sel, o144, [[-16, 9], [0, 16]], "is_ge", 0, 1)], [o144], [sel], ("pool", 144))
+        op(r, "pool", [("sel", sel, sel, [[16, 9], [0, 16]], "is_ge", 15, -1)], [sel], [sel], ("pool", 144))
+        op(r, "pool", [("sel", sel, sel, [[0, 9], [1, 16]], "is_equal", -15, 0)], [sel], [sel], ("pool", 144))
+        cp(r, A("ID", 0, 128), ident)
+        ts(r, A("NID", 0, 128), ident, -1.0, None, MUL)
+        cp(r, A("ID32", 0, 128), ident)
+        cp(r, A("O16", 0, 128), A("ONE", 0, 128))
+        for i, w in enumerate(DIAG):
+            ts(r, A("KM", 128 * i, 128 * i + 128), ident, float(w), None, MUL)
+        if not span[r]:
+            continue
+        job[0] = ("const2", r)
+        b, rot, em = CHAIN[r], A("RO32", 0, 128), A("EM", 0, 256)
+        tt(r, rot, A("EYE", 0, 128), A("EYE", 128, 256), ADD)
+        for i, m in enumerate((ident, rot)):
+            ts(r, A(("ID16", "RO16")[i], 0, 128), m, 1.0 if r in ACROSS else 2.0 ** (-1 - C["REF"]), None, MUL)
+            ts(r, A("IS", 128 * i, 128 * i + 128), m, 1.0 if r in ACROSS else 2.0 ** (-1 - C["REF"]), None, MUL)
+            cp(r, A("IB", 128 * i, 128 * i + 128), m)
+        ts(r, A("IL32", 0, 128), ident, 2.0 ** (C["REF"] - 7), None, MUL)
+        cp(r, blk(em, b), blk(eye, b))
+        op(r, "dve", [("set", blk(em, 1 - b), 0.0)], [], [blk(em, 1 - b)], ("v", 128))
+        for t in span[r]:
+            ts(r, A("ET", t * 256, t * 256 + 256), A("IB", 0, 256) if (r, t) in folded else em, xscale(r, t), None, MUL)
+
+    pending, began = {}, {}
+
+    def unit(r, t, ua, ub, slot):
+        job[0] = ("unit", t, ua)
+        n, h = ub - ua, ua // H
+        L = n // 16
+        nb = 32 * (C["NB"] * n // H // 32)
+        c0, th = lists(t, ua, ub)[0], lists(t, ua, ub)[1:]
+        prev, o, na = xs(t - 1), slot * H, n - nb
+        kb = "ps%d" % slot
+        bsub, d = A(kb, 0, nb), A(kb, 448, 448 + L)
+        k0, k1, k2 = A(kb, 0, L), A(kb, 64, 64 + 2 * L), A(kb, 192, 192 + 2 * L)
+        off = A("OF", slot * 64, slot * 64 + L)
+        li, lf = slot * 384, slot * 256
+        jk, jm, jc = [A("LI", li + 128 * i, li + 128 * i + 2 * L) for i in range(3)]
+        cf = [A("LC", slot * 192 + 64 * i, slot * 192 + 64 * i + L) for i in range(3)] + [A("LF", lf + L, lf + 2 * L)]
+        m1, m13, m2 = A("LF", lf, lf + L), A("LF", lf, lf + 2 * L), A("LF", lf + 128, lf + 128 + 2 * L)
+        took = [A("LB", slot * 256 + 64 * i, slot * 256 + 64 * i + L) for i in range(3)]
+        whole, ones, dd = A("LB", slot * 256 + 192, slot * 256 + 192 + L), A("O16", 0, L), A(kb, 384, 384 + L)
+
+        def sums(out, terms, stop=True):
+            return [("mm", out, A("ID32", 0, 128) if size(v) == 4 else A("KM", 128 * DIAG.index(w), 128 * DIAG.index(w) + 128),
+                     v, i == 0, stop and i == len(terms) - 1) for i, (w, v) in enumerate(terms)]
+
+        def keys(out, c, terms):
+            return sums(out, [(1, c)] + [(w * W, took[j]) for w, j in terms])
+
+        less = []
+        if (r, t, ua) in pack:
+            cf[0], th, less = packed(t, ua, ub)[0], packed(t, ua, ub)[1:], [(-W, ones)]
+            ts(r, off, cf[0], float(H), None, ADD)
+        else:
+            cp(r, off, c0)
+            ts(r, cf[0], c0, -float(H), None, ADD)
+        for m in range(3):
+            g = A("V", o + na, o + n)
+            act(r, g, IND(prev, A("OF", off[2] + na // 16, off[3])))
+            mm(r, [("mm", bsub, A("ID", 0, 128), g, True, False),
+                   ("mm", bsub, A("NID", 0, 128), xs(t, ua + na, ub), False, True)])
+            sp = C["ASPLIT"]
+            cuts = [32 * ((na // 32) * i // sp) for i in range(sp + 1)]
+            for i in range(sp):
+                a, b = cuts[i], cuts[i + 1]
+                tt(r, A("V", o + a, o + b), IND(prev, A("OF", off[2] + a // 16, off[2] + b // 16)), xs(t, ua + a, ua + b), SUB)
+                act(r, A("SQ", o + a, o + b), A("V", o + a, o + b), "Square")
+            act(r, A("SQ", o + na, o + n), bsub, "Square")
+            mm(r, sums(d, [(5, cf[m]), (ONEP, ones)], False) +
+               [("mm", d, A("SEL", 15 - p, 143 - p), A("SQ", o + p, o + n, 16), False, p == 15) for p in range(16)])
+            ts(r, whole, d, BIG, BIG + (LEVEL3 * W if m == 2 else 0.0), ADD, SUB)
+            tt(r, cf[m + 1], d, whole, SUB)
+            if m < 2:
+                ts(r, off, cf[m + 1], float(H), None, ADD)
+            lo, hi = [[A(kb, c + q * L, c + q * L + L) for c in (64, 192)] for q in range(2)]
+            early = keys(k0, cf[0], [(19, 0)]) + keys(lo[0], cf[1], [(17, 1)]) + keys(hi[0], cf[1], [(10.5, 0), (10.5, 1)])
+            mm(r, sums(dd, [(1, whole), (1, cf[m + 1]), (-5, cf[m]), (-0.5, ones)] + less) + (early if m == 2 else []))
+            tt(r, took[m], dd, th[m], "is_lt")
+        mm(r, keys(lo[1], cf[2], [(15, 2)]) + keys(hi[1], cf[2], [(5, 0), (5, 1), (10, 2)]))
+        tt(r, m1, k0, cf[3], MAX)
+        tt(r, m2, k1, m13, MAX)
+        tt(r, jk, k2, m2, MAX)
+        c = t * 256 + ua // 8
+        both, own = A("JL", c, c + 2 * L), t // 2
+        if h == 0:
+            ts(r, jc, jk, 2 * W - 1, None, AND)
+            ts(r, both, jc, -float(H), None, ADD)
+        else:
+            ts(r, jm, jk, W - 1, None, AND)
+            cp(r, both, jm)
+        users = [k for k in CHAIN if t in span[k]]
+        far = [k for k in users if k != r]
+        if C["FUSE"] and len(far) == 2:
+            one, two = [send(r, k, [(both, both)], False, i) for i, k in enumerate(far)]
+            one["mate"], two["cost"], two["ahead"] = two, ("none", 0), 1e3
+            two["deps"][one["id"]] = False
+        else:
+            for k in far:
+                send(r, k, [(both, both)])
+        for k in users:
+            job[0] = ("off", k, t)
+            kb, oc = CHAIN[k], t * 128 + (ua - h * H) // 16
+            moves = [(blk(A("OFF", oc, oc + 128), h), blk(both, kb))] if L == 64 else [
+                (blk(A("OFF", oc + 64 * q, oc + 64 * q + L), h), blk(A("JL", c + q * L, c + q * L + L), kb)) for q in range(2)]
+            if t in C["LATE"]:
+                pending.setdefault((k, t), []).extend(moves)
+            else:
+                for out, src in moves:
+                    cp(k, out, src)
+        job[0] = ("yj", t, ua)
+        if h:
+            ts(r, jc, jk, 2 * W - 1, None, AND)
+        jf = [A("JF", (q * 2 + t % 2) * 128 + ua // 16, (q * 2 + t % 2) * 128 + ub // 16) for q in range(2)]
+        jg = [A("JG", c + q * L, c + q * L + L) for q in range(2)]
+        for q in range(2) if own == r else [None]:
+            out = jf[q] if own == r else A("JG", c, c + 2 * L)
+            a, b = (q * L, q * L + L) if own == r else (0, 2 * L)
+            ts(r, out, A("LI", jc[2] + a, jc[2] + b), -float(H), None, ADD)
+        if own != r:
+            send(r, own, [(jf[q], jg[q]) for q in range(2)])
+
+    def whole_time(r, t, slot):
+        job[0] = ("unit", t, 0)
+        nb = C["NB2"]
+        na, o = H - nb, slot * H
+        c0, th = lists(t, 0, W)[0], lists(t, 0, W)[1:]
+        prev, bk = xs(t - 1), ["ps%d" % slot, "ps%d" % (slot + 1)]
+        d, dd, k0, k1, k2 = A(bk[0], 384, 512), A(bk[1], 384, 512), A(bk[0], 256, 384), A(bk[0], 0, 256), A(bk[1], 0, 256)
+        off = A("OF", slot * 64, slot * 64 + 128)
+        li, lf, lc, lb = slot * 384, slot * 256, slot * 192, slot * 256
+        jk, jc, jm = A("LI", li, li + 256), A("LI", li + 256, li + 512), A("LI", li + 512, li + 640)
+        cf = [A("LC", lc + 128 * i, lc + 128 * i + 128) for i in range(3)] + [A("LF", lf + 64, lf + 192)]
+        m13, m2 = A("LF", lf, lf + 256), A("LF", lf + 256, lf + 512)
+        took = [A("LB", lb + 128 * i, lb + 128 * i + 128) for i in range(3)]
+        whole = A("LB", lb + 384, lb + 512)
+
+        def part(ap, i, n=64):
+            return A(ap[1], ap[2] + n * i, ap[2] + n * i + n)
+
+        def sums(out, terms, stop=True):
+            return [("mm", out, A("ID32", 0, 128) if size(v) == 4 else A("KM", 128 * DIAG.index(w), 128 * DIAG.index(w) + 128),
+                     v, i == 0, stop and i == len(terms) - 1) for i, (w, v) in enumerate(terms)]
+
+        def keys(out, h, m, terms):
+            return sums(out, [(1, part(cf[m], h))] + [(w * W, part(took[j], h)) for w, j in terms])
+
+        less = []
+        if (r, t, 0) in pack:
+            cf[0], th, less = packed(t, 0, W)[0], packed(t, 0, W)[1:], [(-W, A("O16", 0, 128))]
+            ts(r, off, cf[0], float(H), None, ADD)
+        else:
+            cp(r, off, c0)
+            ts(r, cf[0], c0, -float(H), None, ADD)
+        for m in range(3):
+            for h in range(2):
+                u, oc, bsub = o + h * H, off[2] + 64 * h, A(bk[h], 0, nb)
+                g = A("V", u + na, u + H)
+                act(r, g, IND(prev, A("OF", oc + na // 16, oc + 64)))
+                mm(r, [("mm", bsub, A("ID", 0, 128), g, True, False),
+                       ("mm", bsub, A("NID", 0, 128), xs(t, h * H + na, h * H + H), False, True)])
+                sp = C["ASPLIT2"]
+                cuts = [32 * ((na // 32) * i // sp) for i in range(sp + 1)]
+                for a, b in zip(cuts, cuts[1:]):
+                    tt(r, A("V", u + a, u + b), IND(prev, A("OF", oc + a // 16, oc + b // 16)), xs(t, h * H + a, h * H + b), SUB)
+                    act(r, A("SQ", u + a, u + b), A("V", u + a, u + b), "Square")
+                act(r, A("SQ", u + na, u + H), bsub, "Square")
+            for h in range(2):
+                mm(r, sums(part(d, h), [(5, part(cf[m], h)), (ONEP, A("O16", 0, 64))], False) +
+                   [("mm", part(d, h), A("SEL", 15 - p, 143 - p), A("SQ", o + h * H + p, o + h * H + H, 16), False, p == 15)
+                    for p in range(16)])
+            ts(r, whole, d, BIG, BIG + (LEVEL3 * W if m == 2 else 0.0), ADD, SUB)
+            tt(r, cf[m + 1], d, whole, SUB)
+            if m < 2:
+                ts(r, off, cf[m + 1], float(H), None, ADD)
+            mm(r, sums(dd, [(1, whole), (1, cf[m + 1]), (-5, cf[m]), (-0.5, A("O16", 0, 128))] + less))
+            if m == 2:
+                mm(r, sums(k0, [(1, cf[0]), (19 * W, took[0])]) +
+                   [c for h in range(2) for c in keys(part(k1, 3 * h), h, 1, [(17, 1)]) + keys(part(k1, 1 + h), h, 1, [(10.5, 0), (10.5, 1)])])
+            tt(r, took[m], dd, th[m], "is_lt")
+        mm(r, [c for h in range(2) for c in keys(part(k2, 3 * h), h, 2, [(15, 2)]) + keys(part(k2, 1 + h), h, 2, [(5, 0), (5, 1), (10, 2)])])
+        for h in range(2):
+            tt(r, part(m13, 3 * h), part(k0, h), part(m13, 1 + h), MAX)
+        tt(r, m2, k1, m13, MAX)
+        tt(r, jk, k2, m2, MAX)
+        ts(r, jc, jk, 2 * W - 1, None, AND)
+        ts(r, jm, part(jk, 1, 128), W - 1, None, AND)
+        out = []
+        for k in [k for k in CHAIN if t in span[k]]:
+            kb, there = CHAIN[k], A("OFF", t * 128, t * 128 + 128)
+            tile = there if k == r else A("JL", t * 256 + 128 * kb, t * 256 + 128 * kb + 128)
+            ts(r, blk(tile, 0), blk(part(jc, 0, 128), kb), -float(H), None, ADD)
+            cp(r, blk(tile, 1), blk(jm, kb))
+            if k != r:
+                out.append((k, there, tile))
+        if C["FUSE"] and len(out) == 2:
+            one, two = [send(r, k, [(there, tile)], False, i) for i, (k, there, tile) in enumerate(out)]
+            one["mate"], two["cost"], two["ahead"] = two, ("none", 0), 1e3
+            one["deps"].update(two["deps"])
+            two["deps"][one["id"]] = False
+        else:
+            for k, there, tile in out:
+                send(r, k, [(there, tile)])
+        job[0] = ("yj", t, 0)
+        own, c = t // 2, (t % 2) * 128
+        jf = [A("JF", c, c + 64), A("JF", c + 256, c + 320), A("JF", c + 320, c + 384), A("JF", c + 64, c + 128)]
+        if own == r:
+            for a, b in ((0, 1), (1, 3), (3, 4)):
+                ts(r, A("JF", jf[a][2], jf[b - 1][3]), A("LI", jc[2] + 64 * a, jc[2] + 64 * b), -float(H), None, ADD)
+        else:
+            jg = A("JG", t * 256, t * 256 + 256)
+            ts(r, jg, jc, -float(H), None, ADD)
+            send(r, own, [(jf[i], part(jg, i)) for i in range(4)])
+
+    nbank = {r: [0] for r in range(4)}
+
+    def bank(r, n):
+        k = nbank[r][0]
+        while job[0][2] < C["SHARE"] and k == 2:
+            k = (k + 1) % 8
+        nbank[r][0] = (k + 1) % 8
+        return A("ps%d" % k, 0, n)
+
+    def win(t, a=0, b=W):
+        k = (t + 1) // 2 * (t % 2)
+        return A("TB", a, b) if t < 0 else A("WN", k * W + a, k * W + b)
+
+    def xmm(ps, r, t, a, b, rot, stop):
+        if (r, t) in folded:
+            return [("mm", ps, A("ET", t * 256 + 128 * rot, t * 256 + 128 * rot + 128), fx(t, a, b), True, stop)]
+        lst = []
+        for h in range(2):
+            s = 64 * ((h ^ rot) - CHAIN[r])
+            lst.append(("mm", ps, A("ET", t * 256 + 64 - s, t * 256 + 192 - s), xs(t, h * H + a, h * H + b), h == 0, stop and h == 1))
+        return lst
+
+    def step(r, t):
+        fb, last = CHAIN[r], span[r][-1]
+        wn, a, n0 = win(t - 1), 0, len(ops)
+        job[0] = ("off", r, t)
+        for out, src in pending.get((r, t), []):
+            cp(r, out, src)
+        step_pieces(r, t, fb, last, wn, a)
+        ahead[0] = 0.0
+        mine = [o for o in ops[n0:] if o["q"] == "dve"]
+        for o in mine:
+            if o["job"][0] in ("off", "prep") and t in C["LATE"] and (r, t - 1) in began:
+                o["deps"].setdefault(began[r, t - 1], False)
+        began[r, t] = [o["id"] for o in mine if o["job"][0] == "step"][C["AFTER"]]
+
+    def step_pieces(r, t, fb, last, wn, a):
+        small = t == 0
+        i2, r2 = (A("ID16", 0, 128), A("RO16", 0, 128)) if small else (A("IL32" if t == 7 else "ID32", 0, 128), A("RO32", 0, 128))
+        for (way, n, rep, *more) in C["STEPL" if t == 7 else "STEPH" if t == last else "STEP0" if t == 0 else "STEP"]:
+            b = a + n
+            ahead[0] = more[0] if more else 0.0
+            j1, j2 = [IND(wn, A("OFF", t * 128 + 64 * q + a // 16, t * 128 + 64 * q + b // 16)) for q in range(2)]
+            p, q = (A("PB", a, b), A("QH", a, b)) if small else (A("P", a, b), A("Q", a, b))
+            o = A("YS", H * fb + a, H * fb + b) if t == 7 else A("UH", a, b) if t == last else win(t, a, b)
+            other = win(t, H + a, H + b) if t < last else None
+            if way == 1:
+                job[0] = ("prep", r, t)
+                x2 = A("XS", t * 256, t * 256 + n)
+                if (r, t) in folded:
+                    ts(r, x2, fx(t, a, b), xscale(r, t), None, MUL)
+                for h in range(2) if (r, t) not in folded else []:
+                    ts(r, blk(x2, h), blk(xs(t, h * H + a, h * H + b), fb), xscale(r, t), None, MUL)
+                job[0] = ("step", r, t)
+                tt(r, q, j2, x2, ADD)
+                tt(r, o, j1, q, ADD)
+            elif way == 2:
+                job[0] = ("step", r, t)
+                ps = bank(r, n)
+                mm(r, xmm(ps, r, t, a, b, 0, True))
+                if rep == "pq":
+                    pr = bank(r, n)
+                    mm(r, xmm(pr, r, t, a, b, 1, False))
+                act(r, p, j1)
+                tt(r, q, j2, p, ADD)
+                if rep == "pq":
+                    mm(r, [("mm", pr, r2, q, False, True)])
+                    act(r, other, pr)
+                tt(r, o, q, ps, ADD)
+            else:
+                job[0] = ("step", r, t)
+                outs = [(o, 0, i2)] + ([(other, 1, r2)] if other else [])
+                banks = [bank(r, n) for _ in outs]
+                for ps, (_, rot, _m) in zip(banks, outs):
+                    mm(r, xmm(ps, r, t, a, b, rot, False))
+                act(r, p, j1)
+                if way != 4:
+                    if small:
+                        q = A("QB", a, b)
+                    (act if way == 3 else cp)(r, q, j2)
+                    for ps, (_, rot, m) in zip(banks, outs):
+                        m = A("IS", 128 * rot, 128 * rot + 128) if small else m
+                        mm(r, [("mm", ps, m, p, False, False), ("mm", ps, m, q, False, True)])
                 else:
-                    ps = A("ps%d" % nb, 0, n)
-                    nb = (nb + 1) % 8
-                    mm(r, [("mm", ps, A("ID", 0, 128) if made else sid(t), x2 if made else xs(t, a, b), True, way == 2)], pi + 1)
-                    act(r, p, j1, "Copy", 1.0, pi)
-                    if way == 3:
-                        act(r, q, j2, "Copy", 1.0, pi)
-                        mm(r, [("mm", ps, i32, p, False, False)], pi)
+                    tt(r, q, j2, p, ADD)
+                    for ps, (_, rot, m) in zip(banks, outs):
+                        mm(r, [("mm", ps, m, q, False, True)])
+                for ps, (out, rot, _m) in zip(banks, outs):
+                    (cp if (rep == "v" and rot == 0) or size(out) == 2 else act)(r, out, ps)
+            if rep == "po":
+                pr = bank(r, n)
+                mm(r, [("mm", pr, A("RO32", 0, 128), o, True, True)])
+                act(r, other, pr)
+            elif rep in ("cp", "cv"):
+                act(r, blk(other, 1), blk(o, 0))
+                (act if rep == "cp" else cp)(r, blk(other, 0), blk(o, 1))
+            a = b
+
+    def cuts(lst):
+        a = 0
+        for n in lst:
+            yield a, a + n
+            a += n
+
+    def units(r, late):
+        k, slot = C["UNITS"][r].index(None), 0
+        for i, u in enumerate(C["UNITS"][r]):
+            if u and (i > k) == late:
+                if u[2] - u[1] == W:
+                    whole_time(r, u[0], slot % NS)
+                else:
+                    unit(r, u[0], u[1], u[2], slot % NS)
+            slot += (2 if u[2] - u[1] == W else 1) if u else 0
+
+    for r in range(4):
+        units(r, False)
+    for t in range(8):
+        if t == C["HANDT"] + 1:
+            for r in range(4):
+                units(r, True)
+        for r in [k for k in CHAIN if t in span[k]]:
+            fb = CHAIN[r]
+            step(r, t)
+            if t == C["HANDT"]:
+                to = ACROSS[r]
+                job[0] = ("hand", r)
+                for a, b in cuts(C["HAND"]):
+                    send(r, to, [(A("UL", a, b), A("UH", a, b))])
+                    pr = bank(to, b - a)
+                    mm(to, [("mm", pr, A("RO16", 0, 128), A("UL", a, b), True, True)])
+                    ts(to, win(t, a, b), A("UL", a, b), 2.0 ** -8, None, MUL)
+                    act(to, win(t, H + a, H + b), pr)
+            job[0] = ("out", r, t)
+            to = t // 2
+            if t == C["HANDT"] == 1:
+                if r != to:
+                    send(r, to, [(A("UL", 0, H), A("UH", 0, H))])
+                ys = A("YS", fb * H, fb * H + H)
+                ts(to, ys, A("UH" if r == to else "UL", 0, H), 0.25, None, MUL)
+                dma(to, "sp", [(blk(A("ytau", h * H, h * H + H), fb), blk(ys, h)) for h in range(2)])
+                continue
+            for a, b in cuts(C["LAST"] if t == 7 else C["OUT3"] if t == 3 else C["OUT"]) if t % 2 else []:
+                job[0] = ("out", r, t)
+                src, ys = win(t, a, b), A("LA" if to == r and t < 7 else "YS", fb * H + a, fb * H + b)
+                if t == 7 and r != to:
+                    send(r, to, [(ys, ys)], C["WIDE7"])
+                if t in C["OUT16"] and a >= C["FROM16"]:
+                    c = (t // 4) * H
+                    src = A("U16", W + fb * H + a, W + fb * H + b)
+                    ts(r, A("U16", c + a, c + b), win(t, a, b), 2.0 ** (C["REF"] + 1), None, MUL)
+                    send(r, to, [(src, A("U16", c + a, c + b))])
+                    job[0] = ("rx", r, t)
+                    ts(to, ys, src, 2.0 ** (-t - 1), None, MUL)
+                elif t < 7:
+                    if to != r:
+                        src = A("LA", fb * H + a, fb * H + b)
+                        send(r, to, [(src, win(t, a, b))])
+                    job[0] = ("rx", r, t)
+                    if t == C["REF"]:
+                        ys = src
+                    elif fb or span[to]:
+                        act(to, ys, src, "Copy", 2.0 ** (C["REF"] - t))
                     else:
-                        tt(r, q, j2, p, ADD, pi - 1)
-                    if way == 2:
-                        tt(r, o, q, ps, ADD, pi + late)
-                    else:
-                        mm(r, [("mm", ps, i32, q, False, True)], pi)
-                        act(r, o, ps, "Copy", 1.0, pi + late)
-                a = b
-            if t == last:
-                a = 0
-                for n in STORES:
-                    dma(r, "sp", A("ytau", a, a + n), A(out, a, a + n), 950)
-                    a += n
-            if t == hand:
+                        ts(to, ys, src, 2.0 ** (C["REF"] - t), None, MUL)
                 for h in range(2):
-                    ws = A("WS", h * H, h * H + H)
-                    send(r, to, [(ws, ws)], 20)
-                    act(to, A("W0", h * H, h * H + H), ws, "Copy", 2.0 ** (last - hand), 295)
-                    dma(to, "sp", A("ytau", h * H, h * H + H), A("W0", h * H, h * H + H), 950)
-            win = out
+                    dma(to, "act" if h and t == 7 and r != to else "sp", [(blk(A("ytau", h * H + a, h * H + b), fb), blk(ys, h))])
+    job[0] = ("yjstore",)
+    for r in range(4):
+        dma(r, "sp", [(A("yj", 0, 512), A("JF", 0, 512))])
     return ops
 
 
@@ -351,16 +651,26 @@ def finish(o, start, E, pipes, seen):
     end = start + cost(o, E)
     if "pipe" not in o:
         return end, end
+    if o["cost"][0] == "none":
+        return end, pipes[o["r"], 0] + E["rlat"] * 0.5 + E["far"]
     far = o["cost"][0] == "rdma"
     if far and o["r"] not in seen:
         seen.add(o["r"])
         end += E["first"]
+    for k in {"off": (0,), "chip": (1,), "wide": (0, 1)}[o["pipe"]] if far else ():
+        if (o["r"], k) not in seen:
+            seen.add((o["r"], k))
+            end += 8 * E["eng"]
     lat = E["rlat"] if far else E["lat"]
     sets = [(o["r"], k) for k in {"loc": (0, 1), "off": (0,), "chip": (1,), "wide": (0, 1)}[o["pipe"]]]
-    go = max([end + lat * 0.5] + [pipes.get(k, 0.0) for k in sets])
+    if o["pipe"] == "off" and o["bytes"] > 100e3:
+        sets.append((o["r"] % 4, "port"))
+        end0 = max(pipes.get(k, 0.0) for k in sets)
+        for k in sets:
+            pipes[k] = end0
     for k in sets:
-        pipes[k] = go + o["bytes"] / E[o["pipe"]]
-    return end, pipes[sets[0]] + lat * 0.5
+        pipes[k] = max(end + lat * 0.5, pipes.get(k, 0.0)) + o["bytes"] / E[o["pipe"]] + o.get("rows", 8) * E["row"]
+    return end, max(pipes[k] for k in sets) + lat * 0.5 + (E["far"] if o["pipe"] == "off" else 0.0)
 
 
 def ready_at(o, ops, done, E):
@@ -368,29 +678,57 @@ def ready_at(o, ops, done, E):
                         for i, hard in o["deps"].items() if hard])
 
 
-def schedule(ops, E):
-    left = {o["id"]: len(o["deps"]) for o in ops}
-    users = {o["id"]: [] for o in ops}
+def order(ops, users, prio, E, C):
+    left = [len(o["deps"]) for o in ops]
+    ready = {}
     for o in ops:
-        for i in o["deps"]:
-            users[i].append(o["id"])
-    ready = {o["id"]: 0.0 for o in ops if not o["deps"]}
-    free, done, pipes, seen, queues = {}, {}, {}, set(), {}
-    while ready:
-        est = {i: max(t, free.get((ops[i]["r"], ops[i]["q"]), 0.0)) for i, t in ready.items()}
-        i0 = min(est, key=lambda i: (est[i], ops[i]["prio"], i))
-        key = (ops[i0]["r"], ops[i0]["q"])
-        i = min((j for j in est if (ops[j]["r"], ops[j]["q"]) == key and est[j] <= est[i0] + E["look"]),
-                key=lambda j: (ops[j]["prio"], j))
+        if not o["deps"]:
+            ready.setdefault((o["r"], o["q"]), {})[o["id"]] = 0.0
+    free, done, pipes, seen, queues, start = {}, {}, {}, set(), {}, {}
+    for _ in ops:
+        t0, key = min((max(min(lst.values()), free.get(k, 0.0)), k) for k, lst in ready.items() if lst)
+        i = min((j for j, t in ready[key].items() if t <= t0 + E["look"]),
+                key=lambda j: (prio[j] + C["LAM"] * max(0.0, ready[key][j] - t0), j))
         o = ops[i]
-        free[key], done[i] = finish(o, est[i], E, pipes, seen)
-        o["t"] = (est[i], done[i])
+        start[i] = max(ready[key].pop(i), free.get(key, 0.0))
+        free[key], done[i] = finish(o, start[i], E, pipes, seen)
         queues.setdefault(key, []).append(o)
-        del ready[i]
         for u in users[i]:
             left[u] -= 1
             if not left[u]:
-                ready[u] = max(ready_at(ops[u], ops, done, E), ops[u].get("hold", 0.0))
+                v = ops[u]
+                ready.setdefault((v["r"], v["q"]), {})[u] = max(ready_at(v, ops, done, E), C["HOLD"].get(v["job"], 0.0), v.get("hold", 0.0))
+    return queues, start, done
+
+
+def schedule(ops, E, C):
+    users = [[] for o in ops]
+    for o in ops:
+        for i in o["deps"]:
+            users[i].append(o["id"])
+    way = [0.0] * len(ops)
+    for o in reversed(ops):
+        own = cost(o, E) * C["STRETCH"] + E["wake"]
+        if "pipe" in o:
+            own += E["rlat"] + o["bytes"] / E[o["pipe"]]
+        way[o["id"]] = own + max([0.0] + [way[u] for u in users[o["id"]]])
+    prio = [-way[o["id"]] - C["BIAS"].get(o["job"], 0.0) - o["ahead"] for o in ops]
+    best = None
+    for _ in range(C["ROUNDS"] + 1):
+        queues, start, done = order(ops, users, prio, E, C)
+        end = max(done.values())
+        if best is None or end < best[0]:
+            best = (end, queues)
+        late, top = {}, {}
+        for i in sorted(start, key=lambda j: (-start[j], -j)):
+            o = ops[i]
+            key = (o["r"], o["q"])
+            fin = min([end] + [late[u] - E["wake"] for u in users[i]])
+            busy = cost(o, E)
+            late[i] = min(fin - (done[i] - start[i] if "pipe" in o else busy), top.get(key, 1e9) - busy)
+            top[key] = late[i]
+        prio = [C["MIX"] * late[i] + (1 - C["MIX"]) * (prio[i] + (end if _ == 0 else 0.0)) for i in range(len(ops))]
+    queues = best[1]
     for key, lst in queues.items():
         n = 0
         for o in lst:
@@ -402,27 +740,110 @@ def schedule(ops, E):
     return queues
 
 
+F, T_ = False, True
+CFG.update(
+    FUSE=False, OUT3=[512, 512], FROM16=0, LATE=(), AFTER=0, REF=7, MIX=0.5, HANDT=-1, HAND=[512, 512], WIDE7=True, OUT16=(), STEPH=[], LAM=80, SHARE=0, NB2=320, ASPLIT2=2,
+    STEP=[(1, 256, 'cp'), (2, 160, 'po'), (2, 256, 'cv'), (2, 352, 'pq')],
+    STEPL=[(1, 192, ''), (2, 192, 'v'), (3, 192, ''), (4, 160, 'v'), (2, 288, '')], LAST=[192, 192, 192, 160, 288],
+    UNITS={0: [(0, 0, H), (0, H, W), (1, 0, H), (2, 0, H), (4, 0, H), (6, 0, H), N_],
+           2: [(5, 0, H), (5, H, W), (1, H, W), (2, H, W), (4, H, W), (6, H, W), N_],
+           1: [(3, 0, H), (3, H, W), N_], 3: [(7, 0, H), (7, H, W), N_]},
+    BIAS=dict([(("unit",) + k, v) for k, v in {
+        (0, 0): 15, (0, H): 13, (1, 0): 7, (2, 0): 2, (4, 0): -7, (5, 0): 6, (5, H): 10, (1, H): 18, (2, H): 15, (4, H): 5,
+        (3, 0): 43, (3, H): 18, (7, 0): 27, (7, H): 27, (6, 0): -15, (6, H): -4}.items()]
+        + [((k, r), 100) for k in ("io", "const") for r in range(4)]
+        + [(("prep", r, t), 30) for r in (1, 3) for t in (0, 1, 2, 3, 6, 7)]
+        + [(("out", 1, 3), 10), (("out", 3, 3), 37), (("out", 1, 5), -29), (("out", 3, 5), 7)]),
+    HOLD={('unit', 0, 0): 3, ('unit', 1, 0): 1, ('unit', 5, 0): 4, ('unit', 5, H): 1, ('unit', 2, H): 1, ('unit', 3, 0): 2,
+          ('unit', 3, H): 6, ('unit', 7, 0): 12, ('out', 1, 3): 15, ('out', 1, 5): 1, ('unit', 6, 0): 12},
+    IO=[(0, N_, 'c', 0), (0, N_, 'x', -1, 0, W, 0), (0, N_, 'x', 0, 0, H, 0), (0, N_, 'x', 0, H, W, 0), (0, N_, 't', 0, 1, 0),
+        (0, N_, 'x', 1, H, W, 0), (0, N_, 't', 1, 3, 0), (0, N_, 'x', 1, 0, H, 1), (0, N_, 'F', -1, 0, 0, 0), (0, N_, 'F', -1, 1, 1, 0),
+        (1, N_, 'c', 0), (1, N_, 'x', 2, 0, W, 0), (1, N_, 'x', 3, 0, H, 0), (1, N_, 'x', 3, H, W, 0), (1, N_, 't', 0, 3, 0),
+        (2, N_, 'c', 0), (2, N_, 'x', 4, 0, W, 0), (2, N_, 'x', 5, 0, H, 0), (2, N_, 'x', 5, H, W, 0), (2, N_, 't', 0, 3, 0),
+        (3, N_, 'c', 0), (3, N_, 'x', 6, 0, W, 0), (3, N_, 'x', 7, 0, H, 0), (3, N_, 'x', 7, H, W, 0), (3, N_, 't', 0, 3, 0),
+        (0, 2, 'c', 1, H, W, F, 1), (0, 2, 'x', 0, 0, W, T_, 6), (0, 2, 'x', 1, H, W, T_, 1), (0, 2, 't', 1, H, W, F, 6),
+        (0, 2, 'u', 1, H, W, F, 6), (0, 2, 'x', 1, 0, H, F, 2), (0, 1, 'f', -1, 0, F, 18), (0, 3, 'f', -1, 1, F, 0),
+        (2, 3, 'x', 0, H, W, F, 13), (2, 1, 'x', 0, 0, H, F, 0), (2, 3, 'x', 1, H, W, F, 0), (0, 1, 'x', 1, 0, H, F, 24),
+        (1, 0, 'x', 2, 0, H, F, 0), (1, 2, 'x', 2, H, W, F, 3), (1, 0, 'l', 2, 0, H, F, 7), (1, 2, 'l', 2, H, W, F, 0),
+        (1, 2, 'x', 3, 0, W, F, 0), (3, 1, 'x', 6, 0, W, F, 2), (1, 3, 'x', 3, 0, W, F, 1), (3, 0, 'x', 3, 0, W, F, 0),
+        (2, 0, 'x', 4, 0, H, F, 10), (2, 0, 'l', 4, 0, H, F, 12), (0, 1, 'x', 4, 0, H, F, 21), (2, 3, 'x', 4, H, W, F, 28),
+        (3, 1, 'x', 0, H, W, F, 0), (1, 3, 'x', 0, 0, H, F, 0), (1, 3, 'x', 2, 0, W, F, 9), (3, 1, 'x', 1, H, W, F, 10),
+        (1, 3, 'x', 1, 0, H, F, 0), (3, 1, 'x', 7, 0, W, F, 14), (3, 1, 'x', 4, H, W, F, 0), (1, 3, 'x', 4, 0, H, F, 0),
+        (3, 0, 'x', 6, 0, H, F, 15), (3, 2, 'x', 6, H, W, F, 5), (3, 0, 'l', 6, 0, H, F, 0), (3, 2, 'l', 6, H, W, F, 0),
+        (2, 0, 'x', 5, 0, W, F, 15), (0, 1, 'x', 5, 0, H, F, 37), (2, 3, 'x', 5, H, W, F, 35), (1, 3, 'x', 5, 0, H, F, 12),
+        (3, 1, 'x', 5, H, W, F, 0)])
+EST.update(rissue=0.6, first=1.4, rlat=1.9, loc=320e3, chip=165e3, off=110e3, wide=280e3, look=0.6)
+ESTR = dict(EST, cyc=0.99e-3, gat=1.45, pe=0.5e-3, wake=0.11, own=0.06, rissue=0.7, first=1.5, rlat=2.0,
+            loc=300e3, chip=150e3, off=85e3, wide=250e3)
+RUN = dict(
+    CFG, REF=3, LATE=(4, 5), OUT16=(5,), FROM16=512, SHARE=1, LAM=150,
+    STEPL=[(4, 256, 'v'), (4, 288, 'v'), (4, 320, ''), (4, 160, 'v')], LAST=[256, 288, 320, 160],
+    UNITS={0: [(0, 0, H), (0, H, W), (1, 0, H), (1, H, W), (4, 0, H), N_],
+           2: [(5, 0, H), (5, H, W), (2, 0, H), (2, H, W), (4, H, W), N_],
+           1: [(3, 0, H), (3, H, W), (6, H, W), N_], 3: [(7, 0, H), (7, H, W), (6, 0, H), N_]},
+    BIAS=dict(list({('unit', 0, 0): 29, ('unit', 0, H): 17, ('unit', 1, 0): 9, ('unit', 2, 0): 16, ('unit', 4, 0): 29, ('unit', 5, 0): -5, ('unit', 5, H): 1, ('unit', 1, H): 7, ('unit', 2, H): 17, ('unit', 4, H): -9, ('unit', 3, 0): 1, ('unit', 3, H): 20, ('unit', 7, 0): 24, ('unit', 7, H): 42, ('unit', 6, 0): 35, ('unit', 6, H): 14, ('out', 1, 3): 40, ('out', 3, 3): 6, ('out', 1, 5): -6, ('out', 3, 5): -37}.items())
+              + [(("io", r), 100) for r in range(8)] + [(("const", r), 100) for r in range(4)]
+              + [(("prep", r, t), 30) for r in (1, 3) for t in (2, 3, 6, 7)] + [(("pack", 1), 60), (("pack", 3), 40)]),
+    HOLD={('unit', 2, 0): 10, ('unit', 4, 0): 21, ('unit', 5, 0): 4, ('unit', 1, H): 2, ('unit', 2, H): 18, ('unit', 3, H): 1, ('unit', 7, 0): 6, ('unit', 7, H): 8, ('unit', 6, 0): 18, ('unit', 6, H): 6, ('out', 1, 3): 6, ('out', 3, 3): 1, ('out', 1, 5): 6, ('out', 3, 5): 23},
+    IO=[(0, N_, 'c', 0), (3, N_, 'c', 0), (0, N_, 'x', -1, 0, W, 0), (0, N_, 'x', 0, 0, H, 0), (0, N_, 'x', 0, H, W, 0), (3, N_, 'x', 6, 0, W, 0), (0, N_, 't', 0, 1, 3), (0, N_, 't', 1, 3, 0), (1, N_, 'x', 3, 0, H, 0), (0, N_, 'x', 1, 0, W, 0), (0, N_, 'F', -1, 1, 1, 2), (1, N_, 'x', 2, 0, W, 0), (3, N_, 'x', 7, 0, H, 0), (1, N_, 't', 0, 3, 0), (1, N_, 'c', 0), (2, N_, 'x', 5, 0, W, 0), (1, N_, 'x', 3, H, W, 0), (3, N_, 'x', 7, H, W, 0), (2, N_, 'x', 4, 0, W, 0), (0, N_, 'F', -1, 0, 0, 0), (2, N_, 'c', 0), (0, 6, 'x', 0, H, W, T_, 6), (3, N_, 't', 0, 3, 3), (0, 4, 'x', 0, 0, H, T_, 0), (2, N_, 't', 0, 3, 0), (0, 2, 'x', 1, 0, W, T_, 0), (0, 6, 'g', 1, T_, 15), (0, 4, 'g', 0, T_, 1), (6, 3, 'x', 0, H, W, T_, 6), (2, 4, 'x', 5, 0, H, T_, 0), (2, 3, 'x', 5, H, W, T_, 0), (2, 4, 'x', 4, 0, H, T_, 7), (2, 4, 'x', 1, 0, H, T_, 15), (4, 1, 'x', 5, 0, H, T_, 0), (4, 1, 'x', 0, 0, H, F, 0), (2, 6, 'x', 1, H, W, T_, 18), (6, 3, 'f', -1, 1, F, 12), (6, 3, 'x', 1, H, W, T_, 4), (4, 1, 'f', -1, 0, T_, 0), (4, 1, 'x', 1, 0, H, T_, 13), (2, 6, 'x', 4, H, W, F, 3), (4, 1, 'x', 4, 0, H, T_, 2), (1, 3, 'x', 3, 0, W, F, 11), (1, 2, 'x', 2, 0, H, F, 2), (1, 2, 'q', 2, 0, H, F, 0), (6, 3, 'x', 4, H, W, T_, 0), (1, 2, 'q', 2, H, W, T_, 3), (1, 2, 'x', 2, H, W, F, 6), (2, 0, 'x', 4, 0, H, T_, 24), (3, 1, 'x', 6, H, W, F, 9), (3, 1, 'l', 6, H, W, T_, 3), (2, 0, 'l', 4, 0, H, T_, 0), (3, 0, 'x', 3, 0, W, T_, 19), (1, 3, 'x', 5, 0, H, F, 6), (3, 1, 'x', 5, H, W, F, 0), (3, 1, 'x', 6, 0, H, F, 19), (3, 1, 'x', 0, H, W, F, 0), (3, 1, 'x', 1, H, W, T_, 8), (1, 3, 'x', 0, 0, H, T_, 12), (1, 2, 'x', 3, 0, W, T_, 0), (3, 1, 'x', 7, 0, W, F, 15), (1, 3, 'x', 1, 0, H, F, 21), (1, 3, 'x', 2, 0, W, F, 15), (1, 3, 'x', 4, 0, H, F, 0), (3, 1, 'x', 4, H, W, F, 14)])
+EST2 = dict(EST, cyc=1.0e-3, gat=1.52, pe=0.47e-3, own=0.04, wake=0.09, fix=0.065, rissue=0.5, first=2.5, eng=0.08, off=130e3,
+            chip=190e3, wide=340e3, loc=340e3, rlat=1.9, lat=1.9, look=0.6)
+RUN2 = dict(
+    RUN, LATE=(4, 5, 6), SHARE=2,
+    STEP=[(1, 128, 'cp', -1.8), (2, 224, 'pq', -0.2), (2, 256, 'cv', -0.4), (4, 160, '', 0.0), (2, 256, 'cp', 0.4)],
+    UNITS={0: [(0, 0, H), (0, H, W), (1, 0, H), (2, 512, H), (4, 0, H), (6, 0, H), N_],
+           2: [(5, 0, H), (5, H, W), (1, H, W), (2, 1536, W), (4, H, W), (6, H, W), N_],
+           1: [(3, 0, H), (3, H, W), (2, 0, 512), N_], 3: [(7, 0, H), (7, H, W), (2, H, 1536), N_]},
+    BIAS=dict([(("io", r), 100) for r in range(8)] + [(("const", r), 100) for r in range(4)]
+              + [(("prep", r, t), 30) for r in (1, 3) for t in (0, 1, 2, 3)] + [(("pack", 1), 60), (("pack", 3), 20)]))
+RUN2.update(IO=[(2,N_,'c',0),(0,N_,'c',0),(0,N_,'x',-1,0,W,0),(1,N_,'c',0),(1,N_,'x',2,0,W,0),(0,N_,'x',0,0,H,0),(1,N_,'x',3,0,H,0),(0,N_,'x',0,H,W,0),(3,N_,'c',0),(0,N_,'x',1,0,H,0),(0,N_,'x',1,H,W,0),(0,N_,'t',0,1,0),(0,N_,'t',1,3,0),(0,N_,'F',-1,0,0,2),(0,N_,'F',-1,1,1,0),(2,N_,'x',4,0,W,0),(3,N_,'x',6,0,W,0),(3,N_,'x',7,0,H,0),(1,N_,'x',3,H,W,0),(2,N_,'x',5,0,H,0),(2,N_,'x',5,H,W,0),(0,3,'x',1,H,W,F,5),(3,N_,'t',0,3,0),(3,N_,'x',7,H,W,0),(0,2,'c',1,H,W,F,0),(0,2,'x',0,0,W,T_,0),(0,2,'x',1,H,W,F,2),(1,N_,'t',0,3,0),(0,1,'x',1,0,H,T_,3),(2,3,'x',0,H,W,F,0),(0,2,'t',1,H,W,F,1),(2,N_,'t',0,3,0),(0,2,'x',1,0,H,F,0),(0,2,'u',1,H,W,F,13),(0,1,'f',-1,0,T_,10),(1,0,'x',2,512,H,F,0),(1,3,'x',2,0,W,T_,4),(1,3,'l',2,H,1536,T_,1),(1,3,'x',1,0,H,F,7),(1,2,'x',2,1536,W,F,5),(0,3,'f',-1,1,F,0),(1,0,'q',2,512,H,T_,7),(1,2,'q',2,1536,W,F,12),(1,2,'x',3,0,W,T_,15),(3,1,'x',1,H,W,F,15),(1,3,'x',3,0,W,F,16),(2,1,'x',0,0,H,F,16),(3,0,'x',6,0,H,T_,6),(3,2,'x',6,H,W,T_,12),(1,3,'x',0,0,H,F,11),(2,0,'x',4,0,H,F,0),(3,1,'x',0,H,W,T_,12),(3,0,'q',6,0,H,F,5),(3,2,'q',6,H,W,F,13),(2,0,'l',4,0,H,F,20),(2,0,'x',3,0,W,F,12),(2,0,'x',5,0,W,F,3),(2,1,'x',4,0,H,F,14),(2,3,'x',4,H,W,T_,14),(3,1,'x',4,H,W,F,4),(1,3,'x',4,0,H,F,28),(2,3,'x',5,H,W,F,35),(3,1,'x',7,0,W,T_,34),(0,1,'x',5,0,H,T_,34),(3,1,'x',6,0,W,F,26),(3,1,'x',5,H,W,F,11),(1,3,'x',5,0,H,F,0)],HOLD={('out',1,3):6,('out',1,1):12,('unit',0,H):4,('unit',1,0):9,('unit',4,0):24,('unit',6,0):25,('unit',1,H):7,('unit',2,1536):12,('unit',4,H):15,('unit',6,H):21,('unit',2,0):15,('unit',7,H):3,('unit',2,H):1,('rx',1,1):47,('rx',3,1):47},LAM=80)
+RUN2['BIAS'].update({('out',1,3):4,('out',3,3):-19,('out',1,5):10,('out',3,5):1,('out',1,1):19,('out',3,1):10,('unit',0,0):16,('unit',0,H):13,('unit',1,0):3,('unit',2,512):3,('unit',4,0):15,('unit',6,0):-20,('unit',5,0):3,('unit',5,H):-1,('unit',1,H):15,('unit',2,1536):16,('unit',4,H):10,('unit',6,H):4,('unit',3,0):21,('unit',3,H):15,('unit',2,0):15,('unit',7,0):26,('unit',7,H):32,('unit',2,H):12,('rx',1,1):-2,('rx',1,3):6,('rx',1,5):-6,('rx',3,1):1,('rx',3,3):1,('rx',3,5):-2})
+RUN2.update(REF=7, OUT16=(), STEPL=CFG["STEPL"], LAST=CFG["LAST"])
+EST3 = dict(EST, cyc=0.95133e-3, gat=1.49933, pe=0.45867e-3, fix=0.078, wake=0.05867, own=0.054, rissue=0.83233, first=2.63333, lat=1.538,
+            rlat=1.0, loc=395e3, chip=210333.33, off=208e3, wide=378600.0, look=0.6, eng=0.10267, row=0.01267, far=1.15667)
+_h = iter([4, 0, 0, 5, 0, 1, 0, 20, 7, 13, 3, 10, 4, 6, 13, 12, 18, 4, 0, 13, 10, 16, 25, 16, 21, 13, 6, 22, 12, 25, 3, 0, 0, 3, 0, 2, 17, 35, 35, 29, 8])
+RUN3 = dict(
+    CFG, FUSE=True, REF=3, LAM=80, STEP=RUN2["STEP"], LAST=[320, 512, 192],
+    STEPL=[(5, 128, '', 0), (4, 192, '', 0), (5, 256, 'v', 0), (4, 256, '', -0.4), (4, 192, 'v', -0.7)],
+    IO=[e if e[1] is None else e[:2] + ('q' if e[2] == 'l' else e[2],) + e[3:-1] + (next(_h),) for e in CFG["IO"]],
+    BIAS={('unit',0,0):15,('unit',0,H):11,('unit',1,0):9,('unit',2,0):4,('unit',4,0):-14,('unit',5,0):4,('unit',5,H):12,('unit',1,H):23,('unit',2,H):17,('unit',4,H):4,('unit',3,0):36,('unit',3,H):-3,('unit',7,0):24,('unit',7,H):-1,('unit',6,0):-23,('unit',6,H):-3,('io',0):100,('io',1):100,('io',2):100,('io',3):100,('const',0):100,('const',1):100,('const',2):100,('const',3):100,('prep',1,0):30,('prep',1,1):30,('prep',1,2):30,('prep',1,3):30,('prep',1,6):30,('prep',1,7):30,('prep',3,0):30,('prep',3,1):30,('prep',3,2):30,('prep',3,3):30,('prep',3,6):30,('prep',3,7):30,('out',1,3):30,('out',3,3):23,('out',1,5):-26,('out',3,5):-14,('pack',1):60,('pack',3):0,('pack',2):0,('yj',2,0):7,('yj',4,0):-35,('yj',6,0):-4,('yj',1,H):2,('yj',2,H):-12,('yj',6,H):15,('rx',1,1):-7,('out',1,1):1,('rx',1,3):-27,('rx',1,5):-10,('rx',3,1):10,('out',3,1):17,('rx',3,3):-12,('rx',3,5):-2},
+    HOLD={('unit',0,0):4,('unit',5,0):3,('unit',5,H):6,('unit',2,H):8,('unit',4,H):12,('unit',3,H):6,('unit',7,0):12,('unit',7,H):4,('unit',6,0):24,('unit',6,H):2,('out',1,3):30,('out',3,3):12,('out',1,5):4,('out',3,5):2,('yj',2,0):51,('yj',4,0):42,('yj',6,0):48,('yj',1,H):50,('yj',2,H):48,('yj',6,H):50,('rx',1,1):52,('out',1,1):5,('rx',1,3):1,('rx',1,5):1,('rx',3,1):45,('out',3,1):3,('rx',3,3):17})
+EST4 = dict(EST, cyc=.94e-3, gat=1.45, pe=.45e-3, wake=.2, own=.14, off=170e3, chip=200e3, wide=360e3, loc=400e3, rlat=1.6, rissue=.45,
+            first=1.6, eng=.03, row=.004, far=.2, look=.6)
+RUN4 = dict(
+    CFG, SHARE=1, UNITS=RUN["UNITS"], LAST=[352, 320, 352],
+    STEP=[(1, 192, 'cp', -3.2), (2, 224, 'pq', 0.3), (2, 288, 'cv', 0.2), (2, 320, 'pq', 0.5)],
+    STEPL=[(1, 224, '', 0), (3, 128, '', 0), (2, 320, 'v', -0.1), (2, 352, 'v', -1.0)],
+    BIAS=dict([((k, r), 100) for k in ("io", "const") for r in range(4)] + [(("pack", 1), 60), (("pack", 3), 40)]
+              + [(("prep", r, t), 30) for r in (1, 3) for t in (0, 1, 2, 3, 6, 7)]))
+RUN4.update(IO=[(0,N_,'c',0),(0,N_,'x',-1,0,W,0),(0,N_,'x',0,0,H,0),(0,N_,'x',0,H,W,0),(0,N_,'t',0,1,0),(0,N_,'x',1,0,W,0),(1,N_,'c',0),(0,N_,'t',1,3,0),(2,N_,'c',0),(1,N_,'x',2,0,W,0),(1,N_,'x',3,0,H,0),(1,N_,'x',3,H,W,0),(3,N_,'c',0),(0,N_,'F',-1,0,0,0),(0,N_,'F',-1,1,1,0),(1,N_,'t',0,3,3),(3,N_,'x',6,0,W,0),(3,N_,'x',7,0,H,0),(2,N_,'x',5,0,W,0),(3,N_,'t',0,3,0),(3,N_,'x',7,H,W,0),(2,N_,'x',4,0,W,0),(0,2,'x',1,0,W,F,4),(2,N_,'t',0,3,0),(0,1,'f',-1,0,T_,7),(0,3,'f',-1,1,F,2),(0,1,'x',0,0,H,T_,18),(0,3,'x',0,H,W,F,0),(2,1,'x',5,0,H,T_,2),(2,3,'x',5,H,W,T_,4),(2,1,'x',4,0,H,F,14),(2,3,'x',4,H,W,T_,16),(2,1,'x',1,0,H,F,0),(2,3,'x',1,H,W,F,10),(1,2,'x',2,0,H,T_,0),(1,2,'q',2,0,H,F,0),(1,2,'q',2,H,W,F,0),(1,2,'x',2,H,W,T_,2),(2,0,'x',4,0,H,F,3),(2,0,'l',4,0,H,F,13),(1,2,'x',3,0,W,F,0),(1,3,'x',3,0,W,F,8),(3,1,'x',6,H,W,T_,0),(3,1,'l',6,H,W,T_,6),(3,0,'x',3,0,W,F,10),(3,1,'x',7,0,W,T_,0),(3,1,'x',6,0,H,F,0),(1,3,'x',5,0,H,F,0),(3,1,'x',5,H,W,F,0),(1,3,'x',4,0,H,F,0),(3,1,'x',4,H,W,F,0),(1,3,'x',2,0,W,F,14),(3,1,'x',0,H,W,F,6),(3,1,'x',1,H,W,F,7),(1,3,'x',1,0,H,F,0),(1,3,'x',0,0,H,F,2)],HOLD={('unit',0,0):2,('unit',1,0):7,('unit',4,0):8,('unit',5,H):6,('unit',1,H):6,('unit',2,H):12,('unit',4,H):20,('unit',7,H):11,('unit',6,0):5,('unit',6,H):15,('yj',4,0):45,('yj',2,0):48,('yj',2,H):50,('yj',6,H):31,('rx',1,1):47,('rx',1,5):13,('rx',3,1):49,('rx',3,3):1,('rx',3,5):8},LAM=80)
+RUN4['BIAS'].update({('unit',0,0):18,('unit',0,H):13,('unit',1,0):13,('unit',2,0):12,('unit',4,0):-6,('unit',5,0):19,('unit',5,H):6,('unit',1,H):12,('unit',2,H):8,('unit',4,H):5,('unit',3,0):17,('unit',3,H):13,('unit',7,0):42,('unit',7,H):17,('unit',6,0):12,('unit',6,H):15,('out',1,3):-10,('out',3,3):-41,('out',1,5):-74,('out',3,5):99,('yj',4,0):76,('yj',2,0):0,('yj',2,H):3,('yj',6,H):6,('rx',1,1):71,('out',1,1):50,('rx',1,3):-9,('rx',1,5):-23,('rx',3,1):-15,('out',3,1):-19,('rx',3,3):-43,('rx',3,5):-16})
+RUN5 = dict(RUN4, OUT16=(5,), FROM16=0, BIAS={k: v for k, v in RUN4["BIAS"].items() if not (k[0] == "prep" and k[2] < 2)})
+RUN5.update(IO=[(0,N_,'c',0),(0,N_,'x',-1,0,W,0),(0,N_,'x',0,0,H,0),(0,N_,'x',0,H,W,0),(0,N_,'t',0,1,0),(0,N_,'x',1,0,W,0),(1,N_,'c',0),(0,N_,'t',1,3,0),(2,N_,'c',0),(1,N_,'x',2,0,W,0),(1,N_,'x',3,0,H,0),(1,N_,'x',3,H,W,0),(3,N_,'c',0),(0,N_,'F',-1,0,0,0),(0,N_,'F',-1,1,1,0),(0,N_,'F',0,0,2,0),(0,N_,'F',0,1,3,0),(1,N_,'t',0,3,3),(3,N_,'x',6,0,W,0),(3,N_,'x',7,0,H,0),(2,N_,'x',5,0,W,0),(3,N_,'t',0,3,0),(3,N_,'x',7,H,W,0),(2,N_,'x',4,0,W,0),(0,2,'x',1,0,W,F,0),(2,N_,'t',0,3,0),(2,N_,'F',4,0,4,1),(2,N_,'F',4,1,5,0),(0,1,'f',-1,0,T_,16),(0,3,'f',-1,1,F,16),(0,1,'f',0,2,F,7),(0,3,'f',0,3,F,4),(2,1,'x',5,0,H,T_,0),(2,3,'x',5,H,W,T_,6),(2,N_,'R',1,0,0,0),(2,N_,'R',1,1,1,0),(2,1,'f',1,0,F,8),(2,3,'f',1,1,F,12),(2,1,'f',4,4,F,23),(2,3,'f',4,5,F,29),(1,2,'x',2,0,H,T_,1),(1,2,'q',2,0,H,F,0),(1,2,'q',2,H,W,F,0),(1,2,'x',2,H,W,T_,0),(2,0,'x',4,0,H,F,13),(2,0,'l',4,0,H,F,11),(1,2,'x',3,0,W,F,15),(1,3,'x',3,0,W,F,0),(3,1,'x',6,H,W,T_,6),(3,1,'l',6,H,W,T_,7),(3,0,'x',3,0,W,F,8),(3,1,'x',7,0,W,T_,1),(3,1,'x',6,0,H,F,0),(1,3,'x',5,0,H,F,12),(3,1,'x',5,H,W,F,13),(1,3,'x',2,0,W,F,0)],HOLD={('unit',0,H):4,('unit',2,0):9,('unit',4,0):15,('unit',5,H):3,('unit',1,H):3,('unit',2,H):9,('unit',4,H):2,('unit',3,0):6,('unit',7,0):3,('unit',7,H):11,('unit',6,0):4,('unit',6,H):9,('out',1,3):24,('out',3,3):6,('out',1,5):22,('yj',4,0):50,('yj',2,0):51,('yj',2,H):52,('yj',6,H):46,('rx',1,1):46,('rx',1,5):12,('rx',3,1):56,('rx',3,3):15,('rx',3,5):7},LAM=80)
+RUN5['BIAS'].update({('unit',0,0):17,('unit',0,H):13,('unit',1,0):14,('unit',2,0):18,('unit',4,0):-6,('unit',5,0):36,('unit',5,H):1,('unit',1,H):13,('unit',2,H):25,('unit',4,H):18,('unit',3,0):32,('unit',3,H):20,('unit',7,0):55,('unit',7,H):3,('unit',6,0):9,('unit',6,H):6,('out',1,3):-21,('out',3,3):-40,('out',1,5):-12,('out',3,5):17,('yj',4,0):107,('yj',2,0):-20,('yj',2,H):7,('yj',6,H):16,('rx',1,1):97,('out',1,1):17,('rx',1,3):8,('rx',1,5):-4,('rx',3,1):-23,('out',3,1):-32,('rx',3,3):-74,('rx',3,5):-6})
 PLAN = {}
 
 
 def rank_program(g, core, T, topo):
-    r = T.rank_of(core)
-    if r is None:
+    who = with_helpers(list(T.cores), topo)
+    if core not in who:
         return
+    r = who.index(core)
     if not PLAN:
-        PLAN["ops"] = build(list(T.cores), topo)
-        PLAN["queues"] = schedule(PLAN["ops"], EST)
+        PLAN["ops"] = build(list(T.cores), topo, RUN5)
+        PLAN["queues"] = schedule(PLAN["ops"], EST4, RUN5)
     ops, queues = PLAN["ops"], PLAN["queues"]
     Q = {"pe": g.tensor, "act": g.scalar, "dve": g.vector, "pool": g, "sp": g.sync}
     ALU = {"add": AluOpType.add, "subtract": AluOpType.subtract, "mult": AluOpType.mult, "max": AluOpType.max,
-           "min": AluOpType.min, "is_lt": AluOpType.is_lt, "is_ge": AluOpType.is_ge, "is_equal": AluOpType.is_equal,
+           "is_lt": AluOpType.is_lt, "is_ge": AluOpType.is_ge, "is_equal": AluOpType.is_equal,
            "bitwise_and": AluOpType.bitwise_and}
     FN = {"Copy": ActivationFunctionType.Copy, "Square": ActivationFunctionType.Square}
 
     def R(ap):
         if ap[0] == "ind":
             return R(ap[1]).indirect(R(ap[2]))
-        return T[ap[1]][:, ap[2]:ap[3]] if ap[4] == 1 else T[ap[1]][:, ap[2]:ap[3]:ap[4]]
+        rows = slice(None) if (ap[5], ap[6]) == (0, 128) else slice(ap[5], ap[6])
+        return T[ap[1]][rows, ap[2]:ap[3]] if ap[4] == 1 else T[ap[1]][rows, ap[2]:ap[3]:ap[4]]
 
     total, seen_all, sent = {}, {}, 0
     for o in ops:
@@ -463,15 +884,17 @@ def rank_program(g, core, T, topo):
                     ins = eng.affine_select(R(c[1]), R(c[2]), c[3], ALU[c[4]], 0.0, c[5], c[6])
                 elif k == "dma":
                     ins = eng.dma_start(R(c[1]), R(c[2]))
-                else:
+                elif o["cost"][0] != "none":
                     rid, pid = topo.addr(c[1])[:2]
-                    if len(c[2]) == 1:
+                    both = [o] + ([o["mate"]] if "mate" in o else [])
+                    if len(c[2]) == 1 and len(both) == 1:
                         eng.remote_dma(R(c[2][0][0]), R(c[2][0][1]), T.sem[o["sem"]], T.sem.sent, pid, rid, c[3][0])
                     else:
                         eng.remote_dma_fused(
-                            [RemoteDMATransfer(dst_ids=[DstId(rid=rid, pnc=pid)], dma_engine_mask=m, remote_sem=T.sem[o["sem"]],
-                                               src=R(p[1]), dst=R(p[0])) for p, m in zip(c[2], c[3])], local_sem=T.sem.sent)
-                    sent += o["inc"]
+                            [RemoteDMATransfer(dst_ids=[DstId(rid=topo.addr(v["calls"][0][1])[0], pnc=topo.addr(v["calls"][0][1])[1])],
+                                               dma_engine_mask=m, remote_sem=T.sem[v["sem"]], src=R(p[1]), dst=R(p[0]))
+                             for v in both for p, m in zip(v["calls"][0][2], v["calls"][0][3])], local_sem=T.sem.sent)
+                    sent += sum(v["inc"] for v in both)
             if ins is not None:
                 ins.then_inc(T.sem[o["sem"]], o["inc"])
     if sent:

from concourse.bass import DstId, RemoteDMATransfer
from concourse.mybir import AluOpType, ActivationFunctionType

W = 2048
H = 1024
NS = 6
ONEP = 1.0 + 2.0 ** -9
BIG = 1.5 * 2.0 ** 34
LEVEL3 = 13
DIAG = [5, ONEP, 1, -5, -0.5, -W] + [w * W for w in (19, 17, 15, 10.5, 5, 10)]
CHAIN = {0: 0, 2: 1, 1: 0, 3: 1}
ACROSS = {0: 1, 2: 3}

N_ = None
CFG = dict(
    NB=352, ASPLIT=2, STRETCH=1.0, HOLD={}, BIAS={}, ROUNDS=0,
    UNITS={0: [(0, 0, H), (0, H, W), (1, 0, H), (2, 0, H), (6, H, W)],
           2: [(5, 0, H), (1, H, W), (2, H, W), (4, H, W), (5, H, W)],
           1: [(3, 0, H), (3, H, W), (4, 0, H)],
           3: [(7, 0, H), (7, H, W), (6, 0, H)]},
    STEP=[(1, 256, "cp"), (2, 256, "pq"), (2, 256, "pq"), (2, 256, "pq")],
    STEP0=[(5, 256, "v"), (4, 256, "v"), (4, 256, "v"), (4, 256, "v")],
    STEPL=[(1, 256, ""), (3, 256, ""), (2, 256, ""), (2, 256, "")],
    OUT=[512, 512], LAST=[512, 256, 256],
    IO=[(0, N_, "c", 0), (0, N_, "x", -1, 0, W, 0), (0, N_, "x", 0, 0, H, 0), (0, N_, "x", 0, H, W, 0), (0, N_, "t", 0, 1, 0),
        (0, N_, "F", -1, 0, 0, 2), (0, N_, "F", -1, 1, 1, 2), (0, N_, "x", 1, 0, W, 2), (0, N_, "t", 1, 3, 2),
        (0, N_, "F", 0, 0, 2, 2), (0, N_, "F", 1, 0, 3, 2),
        (1, N_, "c", 0), (1, N_, "x", 2, 0, W, 0), (1, N_, "x", 3, 0, W, 0), (1, N_, "t", 0, 3, 0),
        (1, N_, "F", 2, 1, 2, 1), (1, N_, "F", 3, 1, 3, 0),
        (2, N_, "c", 0), (2, N_, "x", 4, 0, W, 0), (2, N_, "x", 5, 0, W, 0), (2, N_, "t", 0, 3, 0),
        (3, N_, "c", 0), (3, N_, "x", 6, 0, W, 0), (3, N_, "x", 7, 0, W, 0), (3, N_, "t", 0, 3, 0),
        (3, N_, "F", 6, 0, 6, 1), (3, N_, "F", 7, 0, 7, 0),
        (0, 2, "c", 1, H, W, False), (0, 2, "x", 0, 0, W, True), (0, 1, "f", -1, 0, False), (0, 3, "f", -1, 1, False),
        (0, 2, "x", 1, 0, W, False), (0, 2, "t", 1, H, W, False), (0, 2, "u", 1, H, W, False),
        (0, 1, "f", 0, 2, False), (0, 1, "f", 1, 3, False),
        (2, 1, "x", 4, 0, H, False), (2, 1, "l", 4, 0, H, False), (2, 3, "x", 5, 0, W, False),
        (2, N_, "R", 0, 1, 0, 0), (2, 3, "f", 0, 0, False), (2, N_, "R", 1, 1, 1, 0), (2, 3, "f", 1, 1, False),
        (2, 0, "x", 5, 0, W, False),
        (2, N_, "F", 4, 0, 2, 0), (2, N_, "F", 4, 1, 3, 0), (2, N_, "F", 5, 0, 4, 0),
        (2, 1, "f", 4, 2, False), (2, 3, "f", 4, 3, False), (2, 1, "f", 5, 4, False),
        (1, 0, "x", 2, 0, H, False), (1, 2, "x", 2, H, W, False), (1, 0, "l", 2, 0, H, False), (1, 2, "l", 2, H, W, False),
        (1, 2, "x", 3, 0, W, False), (1, 3, "f", 2, 2, False), (1, 3, "f", 3, 3, False),
        (3, 0, "x", 6, H, W, False), (3, 0, "l", 6, H, W, False), (3, 1, "f", 6, 6, False), (3, 1, "f", 7, 7, False)],
)

SCRATCH = {n: ("sbuf", [128, c], d) for n, c, d in [
    ("X", 9 * W, "bfloat16"), ("TB", W, "bfloat16"), ("FX", 8 * H, "bfloat16"), ("XS", 8 * 256, "bfloat16"),
    ("CT", 4096, "int32"), ("CQ", 4096, "float16"), ("JL", 2048, "uint16"), ("OFF", 1024, "uint16"), ("JF", 512, "float32"), ("JG", 2048, "float32"),
    ("V", NS * H, "bfloat16"), ("SQ", NS * H, "bfloat16"), ("OF", NS * 64, "uint16"), ("LI", NS * 384, "int32"),
    ("LF", NS * 256, "float32"), ("LB", NS * 256, "float16"), ("LC", NS * 192, "float16"), ("O16", 128, "float16"),
    ("KM", 128 * len(DIAG), "float16"), ("WN", 4 * W, "float32"), ("P", H, "float32"), ("Q", H, "float32"),
    ("PB", H, "bfloat16"), ("QB", H, "bfloat16"), ("QH", H, "float16"), ("UH", H, "float16"), ("UL", H, "float16"),
    ("LA", 2 * H, "float32"), ("YS", 2 * H, "float32"),
    ("ONE", 256, "bfloat16"), ("SEL", 144, "bfloat16"), ("ID", 128, "bfloat16"), ("NID", 128, "bfloat16"),
    ("EYE", 256, "bfloat16"), ("EM", 256, "bfloat16"), ("ET", 8 * 256, "bfloat16"), ("ID32", 128, "float32"),
    ("RO32", 128, "float32"), ("IL32", 128, "float32"), ("ID16", 128, "float16"), ("RO16", 128, "float16"), ("IB", 256, "bfloat16"),
    ("IS", 256, "bfloat16"), ("U16", 4 * H, "uint16")]}
for _b in range(8):
    SCRATCH["ps%d" % _b] = ("psum", [128, 512], "float32")
SEMAPHORES = ["pe", "act", "dve", "pool", "sent"] + ["d%d" % _i for _i in range(90)]
SIZE = {"bfloat16": 2, "float16": 2, "uint16": 2, "int32": 4, "float32": 4}

EST = dict(cyc=1.04e-3, gat=1.56, pe=0.52e-3, fix=0.06, wake=0.12, own=0.08, issue=0.1, rissue=0.7, first=1.5,
           lat=1.8, rlat=2.0, loc=300e3, chip=150e3, off=85e3, wide=250e3, look=0.1, eng=0.0, row=0.0, far=0.0)


def A(name, a, b, step=1, p0=0, p1=128):
    return ("ap", name, a, b, step, p0, p1)


def blk(ap, k):
    return ap[:5] + (64 * k, 64 * k + 64)


def IND(win, off):
    return ("ind", win, off)


def cost(o, E):
    k, n = o["cost"]
    return {"v": max(64, n) * E["cyc"] + E["fix"] * 0.3, "g": n * E["gat"] * E["cyc"] + E["fix"],
            "pe": n * E["pe"] + E["fix"] * 0.3, "pool": 0.17 + 2 * n * E["cyc"], "dma": E["issue"], "rdma": E["rissue"],
            "none": 0.0}[k]


def with_helpers(cores, topo):
    return list(cores) + [[c for c in topo.cores_of(k) if topo.die(c) == topo.die(k) and c not in cores][0] for k in cores]


def build(cores, topo, C):
    cores = with_helpers(cores, topo)
    ops, acc, nsem, job, chain = [], {}, {r: 0 for r in range(len(cores))}, [None], {}

    ahead = [0.0]

    def touch(o, r, ap, wr, rq):
        if ap[0] == "ind":
            touch(o, r, ap[1], wr, rq)
            touch(o, r, ap[2], False, rq)
            return
        name, a, b, p0, p1 = ap[1], ap[2], ap[3], ap[5], ap[6]
        if name not in SCRATCH:
            return
        psum = SCRATCH[name][0] == "psum"
        lst = acc.setdefault((r, name), [])
        for (p, pa, pb, q0, q1, pw, pq) in lst:
            if p is not o and ((pa < b and a < pb and q0 < p1 and p0 < q1 and (wr or pw)) or (psum and pq != rq)):
                assert not ("to" in p and p["to"] != o["r"]), "the source of a remote write is never overwritten"
                hard = not (wr and pq == rq == "pe" and not o["calls"][0][4])
                o["deps"][p["id"]] = o["deps"].get(p["id"], False) or hard
        lst.append((o, a, b, p0, p1, wr, rq))

    def op(r, q, calls, reads, writes, c, **kw):
        o = dict(id=len(ops), r=r, q=q, calls=calls, cost=c, deps={}, job=job[0], ahead=ahead[0], **kw)
        for ap in reads:
            touch(o, r, ap, False, q)
        for ap in writes:
            touch(o, kw.get("to", r), ap, True, "far" if "to" in kw else q)
        ops.append(o)
        return o

    def sem(r):
        nsem[r] += 1
        return "d%d" % (nsem[r] - 1)

    def width(ap):
        return 16 * (ap[2][3] - ap[2][2]) if ap[0] == "ind" else (ap[3] - ap[2] + ap[4] - 1) // ap[4]

    def size(ap):
        return SIZE[SCRATCH[ap[1]][2]]

    def nbytes(ap, other):
        return (ap[6] - ap[5]) * width(ap) * size(ap if ap[1] in SCRATCH else other)

    def tt(r, out, a, b, alu):
        n = width(out)
        c = ("g", n) if a[0] == "ind" else ("v", n if a[1][:2] == "ps" or b[1][:2] == "ps" else 2 * n)
        return op(r, "dve", [("tt", out, a, b, alu)], [a, b], [out], c)

    def ts(r, out, a, s1, s2, o0, o1=None):
        n = width(out) // (2 if size(a) + size(out) == 4 else 1)
        return op(r, "dve", [("ts", out, a, s1, s2, o0, o1)], [a], [out], ("v", n))

    def cp(r, out, a):
        n = width(out) // (2 if a[0] != "ind" and size(a) + size(out) == 4 else 1)
        return op(r, "dve", [("cp", out, a)], [a], [out], ("g" if a[0] == "ind" else "v", n))

    def act(r, out, a, f="Copy", scale=1.0):
        return op(r, "act", [("act", out, a, f, scale)], [a], [out], ("g" if a[0] == "ind" else "v", width(out)))

    def mm(r, lst):
        n = sum(max(64, width(m[1])) * (4 if size(m[2]) == 4 else 1) for m in lst)
        return op(r, "pe", lst, [m[2] for m in lst] + [m[3] for m in lst], [m[1] for m in lst], ("pe", n))

    def follow(o, key):
        if key in chain:
            o["deps"].setdefault(chain[key], False)
        chain[key] = o["id"]

    def dma(r, q, pairs):
        return [op(r, q, [("dma", out, src)], [src], [out], ("dma", 0), sem=sem(r), inc=16, bytes=nbytes(out, src), pipe="loc")
                for out, src in pairs]

    def send(r, to, pairs, wide=False, half=None):
        a, b = cores[r], cores[to]
        eng = topo.engines(a, b)
        same = topo.chip(a) == topo.chip(b)
        if same and not wide:
            far = [c for c in cores if topo.chip(c) != topo.chip(a)][0]
            eng = [e for e in eng if e not in topo.engines(a, far)]
        if half is not None:
            eng = eng[half * len(eng) // 2:(half + 1) * len(eng) // 2]
        per = len(eng) // len(pairs)
        masks = [sum(1 << e for e in eng[i * per:(i + 1) * per]) for i in range(len(pairs))]
        return op(r, "pool", [("send", b, pairs, masks)], [p[1] for p in pairs], [p[0] for p in pairs], ("rdma", 0),
                  to=to, sem=sem(to), inc=per * len(pairs), rows=128 // per, bytes=sum(nbytes(p[0], p[1]) for p in pairs),
                  pipe="wide" if wide and same else "chip" if same else "off")

    def xs(t, a=0, b=W):
        return A("X", (t + 1) * W + a, (t + 1) * W + b)

    def lists(t, a, b):
        c = (t // 2) * 1024 + (t % 2) * 128
        return [A("CT", c + 256 * m + a // 16, c + 256 * m + b // 16) for m in range(4)]

    def packed(t, a, b):
        c, n = t * 512 + a // 4, (b - a) // 16
        return [A("CQ", c + m * n, c + m * n + n) for m in range(4)]

    pack = {(e[1], e[3], e[4]) for e in C["IO"] if e[2] == "q"}

    def fx(k, a=0, b=H):
        return A("FX", k * H + a, k * H + b)

    folded = {(e[1], e[3]) for e in C["IO"] if e[2] == "f"}
    span = {r: range(C["HANDT"] + 1) if r in ACROSS else range(C["HANDT"] + 1, 8) for r in CHAIN}

    def xscale(r, t):
        return 2.0 ** (t + 1 if r in ACROSS else t - C["REF"] if t < 7 else 0)

    ADD, SUB, MUL, MAX, AND = "add", "subtract", "mult", "max", "bitwise_and"

    loads = {r: [] for r in range(len(cores))}
    for e in C["IO"]:
        r, to, k = e[:3]
        job[0] = ("io", r)
        if to is None:
            ct = r * 1024
            if k == "x":
                t, a, b = e[3:6]
                pairs = [(xs(t, a, b), A("xb", a, b) if t < 0 else A("x", (t % 2) * W + a, (t % 2) * W + b))]
            elif k == "c":
                pairs = [(A("CT", ct, ct + 256), A("c0", 0, 256))]
            elif k == "t":
                pairs = [(A("CT", ct + 256 + 256 * e[3], ct + 256 + 256 * e[4]), A("th", 256 * e[3], 256 * e[4]))]
            elif k == "B":
                pairs = [(blk(A("TB", H * (h ^ j), H * (h ^ j) + H), j), blk(A("tb", H * h, H * h + H), 0))
                         for h in range(2) for j in range(2)]
            else:
                t, fb, slot = e[3:6]
                src = [A("tb", h * H, h * H + H) if t < 0 else xs(t, h * H, h * H + H) if k == "R" else
                       A("x", (t % 2) * W + h * H, (t % 2) * W + h * H + H) for h in range(2)]
                pairs = [(blk(fx(slot), h), blk(src[h], fb)) for h in range(2)]
            q = "act" if k == "c" else "sp"
            made = dma(r, q, pairs)
            for o in made:
                follow(o, (r, q))
                if e[-1]:
                    o["deps"][loads[r][-e[-1]]["id"]] = True
            loads[r].append(made[-1])
            continue
        if k == "x":
            pairs = [(xs(*e[3:6]), xs(*e[3:6]))]
        elif k == "q":
            job[0] = ("pack", r)
            for m, (src, dst) in enumerate(zip(lists(*e[3:6]), packed(*e[3:6]))):
                ts(r, dst, src, -float(W if m else H), None, ADD)
            job[0] = ("io", r)
            tile = A("CQ", packed(*e[3:6])[0][2], packed(*e[3:6])[3][3])
            pairs = [(tile, tile)]
        elif k == "g":
            pairs = [(fx(e[3]), fx(e[3]))]
        elif k == "f":
            pairs = [(A("TB", 0, H) if e[3] < 0 else fx(e[3]), fx(e[4]))]
        else:
            aps = lists(*e[3:6])
            pairs = [(p, p) for p in {"l": aps, "c": aps[:1], "t": aps[1:2], "u": aps[2:]}[k]]
        o = send(r, to, pairs, e[-2])
        o["hold"] = e[-1]
        follow(o, (r, o["pipe"] == "off"))
        if k == "f" and e[3] < 0:
            job[0] = ("tb", to)
            cp(to, blk(A("TB", H, W), 1), blk(A("TB", 0, H), 0))
            cp(to, blk(A("TB", H, H + 640), 0), blk(A("TB", 0, 640), 1))
            act(to, blk(A("TB", H + 640, W), 0), blk(A("TB", 640, H), 1))

    for r in range(4):
        job[0] = ("const", r)
        one, sel, eye, ident = A("ONE", 0, 256), A("SEL", 0, 144), A("EYE", 0, 256), A("EYE", 64, 192)
        op(r, "dve", [("set", one, 1.0)], [], [one], ("v", 128))
        o144 = A("ONE", 0, 144)
        op(r, "pool", [("sel", eye, one, [[-1, 256]], "is_equal", 64, 1)], [one], [eye], ("pool", 256))
        op(r, "pool", [("sel", sel, o144, [[-16, 9], [0, 16]], "is_ge", 0, 1)], [o144], [sel], ("pool", 144))
        op(r, "pool", [("sel", sel, sel, [[16, 9], [0, 16]], "is_ge", 15, -1)], [sel], [sel], ("pool", 144))
        op(r, "pool", [("sel", sel, sel, [[0, 9], [1, 16]], "is_equal", -15, 0)], [sel], [sel], ("pool", 144))
        cp(r, A("ID", 0, 128), ident)
        ts(r, A("NID", 0, 128), ident, -1.0, None, MUL)
        cp(r, A("ID32", 0, 128), ident)
        cp(r, A("O16", 0, 128), A("ONE", 0, 128))
        for i, w in enumerate(DIAG):
            ts(r, A("KM", 128 * i, 128 * i + 128), ident, float(w), None, MUL)
        if not span[r]:
            continue
        job[0] = ("const2", r)
        b, rot, em = CHAIN[r], A("RO32", 0, 128), A("EM", 0, 256)
        tt(r, rot, A("EYE", 0, 128), A("EYE", 128, 256), ADD)
        for i, m in enumerate((ident, rot)):
            ts(r, A(("ID16", "RO16")[i], 0, 128), m, 1.0 if r in ACROSS else 2.0 ** (-1 - C["REF"]), None, MUL)
            ts(r, A("IS", 128 * i, 128 * i + 128), m, 1.0 if r in ACROSS else 2.0 ** (-1 - C["REF"]), None, MUL)
            cp(r, A("IB", 128 * i, 128 * i + 128), m)
        ts(r, A("IL32", 0, 128), ident, 2.0 ** (C["REF"] - 7), None, MUL)
        cp(r, blk(em, b), blk(eye, b))
        op(r, "dve", [("set", blk(em, 1 - b), 0.0)], [], [blk(em, 1 - b)], ("v", 128))
        for t in span[r]:
            ts(r, A("ET", t * 256, t * 256 + 256), A("IB", 0, 256) if (r, t) in folded else em, xscale(r, t), None, MUL)

    pending, began = {}, {}

    def unit(r, t, ua, ub, slot):
        job[0] = ("unit", t, ua)
        n, h = ub - ua, ua // H
        L = n // 16
        nb = 32 * (C["NB"] * n // H // 32)
        c0, th = lists(t, ua, ub)[0], lists(t, ua, ub)[1:]
        prev, o, na = xs(t - 1), slot * H, n - nb
        kb = "ps%d" % slot
        bsub, d = A(kb, 0, nb), A(kb, 448, 448 + L)
        k0, k1, k2 = A(kb, 0, L), A(kb, 64, 64 + 2 * L), A(kb, 192, 192 + 2 * L)
        off = A("OF", slot * 64, slot * 64 + L)
        li, lf = slot * 384, slot * 256
        jk, jm, jc = [A("LI", li + 128 * i, li + 128 * i + 2 * L) for i in range(3)]
        cf = [A("LC", slot * 192 + 64 * i, slot * 192 + 64 * i + L) for i in range(3)] + [A("LF", lf + L, lf + 2 * L)]
        m1, m13, m2 = A("LF", lf, lf + L), A("LF", lf, lf + 2 * L), A("LF", lf + 128, lf + 128 + 2 * L)
        took = [A("LB", slot * 256 + 64 * i, slot * 256 + 64 * i + L) for i in range(3)]
        whole, ones, dd = A("LB", slot * 256 + 192, slot * 256 + 192 + L), A("O16", 0, L), A(kb, 384, 384 + L)

        def sums(out, terms, stop=True):
            return [("mm", out, A("ID32", 0, 128) if size(v) == 4 else A("KM", 128 * DIAG.index(w), 128 * DIAG.index(w) + 128),
                     v, i == 0, stop and i == len(terms) - 1) for i, (w, v) in enumerate(terms)]

        def keys(out, c, terms):
            return sums(out, [(1, c)] + [(w * W, took[j]) for w, j in terms])

        less = []
        if (r, t, ua) in pack:
            cf[0], th, less = packed(t, ua, ub)[0], packed(t, ua, ub)[1:], [(-W, ones)]
            ts(r, off, cf[0], float(H), None, ADD)
        else:
            cp(r, off, c0)
            ts(r, cf[0], c0, -float(H), None, ADD)
        for m in range(3):
            g = A("V", o + na, o + n)
            act(r, g, IND(prev, A("OF", off[2] + na // 16, off[3])))
            mm(r, [("mm", bsub, A("ID", 0, 128), g, True, False),
                   ("mm", bsub, A("NID", 0, 128), xs(t, ua + na, ub), False, True)])
            sp = C["ASPLIT"]
            cuts = [32 * ((na // 32) * i // sp) for i in range(sp + 1)]
            for i in range(sp):
                a, b = cuts[i], cuts[i + 1]
                tt(r, A("V", o + a, o + b), IND(prev, A("OF", off[2] + a // 16, off[2] + b // 16)), xs(t, ua + a, ua + b), SUB)
                act(r, A("SQ", o + a, o + b), A("V", o + a, o + b), "Square")
            act(r, A("SQ", o + na, o + n), bsub, "Square")
            mm(r, sums(d, [(5, cf[m]), (ONEP, ones)], False) +
               [("mm", d, A("SEL", 15 - p, 143 - p), A("SQ", o + p, o + n, 16), False, p == 15) for p in range(16)])
            ts(r, whole, d, BIG, BIG + (LEVEL3 * W if m == 2 else 0.0), ADD, SUB)
            tt(r, cf[m + 1], d, whole, SUB)
            if m < 2:
                ts(r, off, cf[m + 1], float(H), None, ADD)
            lo, hi = [[A(kb, c + q * L, c + q * L + L) for c in (64, 192)] for q in range(2)]
            early = keys(k0, cf[0], [(19, 0)]) + keys(lo[0], cf[1], [(17, 1)]) + keys(hi[0], cf[1], [(10.5, 0), (10.5, 1)])
            mm(r, sums(dd, [(1, whole), (1, cf[m + 1]), (-5, cf[m]), (-0.5, ones)] + less) + (early if m == 2 else []))
            tt(r, took[m], dd, th[m], "is_lt")
        mm(r, keys(lo[1], cf[2], [(15, 2)]) + keys(hi[1], cf[2], [(5, 0), (5, 1), (10, 2)]))
        tt(r, m1, k0, cf[3], MAX)
        tt(r, m2, k1, m13, MAX)
        tt(r, jk, k2, m2, MAX)
        c = t * 256 + ua // 8
        both, own = A("JL", c, c + 2 * L), t // 2
        if h == 0:
            ts(r, jc, jk, 2 * W - 1, None, AND)
            ts(r, both, jc, -float(H), None, ADD)
        else:
            ts(r, jm, jk, W - 1, None, AND)
            cp(r, both, jm)
        users = [k for k in CHAIN if t in span[k]]
        far = [k for k in users if k != r]
        if C["FUSE"] and len(far) == 2:
            one, two = [send(r, k, [(both, both)], False, i) for i, k in enumerate(far)]
            one["mate"], two["cost"], two["ahead"] = two, ("none", 0), 1e3
            two["deps"][one["id"]] = False
        else:
            for k in far:
                send(r, k, [(both, both)])
        for k in users:
            job[0] = ("off", k, t)
            kb, oc = CHAIN[k], t * 128 + (ua - h * H) // 16
            moves = [(blk(A("OFF", oc, oc + 128), h), blk(both, kb))] if L == 64 else [
                (blk(A("OFF", oc + 64 * q, oc + 64 * q + L), h), blk(A("JL", c + q * L, c + q * L + L), kb)) for q in range(2)]
            if t in C["LATE"]:
                pending.setdefault((k, t), []).extend(moves)
            else:
                for out, src in moves:
                    cp(k, out, src)
        job[0] = ("yj", t, ua)
        if h:
            ts(r, jc, jk, 2 * W - 1, None, AND)
        jf = [A("JF", (q * 2 + t % 2) * 128 + ua // 16, (q * 2 + t % 2) * 128 + ub // 16) for q in range(2)]
        jg = [A("JG", c + q * L, c + q * L + L) for q in range(2)]
        for q in range(2) if own == r else [None]:
            out = jf[q] if own == r else A("JG", c, c + 2 * L)
            a, b = (q * L, q * L + L) if own == r else (0, 2 * L)
            ts(r, out, A("LI", jc[2] + a, jc[2] + b), -float(H), None, ADD)
        if own != r:
            send(r, own, [(jf[q], jg[q]) for q in range(2)])

    def whole_time(r, t, slot):
        job[0] = ("unit", t, 0)
        nb = C["NB2"]
        na, o = H - nb, slot * H
        c0, th = lists(t, 0, W)[0], lists(t, 0, W)[1:]
        prev, bk = xs(t - 1), ["ps%d" % slot, "ps%d" % (slot + 1)]
        d, dd, k0, k1, k2 = A(bk[0], 384, 512), A(bk[1], 384, 512), A(bk[0], 256, 384), A(bk[0], 0, 256), A(bk[1], 0, 256)
        off = A("OF", slot * 64, slot * 64 + 128)
        li, lf, lc, lb = slot * 384, slot * 256, slot * 192, slot * 256
        jk, jc, jm = A("LI", li, li + 256), A("LI", li + 256, li + 512), A("LI", li + 512, li + 640)
        cf = [A("LC", lc + 128 * i, lc + 128 * i + 128) for i in range(3)] + [A("LF", lf + 64, lf + 192)]
        m13, m2 = A("LF", lf, lf + 256), A("LF", lf + 256, lf + 512)
        took = [A("LB", lb + 128 * i, lb + 128 * i + 128) for i in range(3)]
        whole = A("LB", lb + 384, lb + 512)

        def part(ap, i, n=64):
            return A(ap[1], ap[2] + n * i, ap[2] + n * i + n)

        def sums(out, terms, stop=True):
            return [("mm", out, A("ID32", 0, 128) if size(v) == 4 else A("KM", 128 * DIAG.index(w), 128 * DIAG.index(w) + 128),
                     v, i == 0, stop and i == len(terms) - 1) for i, (w, v) in enumerate(terms)]

        def keys(out, h, m, terms):
            return sums(out, [(1, part(cf[m], h))] + [(w * W, part(took[j], h)) for w, j in terms])

        less = []
        if (r, t, 0) in pack:
            cf[0], th, less = packed(t, 0, W)[0], packed(t, 0, W)[1:], [(-W, A("O16", 0, 128))]
            ts(r, off, cf[0], float(H), None, ADD)
        else:
            cp(r, off, c0)
            ts(r, cf[0], c0, -float(H), None, ADD)
        for m in range(3):
            for h in range(2):
                u, oc, bsub = o + h * H, off[2] + 64 * h, A(bk[h], 0, nb)
                g = A("V", u + na, u + H)
                act(r, g, IND(prev, A("OF", oc + na // 16, oc + 64)))
                mm(r, [("mm", bsub, A("ID", 0, 128), g, True, False),
                       ("mm", bsub, A("NID", 0, 128), xs(t, h * H + na, h * H + H), False, True)])
                sp = C["ASPLIT2"]
                cuts = [32 * ((na // 32) * i // sp) for i in range(sp + 1)]
                for a, b in zip(cuts, cuts[1:]):
                    tt(r, A("V", u + a, u + b), IND(prev, A("OF", oc + a // 16, oc + b // 16)), xs(t, h * H + a, h * H + b), SUB)
                    act(r, A("SQ", u + a, u + b), A("V", u + a, u + b), "Square")
                act(r, A("SQ", u + na, u + H), bsub, "Square")
            for h in range(2):
                mm(r, sums(part(d, h), [(5, part(cf[m], h)), (ONEP, A("O16", 0, 64))], False) +
                   [("mm", part(d, h), A("SEL", 15 - p, 143 - p), A("SQ", o + h * H + p, o + h * H + H, 16), False, p == 15)
                    for p in range(16)])
            ts(r, whole, d, BIG, BIG + (LEVEL3 * W if m == 2 else 0.0), ADD, SUB)
            tt(r, cf[m + 1], d, whole, SUB)
            if m < 2:
                ts(r, off, cf[m + 1], float(H), None, ADD)
            mm(r, sums(dd, [(1, whole), (1, cf[m + 1]), (-5, cf[m]), (-0.5, A("O16", 0, 128))] + less))
            if m == 2:
                mm(r, sums(k0, [(1, cf[0]), (19 * W, took[0])]) +
                   [c for h in range(2) for c in keys(part(k1, 3 * h), h, 1, [(17, 1)]) + keys(part(k1, 1 + h), h, 1, [(10.5, 0), (10.5, 1)])])
            tt(r, took[m], dd, th[m], "is_lt")
        mm(r, [c for h in range(2) for c in keys(part(k2, 3 * h), h, 2, [(15, 2)]) + keys(part(k2, 1 + h), h, 2, [(5, 0), (5, 1), (10, 2)])])
        for h in range(2):
            tt(r, part(m13, 3 * h), part(k0, h), part(m13, 1 + h), MAX)
        tt(r, m2, k1, m13, MAX)
        tt(r, jk, k2, m2, MAX)
        ts(r, jc, jk, 2 * W - 1, None, AND)
        ts(r, jm, part(jk, 1, 128), W - 1, None, AND)
        out = []
        for k in [k for k in CHAIN if t in span[k]]:
            kb, there = CHAIN[k], A("OFF", t * 128, t * 128 + 128)
            tile = there if k == r else A("JL", t * 256 + 128 * kb, t * 256 + 128 * kb + 128)
            ts(r, blk(tile, 0), blk(part(jc, 0, 128), kb), -float(H), None, ADD)
            cp(r, blk(tile, 1), blk(jm, kb))
            if k != r:
                out.append((k, there, tile))
        if C["FUSE"] and len(out) == 2:
            one, two = [send(r, k, [(there, tile)], False, i) for i, (k, there, tile) in enumerate(out)]
            one["mate"], two["cost"], two["ahead"] = two, ("none", 0), 1e3
            one["deps"].update(two["deps"])
            two["deps"][one["id"]] = False
        else:
            for k, there, tile in out:
                send(r, k, [(there, tile)])
        job[0] = ("yj", t, 0)
        own, c = t // 2, (t % 2) * 128
        jf = [A("JF", c, c + 64), A("JF", c + 256, c + 320), A("JF", c + 320, c + 384), A("JF", c + 64, c + 128)]
        if own == r:
            for a, b in ((0, 1), (1, 3), (3, 4)):
                ts(r, A("JF", jf[a][2], jf[b - 1][3]), A("LI", jc[2] + 64 * a, jc[2] + 64 * b), -float(H), None, ADD)
        else:
            jg = A("JG", t * 256, t * 256 + 256)
            ts(r, jg, jc, -float(H), None, ADD)
            send(r, own, [(jf[i], part(jg, i)) for i in range(4)])

    nbank = {r: [0] for r in range(4)}

    def bank(r, n):
        k = nbank[r][0]
        while job[0][2] < C["SHARE"] and k == 2:
            k = (k + 1) % 8
        nbank[r][0] = (k + 1) % 8
        return A("ps%d" % k, 0, n)

    def win(t, a=0, b=W):
        k = (t + 1) // 2 * (t % 2)
        return A("TB", a, b) if t < 0 else A("WN", k * W + a, k * W + b)

    def xmm(ps, r, t, a, b, rot, stop):
        if (r, t) in folded:
            return [("mm", ps, A("ET", t * 256 + 128 * rot, t * 256 + 128 * rot + 128), fx(t, a, b), True, stop)]
        lst = []
        for h in range(2):
            s = 64 * ((h ^ rot) - CHAIN[r])
            lst.append(("mm", ps, A("ET", t * 256 + 64 - s, t * 256 + 192 - s), xs(t, h * H + a, h * H + b), h == 0, stop and h == 1))
        return lst

    def step(r, t):
        fb, last = CHAIN[r], span[r][-1]
        wn, a, n0 = win(t - 1), 0, len(ops)
        job[0] = ("off", r, t)
        for out, src in pending.get((r, t), []):
            cp(r, out, src)
        step_pieces(r, t, fb, last, wn, a)
        ahead[0] = 0.0
        mine = [o for o in ops[n0:] if o["q"] == "dve"]
        for o in mine:
            if o["job"][0] in ("off", "prep") and t in C["LATE"] and (r, t - 1) in began:
                o["deps"].setdefault(began[r, t - 1], False)
        began[r, t] = [o["id"] for o in mine if o["job"][0] == "step"][C["AFTER"]]

    def step_pieces(r, t, fb, last, wn, a):
        small = t == 0
        i2, r2 = (A("ID16", 0, 128), A("RO16", 0, 128)) if small else (A("IL32" if t == 7 else "ID32", 0, 128), A("RO32", 0, 128))
        for (way, n, rep, *more) in C["STEPL" if t == 7 else "STEPH" if t == last else "STEP0" if t == 0 else "STEP"]:
            b = a + n
            ahead[0] = more[0] if more else 0.0
            j1, j2 = [IND(wn, A("OFF", t * 128 + 64 * q + a // 16, t * 128 + 64 * q + b // 16)) for q in range(2)]
            p, q = (A("PB", a, b), A("QH", a, b)) if small else (A("P", a, b), A("Q", a, b))
            o = A("YS", H * fb + a, H * fb + b) if t == 7 else A("UH", a, b) if t == last else win(t, a, b)
            other = win(t, H + a, H + b) if t < last else None
            if way == 1:
                job[0] = ("prep", r, t)
                x2 = A("XS", t * 256, t * 256 + n)
                if (r, t) in folded:
                    ts(r, x2, fx(t, a, b), xscale(r, t), None, MUL)
                for h in range(2) if (r, t) not in folded else []:
                    ts(r, blk(x2, h), blk(xs(t, h * H + a, h * H + b), fb), xscale(r, t), None, MUL)
                job[0] = ("step", r, t)
                tt(r, q, j2, x2, ADD)
                tt(r, o, j1, q, ADD)
            elif way == 2:
                job[0] = ("step", r, t)
                ps = bank(r, n)
                mm(r, xmm(ps, r, t, a, b, 0, True))
                if rep == "pq":
                    pr = bank(r, n)
                    mm(r, xmm(pr, r, t, a, b, 1, False))
                act(r, p, j1)
                tt(r, q, j2, p, ADD)
                if rep == "pq":
                    mm(r, [("mm", pr, r2, q, False, True)])
                    act(r, other, pr)
                tt(r, o, q, ps, ADD)
            else:
                job[0] = ("step", r, t)
                outs = [(o, 0, i2)] + ([(other, 1, r2)] if other else [])
                banks = [bank(r, n) for _ in outs]
                for ps, (_, rot, _m) in zip(banks, outs):
                    mm(r, xmm(ps, r, t, a, b, rot, False))
                act(r, p, j1)
                if way != 4:
                    if small:
                        q = A("QB", a, b)
                    (act if way == 3 else cp)(r, q, j2)
                    for ps, (_, rot, m) in zip(banks, outs):
                        m = A("IS", 128 * rot, 128 * rot + 128) if small else m
                        mm(r, [("mm", ps, m, p, False, False), ("mm", ps, m, q, False, True)])
                else:
                    tt(r, q, j2, p, ADD)
                    for ps, (_, rot, m) in zip(banks, outs):
                        mm(r, [("mm", ps, m, q, False, True)])
                for ps, (out, rot, _m) in zip(banks, outs):
                    (cp if (rep == "v" and rot == 0) or size(out) == 2 else act)(r, out, ps)
            if rep == "po":
                pr = bank(r, n)
                mm(r, [("mm", pr, A("RO32", 0, 128), o, True, True)])
                act(r, other, pr)
            elif rep in ("cp", "cv"):
                act(r, blk(other, 1), blk(o, 0))
                (act if rep == "cp" else cp)(r, blk(other, 0), blk(o, 1))
            a = b

    def cuts(lst):
        a = 0
        for n in lst:
            yield a, a + n
            a += n

    def units(r, late):
        k, slot = C["UNITS"][r].index(None), 0
        for i, u in enumerate(C["UNITS"][r]):
            if u and (i > k) == late:
                if u[2] - u[1] == W:
                    whole_time(r, u[0], slot % NS)
                else:
                    unit(r, u[0], u[1], u[2], slot % NS)
            slot += (2 if u[2] - u[1] == W else 1) if u else 0

    for r in range(4):
        units(r, False)
    for t in range(8):
        if t == C["HANDT"] + 1:
            for r in range(4):
                units(r, True)
        for r in [k for k in CHAIN if t in span[k]]:
            fb = CHAIN[r]
            step(r, t)
            if t == C["HANDT"]:
                to = ACROSS[r]
                job[0] = ("hand", r)
                for a, b in cuts(C["HAND"]):
                    send(r, to, [(A("UL", a, b), A("UH", a, b))])
                    pr = bank(to, b - a)
                    mm(to, [("mm", pr, A("RO16", 0, 128), A("UL", a, b), True, True)])
                    ts(to, win(t, a, b), A("UL", a, b), 2.0 ** -8, None, MUL)
                    act(to, win(t, H + a, H + b), pr)
            job[0] = ("out", r, t)
            to = t // 2
            if t == C["HANDT"] == 1:
                if r != to:
                    send(r, to, [(A("UL", 0, H), A("UH", 0, H))])
                ys = A("YS", fb * H, fb * H + H)
                ts(to, ys, A("UH" if r == to else "UL", 0, H), 0.25, None, MUL)
                dma(to, "sp", [(blk(A("ytau", h * H, h * H + H), fb), blk(ys, h)) for h in range(2)])
                continue
            for a, b in cuts(C["LAST"] if t == 7 else C["OUT3"] if t == 3 else C["OUT"]) if t % 2 else []:
                job[0] = ("out", r, t)
                src, ys = win(t, a, b), A("LA" if to == r and t < 7 else "YS", fb * H + a, fb * H + b)
                if t == 7 and r != to:
                    send(r, to, [(ys, ys)], C["WIDE7"])
                if t in C["OUT16"] and a >= C["FROM16"]:
                    c = (t // 4) * H
                    src = A("U16", W + fb * H + a, W + fb * H + b)
                    ts(r, A("U16", c + a, c + b), win(t, a, b), 2.0 ** (C["REF"] + 1), None, MUL)
                    send(r, to, [(src, A("U16", c + a, c + b))])
                    job[0] = ("rx", r, t)
                    ts(to, ys, src, 2.0 ** (-t - 1), None, MUL)
                elif t < 7:
                    if to != r:
                        src = A("LA", fb * H + a, fb * H + b)
                        send(r, to, [(src, win(t, a, b))])
                    job[0] = ("rx", r, t)
                    if t == C["REF"]:
                        ys = src
                    elif fb or span[to]:
                        act(to, ys, src, "Copy", 2.0 ** (C["REF"] - t))
                    else:
                        ts(to, ys, src, 2.0 ** (C["REF"] - t), None, MUL)
                for h in range(2):
                    dma(to, "act" if h and t == 7 and r != to else "sp", [(blk(A("ytau", h * H + a, h * H + b), fb), blk(ys, h))])
    job[0] = ("yjstore",)
    for r in range(4):
        dma(r, "sp", [(A("yj", 0, 512), A("JF", 0, 512))])
    return ops


def finish(o, start, E, pipes, seen):
    end = start + cost(o, E)
    if "pipe" not in o:
        return end, end
    if o["cost"][0] == "none":
        return end, pipes[o["r"], 0] + E["rlat"] * 0.5 + E["far"]
    far = o["cost"][0] == "rdma"
    if far and o["r"] not in seen:
        seen.add(o["r"])
        end += E["first"]
    for k in {"off": (0,), "chip": (1,), "wide": (0, 1)}[o["pipe"]] if far else ():
        if (o["r"], k) not in seen:
            seen.add((o["r"], k))
            end += 8 * E["eng"]
    lat = E["rlat"] if far else E["lat"]
    sets = [(o["r"], k) for k in {"loc": (0, 1), "off": (0,), "chip": (1,), "wide": (0, 1)}[o["pipe"]]]
    if o["pipe"] == "off" and o["bytes"] > 100e3:
        sets.append((o["r"] % 4, "port"))
        end0 = max(pipes.get(k, 0.0) for k in sets)
        for k in sets:
            pipes[k] = end0
    for k in sets:
        pipes[k] = max(end + lat * 0.5, pipes.get(k, 0.0)) + o["bytes"] / E[o["pipe"]] + o.get("rows", 8) * E["row"]
    return end, max(pipes[k] for k in sets) + lat * 0.5 + (E["far"] if o["pipe"] == "off" else 0.0)


def ready_at(o, ops, done, E):
    return max([0.0] + [done[i] + (E["own"] if (ops[i]["r"], ops[i]["q"]) == (o["r"], o["q"]) else E["wake"])
                        for i, hard in o["deps"].items() if hard])


def order(ops, users, prio, E, C):
    left = [len(o["deps"]) for o in ops]
    ready = {}
    for o in ops:
        if not o["deps"]:
            ready.setdefault((o["r"], o["q"]), {})[o["id"]] = 0.0
    free, done, pipes, seen, queues, start = {}, {}, {}, set(), {}, {}
    for _ in ops:
        t0, key = min((max(min(lst.values()), free.get(k, 0.0)), k) for k, lst in ready.items() if lst)
        i = min((j for j, t in ready[key].items() if t <= t0 + E["look"]),
                key=lambda j: (prio[j] + C["LAM"] * max(0.0, ready[key][j] - t0), j))
        o = ops[i]
        start[i] = max(ready[key].pop(i), free.get(key, 0.0))
        free[key], done[i] = finish(o, start[i], E, pipes, seen)
        queues.setdefault(key, []).append(o)
        for u in users[i]:
            left[u] -= 1
            if not left[u]:
                v = ops[u]
                ready.setdefault((v["r"], v["q"]), {})[u] = max(ready_at(v, ops, done, E), C["HOLD"].get(v["job"], 0.0), v.get("hold", 0.0))
    return queues, start, done


def schedule(ops, E, C):
    users = [[] for o in ops]
    for o in ops:
        for i in o["deps"]:
            users[i].append(o["id"])
    way = [0.0] * len(ops)
    for o in reversed(ops):
        own = cost(o, E) * C["STRETCH"] + E["wake"]
        if "pipe" in o:
            own += E["rlat"] + o["bytes"] / E[o["pipe"]]
        way[o["id"]] = own + max([0.0] + [way[u] for u in users[o["id"]]])
    prio = [-way[o["id"]] - C["BIAS"].get(o["job"], 0.0) - o["ahead"] for o in ops]
    best = None
    for _ in range(C["ROUNDS"] + 1):
        queues, start, done = order(ops, users, prio, E, C)
        end = max(done.values())
        if best is None or end < best[0]:
            best = (end, queues)
        late, top = {}, {}
        for i in sorted(start, key=lambda j: (-start[j], -j)):
            o = ops[i]
            key = (o["r"], o["q"])
            fin = min([end] + [late[u] - E["wake"] for u in users[i]])
            busy = cost(o, E)
            late[i] = min(fin - (done[i] - start[i] if "pipe" in o else busy), top.get(key, 1e9) - busy)
            top[key] = late[i]
        prio = [C["MIX"] * late[i] + (1 - C["MIX"]) * (prio[i] + (end if _ == 0 else 0.0)) for i in range(len(ops))]
    queues = best[1]
    for key, lst in queues.items():
        n = 0
        for o in lst:
            if "sem" not in o:
                n += 1
                o["sem"], o["inc"], o["val"] = key[1], 1, n
            else:
                o["val"] = o["inc"]
    return queues


F, T_ = False, True
CFG.update(
    FUSE=False, OUT3=[512, 512], FROM16=0, LATE=(), AFTER=0, REF=7, MIX=0.5, HANDT=-1, HAND=[512, 512], WIDE7=True, OUT16=(), STEPH=[], LAM=80, SHARE=0, NB2=320, ASPLIT2=2,
    STEP=[(1, 256, 'cp'), (2, 160, 'po'), (2, 256, 'cv'), (2, 352, 'pq')],
    STEPL=[(1, 192, ''), (2, 192, 'v'), (3, 192, ''), (4, 160, 'v'), (2, 288, '')], LAST=[192, 192, 192, 160, 288],
    UNITS={0: [(0, 0, H), (0, H, W), (1, 0, H), (2, 0, H), (4, 0, H), (6, 0, H), N_],
           2: [(5, 0, H), (5, H, W), (1, H, W), (2, H, W), (4, H, W), (6, H, W), N_],
           1: [(3, 0, H), (3, H, W), N_], 3: [(7, 0, H), (7, H, W), N_]},
    BIAS=dict([(("unit",) + k, v) for k, v in {
        (0, 0): 15, (0, H): 13, (1, 0): 7, (2, 0): 2, (4, 0): -7, (5, 0): 6, (5, H): 10, (1, H): 18, (2, H): 15, (4, H): 5,
        (3, 0): 43, (3, H): 18, (7, 0): 27, (7, H): 27, (6, 0): -15, (6, H): -4}.items()]
        + [((k, r), 100) for k in ("io", "const") for r in range(4)]
        + [(("prep", r, t), 30) for r in (1, 3) for t in (0, 1, 2, 3, 6, 7)]
        + [(("out", 1, 3), 10), (("out", 3, 3), 37), (("out", 1, 5), -29), (("out", 3, 5), 7)]),
    HOLD={('unit', 0, 0): 3, ('unit', 1, 0): 1, ('unit', 5, 0): 4, ('unit', 5, H): 1, ('unit', 2, H): 1, ('unit', 3, 0): 2,
          ('unit', 3, H): 6, ('unit', 7, 0): 12, ('out', 1, 3): 15, ('out', 1, 5): 1, ('unit', 6, 0): 12},
    IO=[(0, N_, 'c', 0), (0, N_, 'x', -1, 0, W, 0), (0, N_, 'x', 0, 0, H, 0), (0, N_, 'x', 0, H, W, 0), (0, N_, 't', 0, 1, 0),
        (0, N_, 'x', 1, H, W, 0), (0, N_, 't', 1, 3, 0), (0, N_, 'x', 1, 0, H, 1), (0, N_, 'F', -1, 0, 0, 0), (0, N_, 'F', -1, 1, 1, 0),
        (1, N_, 'c', 0), (1, N_, 'x', 2, 0, W, 0), (1, N_, 'x', 3, 0, H, 0), (1, N_, 'x', 3, H, W, 0), (1, N_, 't', 0, 3, 0),
        (2, N_, 'c', 0), (2, N_, 'x', 4, 0, W, 0), (2, N_, 'x', 5, 0, H, 0), (2, N_, 'x', 5, H, W, 0), (2, N_, 't', 0, 3, 0),
        (3, N_, 'c', 0), (3, N_, 'x', 6, 0, W, 0), (3, N_, 'x', 7, 0, H, 0), (3, N_, 'x', 7, H, W, 0), (3, N_, 't', 0, 3, 0),
        (0, 2, 'c', 1, H, W, F, 1), (0, 2, 'x', 0, 0, W, T_, 6), (0, 2, 'x', 1, H, W, T_, 1), (0, 2, 't', 1, H, W, F, 6),
        (0, 2, 'u', 1, H, W, F, 6), (0, 2, 'x', 1, 0, H, F, 2), (0, 1, 'f', -1, 0, F, 18), (0, 3, 'f', -1, 1, F, 0),
        (2, 3, 'x', 0, H, W, F, 13), (2, 1, 'x', 0, 0, H, F, 0), (2, 3, 'x', 1, H, W, F, 0), (0, 1, 'x', 1, 0, H, F, 24),
        (1, 0, 'x', 2, 0, H, F, 0), (1, 2, 'x', 2, H, W, F, 3), (1, 0, 'l', 2, 0, H, F, 7), (1, 2, 'l', 2, H, W, F, 0),
        (1, 2, 'x', 3, 0, W, F, 0), (3, 1, 'x', 6, 0, W, F, 2), (1, 3, 'x', 3, 0, W, F, 1), (3, 0, 'x', 3, 0, W, F, 0),
        (2, 0, 'x', 4, 0, H, F, 10), (2, 0, 'l', 4, 0, H, F, 12), (0, 1, 'x', 4, 0, H, F, 21), (2, 3, 'x', 4, H, W, F, 28),
        (3, 1, 'x', 0, H, W, F, 0), (1, 3, 'x', 0, 0, H, F, 0), (1, 3, 'x', 2, 0, W, F, 9), (3, 1, 'x', 1, H, W, F, 10),
        (1, 3, 'x', 1, 0, H, F, 0), (3, 1, 'x', 7, 0, W, F, 14), (3, 1, 'x', 4, H, W, F, 0), (1, 3, 'x', 4, 0, H, F, 0),
        (3, 0, 'x', 6, 0, H, F, 15), (3, 2, 'x', 6, H, W, F, 5), (3, 0, 'l', 6, 0, H, F, 0), (3, 2, 'l', 6, H, W, F, 0),
        (2, 0, 'x', 5, 0, W, F, 15), (0, 1, 'x', 5, 0, H, F, 37), (2, 3, 'x', 5, H, W, F, 35), (1, 3, 'x', 5, 0, H, F, 12),
        (3, 1, 'x', 5, H, W, F, 0)])
EST.update(rissue=0.6, first=1.4, rlat=1.9, loc=320e3, chip=165e3, off=110e3, wide=280e3, look=0.6)
ESTR = dict(EST, cyc=0.99e-3, gat=1.45, pe=0.5e-3, wake=0.11, own=0.06, rissue=0.7, first=1.5, rlat=2.0,
            loc=300e3, chip=150e3, off=85e3, wide=250e3)
RUN = dict(
    CFG, REF=3, LATE=(4, 5), OUT16=(5,), FROM16=512, SHARE=1, LAM=150,
    STEPL=[(4, 256, 'v'), (4, 288, 'v'), (4, 320, ''), (4, 160, 'v')], LAST=[256, 288, 320, 160],
    UNITS={0: [(0, 0, H), (0, H, W), (1, 0, H), (1, H, W), (4, 0, H), N_],
           2: [(5, 0, H), (5, H, W), (2, 0, H), (2, H, W), (4, H, W), N_],
           1: [(3, 0, H), (3, H, W), (6, H, W), N_], 3: [(7, 0, H), (7, H, W), (6, 0, H), N_]},
    BIAS=dict(list({('unit', 0, 0): 29, ('unit', 0, H): 17, ('unit', 1, 0): 9, ('unit', 2, 0): 16, ('unit', 4, 0): 29, ('unit', 5, 0): -5, ('unit', 5, H): 1, ('unit', 1, H): 7, ('unit', 2, H): 17, ('unit', 4, H): -9, ('unit', 3, 0): 1, ('unit', 3, H): 20, ('unit', 7, 0): 24, ('unit', 7, H): 42, ('unit', 6, 0): 35, ('unit', 6, H): 14, ('out', 1, 3): 40, ('out', 3, 3): 6, ('out', 1, 5): -6, ('out', 3, 5): -37}.items())
              + [(("io", r), 100) for r in range(8)] + [(("const", r), 100) for r in range(4)]
              + [(("prep", r, t), 30) for r in (1, 3) for t in (2, 3, 6, 7)] + [(("pack", 1), 60), (("pack", 3), 40)]),
    HOLD={('unit', 2, 0): 10, ('unit', 4, 0): 21, ('unit', 5, 0): 4, ('unit', 1, H): 2, ('unit', 2, H): 18, ('unit', 3, H): 1, ('unit', 7, 0): 6, ('unit', 7, H): 8, ('unit', 6, 0): 18, ('unit', 6, H): 6, ('out', 1, 3): 6, ('out', 3, 3): 1, ('out', 1, 5): 6, ('out', 3, 5): 23},
    IO=[(0, N_, 'c', 0), (3, N_, 'c', 0), (0, N_, 'x', -1, 0, W, 0), (0, N_, 'x', 0, 0, H, 0), (0, N_, 'x', 0, H, W, 0), (3, N_, 'x', 6, 0, W, 0), (0, N_, 't', 0, 1, 3), (0, N_, 't', 1, 3, 0), (1, N_, 'x', 3, 0, H, 0), (0, N_, 'x', 1, 0, W, 0), (0, N_, 'F', -1, 1, 1, 2), (1, N_, 'x', 2, 0, W, 0), (3, N_, 'x', 7, 0, H, 0), (1, N_, 't', 0, 3, 0), (1, N_, 'c', 0), (2, N_, 'x', 5, 0, W, 0), (1, N_, 'x', 3, H, W, 0), (3, N_, 'x', 7, H, W, 0), (2, N_, 'x', 4, 0, W, 0), (0, N_, 'F', -1, 0, 0, 0), (2, N_, 'c', 0), (0, 6, 'x', 0, H, W, T_, 6), (3, N_, 't', 0, 3, 3), (0, 4, 'x', 0, 0, H, T_, 0), (2, N_, 't', 0, 3, 0), (0, 2, 'x', 1, 0, W, T_, 0), (0, 6, 'g', 1, T_, 15), (0, 4, 'g', 0, T_, 1), (6, 3, 'x', 0, H, W, T_, 6), (2, 4, 'x', 5, 0, H, T_, 0), (2, 3, 'x', 5, H, W, T_, 0), (2, 4, 'x', 4, 0, H, T_, 7), (2, 4, 'x', 1, 0, H, T_, 15), (4, 1, 'x', 5, 0, H, T_, 0), (4, 1, 'x', 0, 0, H, F, 0), (2, 6, 'x', 1, H, W, T_, 18), (6, 3, 'f', -1, 1, F, 12), (6, 3, 'x', 1, H, W, T_, 4), (4, 1, 'f', -1, 0, T_, 0), (4, 1, 'x', 1, 0, H, T_, 13), (2, 6, 'x', 4, H, W, F, 3), (4, 1, 'x', 4, 0, H, T_, 2), (1, 3, 'x', 3, 0, W, F, 11), (1, 2, 'x', 2, 0, H, F, 2), (1, 2, 'q', 2, 0, H, F, 0), (6, 3, 'x', 4, H, W, T_, 0), (1, 2, 'q', 2, H, W, T_, 3), (1, 2, 'x', 2, H, W, F, 6), (2, 0, 'x', 4, 0, H, T_, 24), (3, 1, 'x', 6, H, W, F, 9), (3, 1, 'l', 6, H, W, T_, 3), (2, 0, 'l', 4, 0, H, T_, 0), (3, 0, 'x', 3, 0, W, T_, 19), (1, 3, 'x', 5, 0, H, F, 6), (3, 1, 'x', 5, H, W, F, 0), (3, 1, 'x', 6, 0, H, F, 19), (3, 1, 'x', 0, H, W, F, 0), (3, 1, 'x', 1, H, W, T_, 8), (1, 3, 'x', 0, 0, H, T_, 12), (1, 2, 'x', 3, 0, W, T_, 0), (3, 1, 'x', 7, 0, W, F, 15), (1, 3, 'x', 1, 0, H, F, 21), (1, 3, 'x', 2, 0, W, F, 15), (1, 3, 'x', 4, 0, H, F, 0), (3, 1, 'x', 4, H, W, F, 14)])
EST2 = dict(EST, cyc=1.0e-3, gat=1.52, pe=0.47e-3, own=0.04, wake=0.09, fix=0.065, rissue=0.5, first=2.5, eng=0.08, off=130e3,
            chip=190e3, wide=340e3, loc=340e3, rlat=1.9, lat=1.9, look=0.6)
RUN2 = dict(
    RUN, LATE=(4, 5, 6), SHARE=2,
    STEP=[(1, 128, 'cp', -1.8), (2, 224, 'pq', -0.2), (2, 256, 'cv', -0.4), (4, 160, '', 0.0), (2, 256, 'cp', 0.4)],
    UNITS={0: [(0, 0, H), (0, H, W), (1, 0, H), (2, 512, H), (4, 0, H), (6, 0, H), N_],
           2: [(5, 0, H), (5, H, W), (1, H, W), (2, 1536, W), (4, H, W), (6, H, W), N_],
           1: [(3, 0, H), (3, H, W), (2, 0, 512), N_], 3: [(7, 0, H), (7, H, W), (2, H, 1536), N_]},
    BIAS=dict([(("io", r), 100) for r in range(8)] + [(("const", r), 100) for r in range(4)]
              + [(("prep", r, t), 30) for r in (1, 3) for t in (0, 1, 2, 3)] + [(("pack", 1), 60), (("pack", 3), 20)]))
RUN2.update(IO=[(2,N_,'c',0),(0,N_,'c',0),(0,N_,'x',-1,0,W,0),(1,N_,'c',0),(1,N_,'x',2,0,W,0),(0,N_,'x',0,0,H,0),(1,N_,'x',3,0,H,0),(0,N_,'x',0,H,W,0),(3,N_,'c',0),(0,N_,'x',1,0,H,0),(0,N_,'x',1,H,W,0),(0,N_,'t',0,1,0),(0,N_,'t',1,3,0),(0,N_,'F',-1,0,0,2),(0,N_,'F',-1,1,1,0),(2,N_,'x',4,0,W,0),(3,N_,'x',6,0,W,0),(3,N_,'x',7,0,H,0),(1,N_,'x',3,H,W,0),(2,N_,'x',5,0,H,0),(2,N_,'x',5,H,W,0),(0,3,'x',1,H,W,F,5),(3,N_,'t',0,3,0),(3,N_,'x',7,H,W,0),(0,2,'c',1,H,W,F,0),(0,2,'x',0,0,W,T_,0),(0,2,'x',1,H,W,F,2),(1,N_,'t',0,3,0),(0,1,'x',1,0,H,T_,3),(2,3,'x',0,H,W,F,0),(0,2,'t',1,H,W,F,1),(2,N_,'t',0,3,0),(0,2,'x',1,0,H,F,0),(0,2,'u',1,H,W,F,13),(0,1,'f',-1,0,T_,10),(1,0,'x',2,512,H,F,0),(1,3,'x',2,0,W,T_,4),(1,3,'l',2,H,1536,T_,1),(1,3,'x',1,0,H,F,7),(1,2,'x',2,1536,W,F,5),(0,3,'f',-1,1,F,0),(1,0,'q',2,512,H,T_,7),(1,2,'q',2,1536,W,F,12),(1,2,'x',3,0,W,T_,15),(3,1,'x',1,H,W,F,15),(1,3,'x',3,0,W,F,16),(2,1,'x',0,0,H,F,16),(3,0,'x',6,0,H,T_,6),(3,2,'x',6,H,W,T_,12),(1,3,'x',0,0,H,F,11),(2,0,'x',4,0,H,F,0),(3,1,'x',0,H,W,T_,12),(3,0,'q',6,0,H,F,5),(3,2,'q',6,H,W,F,13),(2,0,'l',4,0,H,F,20),(2,0,'x',3,0,W,F,12),(2,0,'x',5,0,W,F,3),(2,1,'x',4,0,H,F,14),(2,3,'x',4,H,W,T_,14),(3,1,'x',4,H,W,F,4),(1,3,'x',4,0,H,F,28),(2,3,'x',5,H,W,F,35),(3,1,'x',7,0,W,T_,34),(0,1,'x',5,0,H,T_,34),(3,1,'x',6,0,W,F,26),(3,1,'x',5,H,W,F,11),(1,3,'x',5,0,H,F,0)],HOLD={('out',1,3):6,('out',1,1):12,('unit',0,H):4,('unit',1,0):9,('unit',4,0):24,('unit',6,0):25,('unit',1,H):7,('unit',2,1536):12,('unit',4,H):15,('unit',6,H):21,('unit',2,0):15,('unit',7,H):3,('unit',2,H):1,('rx',1,1):47,('rx',3,1):47},LAM=80)
RUN2['BIAS'].update({('out',1,3):4,('out',3,3):-19,('out',1,5):10,('out',3,5):1,('out',1,1):19,('out',3,1):10,('unit',0,0):16,('unit',0,H):13,('unit',1,0):3,('unit',2,512):3,('unit',4,0):15,('unit',6,0):-20,('unit',5,0):3,('unit',5,H):-1,('unit',1,H):15,('unit',2,1536):16,('unit',4,H):10,('unit',6,H):4,('unit',3,0):21,('unit',3,H):15,('unit',2,0):15,('unit',7,0):26,('unit',7,H):32,('unit',2,H):12,('rx',1,1):-2,('rx',1,3):6,('rx',1,5):-6,('rx',3,1):1,('rx',3,3):1,('rx',3,5):-2})
RUN2.update(REF=7, OUT16=(), STEPL=CFG["STEPL"], LAST=CFG["LAST"])
EST3 = dict(EST, cyc=0.95133e-3, gat=1.49933, pe=0.45867e-3, fix=0.078, wake=0.05867, own=0.054, rissue=0.83233, first=2.63333, lat=1.538,
            rlat=1.0, loc=395e3, chip=210333.33, off=208e3, wide=378600.0, look=0.6, eng=0.10267, row=0.01267, far=1.15667)
_h = iter([4, 0, 0, 5, 0, 1, 0, 20, 7, 13, 3, 10, 4, 6, 13, 12, 18, 4, 0, 13, 10, 16, 25, 16, 21, 13, 6, 22, 12, 25, 3, 0, 0, 3, 0, 2, 17, 35, 35, 29, 8])
RUN3 = dict(
    CFG, FUSE=True, REF=3, LAM=80, STEP=RUN2["STEP"], LAST=[320, 512, 192],
    STEPL=[(5, 128, '', 0), (4, 192, '', 0), (5, 256, 'v', 0), (4, 256, '', -0.4), (4, 192, 'v', -0.7)],
    IO=[e if e[1] is None else e[:2] + ('q' if e[2] == 'l' else e[2],) + e[3:-1] + (next(_h),) for e in CFG["IO"]],
    BIAS={('unit',0,0):15,('unit',0,H):11,('unit',1,0):9,('unit',2,0):4,('unit',4,0):-14,('unit',5,0):4,('unit',5,H):12,('unit',1,H):23,('unit',2,H):17,('unit',4,H):4,('unit',3,0):36,('unit',3,H):-3,('unit',7,0):24,('unit',7,H):-1,('unit',6,0):-23,('unit',6,H):-3,('io',0):100,('io',1):100,('io',2):100,('io',3):100,('const',0):100,('const',1):100,('const',2):100,('const',3):100,('prep',1,0):30,('prep',1,1):30,('prep',1,2):30,('prep',1,3):30,('prep',1,6):30,('prep',1,7):30,('prep',3,0):30,('prep',3,1):30,('prep',3,2):30,('prep',3,3):30,('prep',3,6):30,('prep',3,7):30,('out',1,3):30,('out',3,3):23,('out',1,5):-26,('out',3,5):-14,('pack',1):60,('pack',3):0,('pack',2):0,('yj',2,0):7,('yj',4,0):-35,('yj',6,0):-4,('yj',1,H):2,('yj',2,H):-12,('yj',6,H):15,('rx',1,1):-7,('out',1,1):1,('rx',1,3):-27,('rx',1,5):-10,('rx',3,1):10,('out',3,1):17,('rx',3,3):-12,('rx',3,5):-2},
    HOLD={('unit',0,0):4,('unit',5,0):3,('unit',5,H):6,('unit',2,H):8,('unit',4,H):12,('unit',3,H):6,('unit',7,0):12,('unit',7,H):4,('unit',6,0):24,('unit',6,H):2,('out',1,3):30,('out',3,3):12,('out',1,5):4,('out',3,5):2,('yj',2,0):51,('yj',4,0):42,('yj',6,0):48,('yj',1,H):50,('yj',2,H):48,('yj',6,H):50,('rx',1,1):52,('out',1,1):5,('rx',1,3):1,('rx',1,5):1,('rx',3,1):45,('out',3,1):3,('rx',3,3):17})
EST4 = dict(EST, cyc=.94e-3, gat=1.45, pe=.45e-3, wake=.2, own=.14, off=170e3, chip=200e3, wide=360e3, loc=400e3, rlat=1.6, rissue=.45,
            first=1.6, eng=.03, row=.004, far=.2, look=.6)
RUN4 = dict(
    CFG, SHARE=1, UNITS=RUN["UNITS"], LAST=[352, 320, 352],
    STEP=[(1, 192, 'cp', -3.2), (2, 224, 'pq', 0.3), (2, 288, 'cv', 0.2), (2, 320, 'pq', 0.5)],
    STEPL=[(1, 224, '', 0), (3, 128, '', 0), (2, 320, 'v', -0.1), (2, 352, 'v', -1.0)],
    BIAS=dict([((k, r), 100) for k in ("io", "const") for r in range(4)] + [(("pack", 1), 60), (("pack", 3), 40)]
              + [(("prep", r, t), 30) for r in (1, 3) for t in (0, 1, 2, 3, 6, 7)]))
RUN4.update(IO=[(0,N_,'c',0),(0,N_,'x',-1,0,W,0),(0,N_,'x',0,0,H,0),(0,N_,'x',0,H,W,0),(0,N_,'t',0,1,0),(0,N_,'x',1,0,W,0),(1,N_,'c',0),(0,N_,'t',1,3,0),(2,N_,'c',0),(1,N_,'x',2,0,W,0),(1,N_,'x',3,0,H,0),(1,N_,'x',3,H,W,0),(3,N_,'c',0),(0,N_,'F',-1,0,0,0),(0,N_,'F',-1,1,1,0),(1,N_,'t',0,3,3),(3,N_,'x',6,0,W,0),(3,N_,'x',7,0,H,0),(2,N_,'x',5,0,W,0),(3,N_,'t',0,3,0),(3,N_,'x',7,H,W,0),(2,N_,'x',4,0,W,0),(0,2,'x',1,0,W,F,4),(2,N_,'t',0,3,0),(0,1,'f',-1,0,T_,7),(0,3,'f',-1,1,F,2),(0,1,'x',0,0,H,T_,18),(0,3,'x',0,H,W,F,0),(2,1,'x',5,0,H,T_,2),(2,3,'x',5,H,W,T_,4),(2,1,'x',4,0,H,F,14),(2,3,'x',4,H,W,T_,16),(2,1,'x',1,0,H,F,0),(2,3,'x',1,H,W,F,10),(1,2,'x',2,0,H,T_,0),(1,2,'q',2,0,H,F,0),(1,2,'q',2,H,W,F,0),(1,2,'x',2,H,W,T_,2),(2,0,'x',4,0,H,F,3),(2,0,'l',4,0,H,F,13),(1,2,'x',3,0,W,F,0),(1,3,'x',3,0,W,F,8),(3,1,'x',6,H,W,T_,0),(3,1,'l',6,H,W,T_,6),(3,0,'x',3,0,W,F,10),(3,1,'x',7,0,W,T_,0),(3,1,'x',6,0,H,F,0),(1,3,'x',5,0,H,F,0),(3,1,'x',5,H,W,F,0),(1,3,'x',4,0,H,F,0),(3,1,'x',4,H,W,F,0),(1,3,'x',2,0,W,F,14),(3,1,'x',0,H,W,F,6),(3,1,'x',1,H,W,F,7),(1,3,'x',1,0,H,F,0),(1,3,'x',0,0,H,F,2)],HOLD={('unit',0,0):2,('unit',1,0):7,('unit',4,0):8,('unit',5,H):6,('unit',1,H):6,('unit',2,H):12,('unit',4,H):20,('unit',7,H):11,('unit',6,0):5,('unit',6,H):15,('yj',4,0):45,('yj',2,0):48,('yj',2,H):50,('yj',6,H):31,('rx',1,1):47,('rx',1,5):13,('rx',3,1):49,('rx',3,3):1,('rx',3,5):8},LAM=80)
RUN4['BIAS'].update({('unit',0,0):18,('unit',0,H):13,('unit',1,0):13,('unit',2,0):12,('unit',4,0):-6,('unit',5,0):19,('unit',5,H):6,('unit',1,H):12,('unit',2,H):8,('unit',4,H):5,('unit',3,0):17,('unit',3,H):13,('unit',7,0):42,('unit',7,H):17,('unit',6,0):12,('unit',6,H):15,('out',1,3):-10,('out',3,3):-41,('out',1,5):-74,('out',3,5):99,('yj',4,0):76,('yj',2,0):0,('yj',2,H):3,('yj',6,H):6,('rx',1,1):71,('out',1,1):50,('rx',1,3):-9,('rx',1,5):-23,('rx',3,1):-15,('out',3,1):-19,('rx',3,3):-43,('rx',3,5):-16})
RUN5 = dict(RUN4, OUT16=(5,), FROM16=0, BIAS={k: v for k, v in RUN4["BIAS"].items() if not (k[0] == "prep" and k[2] < 2)})
RUN5.update(IO=[(0,N_,'c',0),(0,N_,'x',-1,0,W,0),(0,N_,'x',0,0,H,0),(0,N_,'x',0,H,W,0),(0,N_,'t',0,1,0),(0,N_,'x',1,0,W,0),(1,N_,'c',0),(0,N_,'t',1,3,0),(2,N_,'c',0),(1,N_,'x',2,0,W,0),(1,N_,'x',3,0,H,0),(1,N_,'x',3,H,W,0),(3,N_,'c',0),(0,N_,'F',-1,0,0,0),(0,N_,'F',-1,1,1,0),(0,N_,'F',0,0,2,0),(0,N_,'F',0,1,3,0),(1,N_,'t',0,3,3),(3,N_,'x',6,0,W,0),(3,N_,'x',7,0,H,0),(2,N_,'x',5,0,W,0),(3,N_,'t',0,3,0),(3,N_,'x',7,H,W,0),(2,N_,'x',4,0,W,0),(0,2,'x',1,0,W,F,0),(2,N_,'t',0,3,0),(2,N_,'F',4,0,4,1),(2,N_,'F',4,1,5,0),(0,1,'f',-1,0,T_,16),(0,3,'f',-1,1,F,16),(0,1,'f',0,2,F,7),(0,3,'f',0,3,F,4),(2,1,'x',5,0,H,T_,0),(2,3,'x',5,H,W,T_,6),(2,N_,'R',1,0,0,0),(2,N_,'R',1,1,1,0),(2,1,'f',1,0,F,8),(2,3,'f',1,1,F,12),(2,1,'f',4,4,F,23),(2,3,'f',4,5,F,29),(1,2,'x',2,0,H,T_,1),(1,2,'q',2,0,H,F,0),(1,2,'q',2,H,W,F,0),(1,2,'x',2,H,W,T_,0),(2,0,'x',4,0,H,F,13),(2,0,'l',4,0,H,F,11),(1,2,'x',3,0,W,F,15),(1,3,'x',3,0,W,F,0),(3,1,'x',6,H,W,T_,6),(3,1,'l',6,H,W,T_,7),(3,0,'x',3,0,W,F,8),(3,1,'x',7,0,W,T_,1),(3,1,'x',6,0,H,F,0),(1,3,'x',5,0,H,F,12),(3,1,'x',5,H,W,F,13),(1,3,'x',2,0,W,F,0)],HOLD={('unit',0,H):4,('unit',2,0):9,('unit',4,0):15,('unit',5,H):3,('unit',1,H):3,('unit',2,H):9,('unit',4,H):2,('unit',3,0):6,('unit',7,0):3,('unit',7,H):11,('unit',6,0):4,('unit',6,H):9,('out',1,3):24,('out',3,3):6,('out',1,5):22,('yj',4,0):50,('yj',2,0):51,('yj',2,H):52,('yj',6,H):46,('rx',1,1):46,('rx',1,5):12,('rx',3,1):56,('rx',3,3):15,('rx',3,5):7},LAM=80)
RUN5['BIAS'].update({('unit',0,0):17,('unit',0,H):13,('unit',1,0):14,('unit',2,0):18,('unit',4,0):-6,('unit',5,0):36,('unit',5,H):1,('unit',1,H):13,('unit',2,H):25,('unit',4,H):18,('unit',3,0):32,('unit',3,H):20,('unit',7,0):55,('unit',7,H):3,('unit',6,0):9,('unit',6,H):6,('out',1,3):-21,('out',3,3):-40,('out',1,5):-12,('out',3,5):17,('yj',4,0):107,('yj',2,0):-20,('yj',2,H):7,('yj',6,H):16,('rx',1,1):97,('out',1,1):17,('rx',1,3):8,('rx',1,5):-4,('rx',3,1):-23,('out',3,1):-32,('rx',3,3):-74,('rx',3,5):-6})
PLAN = {}


def rank_program(g, core, T, topo):
    who = with_helpers(list(T.cores), topo)
    if core not in who:
        return
    r = who.index(core)
    if not PLAN:
        PLAN["ops"] = build(list(T.cores), topo, RUN5)
        PLAN["queues"] = schedule(PLAN["ops"], EST4, RUN5)
    ops, queues = PLAN["ops"], PLAN["queues"]
    Q = {"pe": g.tensor, "act": g.scalar, "dve": g.vector, "pool": g, "sp": g.sync}
    ALU = {"add": AluOpType.add, "subtract": AluOpType.subtract, "mult": AluOpType.mult, "max": AluOpType.max,
           "is_lt": AluOpType.is_lt, "is_ge": AluOpType.is_ge, "is_equal": AluOpType.is_equal,
           "bitwise_and": AluOpType.bitwise_and}
    FN = {"Copy": ActivationFunctionType.Copy, "Square": ActivationFunctionType.Square}

    def R(ap):
        if ap[0] == "ind":
            return R(ap[1]).indirect(R(ap[2]))
        rows = slice(None) if (ap[5], ap[6]) == (0, 128) else slice(ap[5], ap[6])
        return T[ap[1]][rows, ap[2]:ap[3]] if ap[4] == 1 else T[ap[1]][rows, ap[2]:ap[3]:ap[4]]

    total, seen_all, sent = {}, {}, 0
    for o in ops:
        if o.get("to", o["r"]) == r:
            total[o["sem"]] = max(total.get(o["sem"], 0), o["val"])
    for q in ("sp", "act", "dve", "pe", "pool"):
        eng, seen = Q[q], {}
        for o in queues.get((r, q), []):
            want = {}
            for i, hard in o["deps"].items():
                if hard:
                    want[ops[i]["sem"]] = max(want.get(ops[i]["sem"], 0), ops[i]["val"])
            for s, v in want.items():
                if seen.get(s, 0) < v:
                    eng.wait_ge(T.sem[s], v)
                    seen[s] = v
                    seen_all[s] = max(seen_all.get(s, 0), v)
            ins = None
            for c in o["calls"]:
                k = c[0]
                if k == "tt":
                    ins = eng.tensor_tensor(R(c[1]), R(c[2]), R(c[3]), ALU[c[4]])
                elif k == "ts" and c[6] is None:
                    ins = eng.tensor_scalar(R(c[1]), R(c[2]), c[3], None, ALU[c[5]])
                elif k == "ts":
                    ins = eng.tensor_scalar(R(c[1]), R(c[2]), c[3], c[4], ALU[c[5]], ALU[c[6]])
                elif k == "cp":
                    ins = eng.tensor_copy(R(c[1]), R(c[2]))
                elif k == "set":
                    ins = eng.memset(R(c[1]), c[2])
                elif k == "act" and c[4] == 1.0:
                    ins = eng.activation(R(c[1]), R(c[2]), FN[c[3]])
                elif k == "act":
                    ins = eng.activation(R(c[1]), R(c[2]), FN[c[3]], scale=c[4])
                elif k == "mm":
                    ins = eng.matmul(R(c[1]), R(c[2]), R(c[3]), c[4], c[5])
                elif k == "sel":
                    ins = eng.affine_select(R(c[1]), R(c[2]), c[3], ALU[c[4]], 0.0, c[5], c[6])
                elif k == "dma":
                    ins = eng.dma_start(R(c[1]), R(c[2]))
                elif o["cost"][0] != "none":
                    rid, pid = topo.addr(c[1])[:2]
                    both = [o] + ([o["mate"]] if "mate" in o else [])
                    if len(c[2]) == 1 and len(both) == 1:
                        eng.remote_dma(R(c[2][0][0]), R(c[2][0][1]), T.sem[o["sem"]], T.sem.sent, pid, rid, c[3][0])
                    else:
                        eng.remote_dma_fused(
                            [RemoteDMATransfer(dst_ids=[DstId(rid=topo.addr(v["calls"][0][1])[0], pnc=topo.addr(v["calls"][0][1])[1])],
                                               dma_engine_mask=m, remote_sem=T.sem[v["sem"]], src=R(p[1]), dst=R(p[0]))
                             for v in both for p, m in zip(v["calls"][0][2], v["calls"][0][3])], local_sem=T.sem.sent)
                    sent += sum(v["inc"] for v in both)
            if ins is not None:
                ins.then_inc(T.sem[o["sem"]], o["inc"])
    if sent:
        g.wait_ge(T.sem.sent, sent)
    for s, v in total.items():
        if seen_all.get(s, 0) < v:
            g.wait_ge(T.sem[s], v)
